import numpy as np
import ml_dtypes


def mxq(x, axis, fmt="e4m3"):
    dtype, down = {"e4m3": (ml_dtypes.float8_e4m3fn, 7), "e5m2": (ml_dtypes.float8_e5m2, 14)}[fmt]
    v = np.moveaxis(np.asarray(x, np.float32).astype(ml_dtypes.bfloat16).astype(np.float64), axis, -1)
    blocks = v.reshape(v.shape[:-1] + (-1, 32))
    amax = np.abs(blocks).max(-1, keepdims=True)
    byte = np.maximum(np.where(amax > 0, np.frexp(amax)[1] - 1 + 127, 0) - down, 1)
    scale = np.exp2(byte - 127.0)
    codes = (blocks / scale).astype(np.float32).astype(dtype).astype(np.float64)
    return np.moveaxis((codes * scale).reshape(v.shape), -1, axis)


WIDE = False


def mx_kscale(k):
    if not WIDE:
        return np.ones(k)
    levels = np.array([24, -24, 12, -12, 0])
    if k % 512:
        return np.exp2(np.random.permutation(np.resize(levels, k // 32))).repeat(32)
    a = np.empty((k // 512, 16))
    for p in range(k // 512):
        a[p, :8] = np.random.permutation(np.resize(levels, 8))
        for g in range(8):
            far = levels[np.abs(levels - a[p, g]) >= 10]
            a[p, g + 8] = far[np.random.randint(len(far))]
    return np.exp2(a.ravel()).repeat(32)


def f64(x):
    return np.asarray(x).astype(np.float64)


def striped(idx):
    return np.tile(idx.reshape(-1, 16).T, (8, 1)).astype(np.uint16)


def unstriped(offs):
    return offs[:16].T.reshape(-1).astype(np.int64)


E2M1 = np.array([0.0, 0.5, 1.0, 1.5, 2.0, 3.0, 4.0, 6.0, -0.0, -0.5, -1.0, -1.5, -2.0, -3.0, -4.0, -6.0])


def pack_weight(w, fmt):
    k, n = w.shape
    w = f64(np.asarray(w, np.float32).astype(ml_dtypes.bfloat16)).reshape(k // 32, 32, n)
    amax = np.abs(w).max(1)
    if fmt == "e4m3":
        byte = np.frexp(amax)[1] - 1 + 127 - 7
    else:
        mant, ex = np.frexp(amax / 6.0)
        byte = np.where(mant > 0.5, ex, ex - 1) + 127
    byte = np.clip(np.where(amax > 0, byte, 1), 1, 254)
    scaled = (w * np.exp2(127.0 - byte)[:, None, :]).reshape(k, n).astype(np.float32)
    by_word = np.ascontiguousarray(scaled.reshape(k // 512, 128, 4, n).transpose(0, 1, 3, 2))
    if fmt == "e4m3":
        words = by_word.astype(ml_dtypes.float8_e4m3fn).view(np.uint8)
    else:
        c = by_word.astype(ml_dtypes.float4_e2m1fn).view(np.uint8) & 0xF
        words = (c[..., 0::2] | (c[..., 1::2] << 4)).reshape(k // 512, 128, 2 * n)
    return np.ascontiguousarray(words), np.ascontiguousarray(byte.astype(np.uint8).reshape(k // 512, 16, n))


def unpack_weight(words, scales, fmt):
    g, _, n = scales.shape
    words = np.ascontiguousarray(words).reshape(g, 128, n, -1)
    if fmt == "e4m3":
        vals = words.view(ml_dtypes.float8_e4m3fn).astype(np.float64)
    else:
        nib = np.empty((g, 128, n, 4), np.uint8)
        nib[..., 0::2] = words & 0xF
        nib[..., 1::2] = words >> 4
        vals = E2M1[nib]
    vals = vals * np.repeat(np.exp2(scales.astype(np.float64) - 127.0), 8, axis=1)[..., None]
    return vals.transpose(0, 1, 3, 2).reshape(g * 512, n)


K, R, N, T, J = 1024, 512, 512, 2048, 1024


def setup_inputs():
    n = np.random.standard_normal
    s = mx_kscale(K)[:, None]
    u = mx_kscale(R)[:, None]
    wd = n((R, N)) / np.sqrt(R) / u
    wd4 = pack_weight(wd, "e2m1")
    wdrest = wd - unpack_weight(*wd4, "e2m1")
    p_tab = pack_weight(n((K, T)) * s, "e4m3")
    p_wd8 = pack_weight(wdrest, "e4m3")
    return {
        "tab_words": p_tab[0],
        "tab_scales": p_tab[1],
        "wu": (n((K, R)) / np.sqrt(K) / s * u.T).astype(np.float32),
        "wd4_words": wd4[0],
        "wd4_scales": wd4[1],
        "wd8_words": p_wd8[0],
        "wd8_scales": p_wd8[1],
        "rT": (n((N, T))).astype(np.float32),
        "wgo": np.tile(np.random.uniform(0.5, 2.0, J), (128, 1)).astype(np.float32),
        "offs": striped(np.random.permutation(T)[:J]),
    }


def reference(tab_words, tab_scales, wu, wd4_words, wd4_scales, wd8_words, wd8_scales, rT, wgo, offs):
    idx = unstriped(offs)
    tab_ = unpack_weight(tab_words, tab_scales, "e4m3")[:, idx]
    wu_ = mxq(f64(wu), 0, "e4m3")
    a = wu_.T @ tab_
    h = np.maximum(a, 0.0)
    h_ = mxq(h, 0, "e4m3")
    wd4_ = unpack_weight(wd4_words, wd4_scales, "e2m1")
    wd8_ = unpack_weight(wd8_words, wd8_scales, "e4m3")
    y = wd4_.T @ h_ + wd8_.T @ h_
    out = np.zeros((N, T))
    out[:, idx] = f64(wgo)[0] * (y + f64(rT)[:, idx])
    return out

@@ -1,0 +1,178 @@
+from contextlib import ExitStack
+
+import concourse.mybir as mybir
+
+K, R, N, T, J = 1024, 512, 512, 2048, 1024
+FLOPS = 2 * K * R * J + 2 * 2 * R * N * J
+
+F32 = mybir.dt.float32
+BF16 = mybir.dt.bfloat16
+I32 = mybir.dt.int32
+U32 = mybir.dt.uint32
+U16 = mybir.dt.uint16
+U8 = mybir.dt.uint8
+FP8X4 = mybir.dt.float8_e4m3fn_x4
+FP4X4 = mybir.dt.float4_e2m1fn_x4
+ADD = mybir.AluOpType.add
+MULT = mybir.AluOpType.mult
+COPY = mybir.ActivationFunctionType.Copy
+RELU = mybir.ActivationFunctionType.Relu
+
+P = 128
+HALF = 512
+BLK = 128
+
+
+def tile_list_modp_relu_res_res_kernel(
+    tc, tab_words, tab_scales, wu, wd4_words, wd4_scales, wd8_words, wd8_scales, rT, wgo, offs, out
+):
+    nc = tc.nc
+    with ExitStack() as ctx:
+        keep = ctx.enter_context(tc.tile_pool(name="keep", bufs=1))
+        ring = ctx.enter_context(tc.tile_pool(name="ring", bufs=4))
+        pair = ctx.enter_context(tc.tile_pool(name="pair", bufs=2))
+        ps_a = ctx.enter_context(tc.psum_pool(name="ps_a", bufs=4))
+        ps_y = ctx.enter_context(tc.psum_pool(name="ps_y", bufs=4))
+
+        offsets = keep.tile([P, J // 16], U16, name="offsets")
+        nc.sync.dma_start(offsets[:], offs)
+
+        tab_s = keep.tile([P, T // 4], I32, name="tab_s", align_bytes=64)
+        wd_s = keep.tile([P, 2, N // 4], I32, name="wd_s", align_bytes=64)
+        nc.vector.memset(tab_s[:], 0)
+        nc.vector.memset(wd_s[:], 0)
+        placed = [keep.tile([P, T], F32, name="placed0")]
+        nc.vector.memset(placed[0][:], 0.0)
+        for q in range(4):
+            nc.sync.dma_start(tab_s[32 * q : 32 * q + 8, :], tab_scales[:, 4 * q : 4 * q + 4, :].bitcast(I32))
+        for i, src in enumerate((wd4_scales, wd8_scales)):
+            for q in range(4):
+                nc.gpsimd.dma_start(wd_s[32 * q : 32 * q + 4, i, :], src[0, 4 * q : 4 * q + 4, :].bitcast(I32))
+
+        tab_w = [keep.tile([P, T], I32, name="tab_w%d" % a) for a in range(2)]
+        wu_raw = [[keep.tile([P, 4, R // 2], F32, name="wu_raw%d%d" % (a, c)) for c in range(2)] for a in range(2)]
+        wd4_w = keep.tile([P, N // 2], I32, name="wd4_w", align_bytes=64)
+        wd8_w = keep.tile([P, N], I32, name="wd8_w", align_bytes=64)
+        r_all = [keep.tile([P, T], F32, name="r_all%d" % i) for i in range(4)]
+        gate = keep.tile([P, J], F32, name="gate")
+
+        def load_tab(a):
+            nc.sync.dma_start(tab_w[a][:], tab_words[a].rearrange("p t i -> p (t i)").bitcast(I32))
+
+        def load_wu(a, c):
+            rows = wu[512 * a : 512 * (a + 1), 256 * c : 256 * (c + 1)]
+            nc.sync.dma_start(wu_raw[a][c][:], rows.rearrange("(p j) c -> p j c", j=4))
+
+        load_tab(0)
+        for a in range(2):
+            for c in range(2):
+                load_wu(a, c)
+        load_tab(1)
+        nc.sync.dma_start(wd4_w[:], wd4_words[0].bitcast(I32))
+        nc.sync.dma_start(wd8_w[:], wd8_words[0].rearrange("p n i -> p (n i)").bitcast(I32))
+        nc.sync.dma_start(r_all[0][:], rT[0:P, :])
+        nc.sync.dma_start(gate[:], wgo)
+        for nt in range(1, 4):
+            nc.sync.dma_start(r_all[nt][:], rT[nt * P : (nt + 1) * P, :])
+
+        def part(lo, hi):
+            return offsets[:, lo // 16 : hi // 16]
+
+        got_w = [keep.tile([P, J], U32, name="got_w%d" % a, align_bytes=64) for a in range(2)]
+        got_s = keep.tile([P, J], U8, name="got_s", align_bytes=64)
+        wu_bf = [keep.tile([P, 4 * R], BF16, name="wu_bf%d" % a, align_bytes=64) for a in range(2)]
+        wu_q = keep.tile([P, 2, R], U32, name="wu_q", align_bytes=64)
+        wu_s = keep.tile([P, 2, R], U8, name="wu_s", align_bytes=64)
+        h_bf = keep.tile([P, 4 * J], BF16, name="h_bf", tag="late", align_bytes=64)
+        h_q = keep.tile([P, J], U32, name="h_q", align_bytes=64)
+        h_s = keep.tile([P, J], U8, name="h_s", align_bytes=64)
+        r_got = {}
+
+        def gather_words(a, lo, hi):
+            nc.vector.tensor_copy(got_w[a][:, lo:hi], tab_w[a][:].bitcast(U32).indirect(part(lo, hi)))
+
+        def cast_wu(a, c):
+            dst = wu_bf[a][:].rearrange("p (t m j) -> p m j t", t=4, j=4)[:, 64 * c : 64 * (c + 1), :, :]
+            nc.scalar.activation(dst, wu_raw[a][c][:].rearrange("p j (m t) -> p m j t", t=4), COPY)
+
+        def quant_wu(a):
+            nc.vector.quantize_mx(out=wu_q[:, a, :].bitcast(FP8X4), scales=wu_s[:, a, :], in_=wu_bf[a][:])
+
+        def up(b):
+            cols = slice(b * BLK, (b + 1) * BLK)
+            bank = ps_a.tile([P, 4, BLK], F32, name="bank_a")
+            for t in range(4):
+                for a in range(2):
+                    nc.tensor.matmul_mx(
+                        out=bank[:, t, :],
+                        lhsT=wu_q[:, a, t * P : (t + 1) * P].bitcast(FP8X4),
+                        lhsT_scale=wu_s[:, a, t * P : (t + 1) * P],
+                        rhs=got_w[a][:, cols].bitcast(FP8X4),
+                        rhs_scale=got_s[4 * a :, cols],
+                        start=(a == 0),
+                        stop=(a == 1),
+                    )
+            dst = h_bf[:, 4 * b * BLK : 4 * (b + 1) * BLK].rearrange("p (n t) -> p n t", t=4)
+            nc.scalar.activation(dst, bank[:].rearrange("p t n -> p n t"), RELU)
+
+        def quant_h(lo, hi):
+            nc.vector.quantize_mx(out=h_q[:, lo:hi].bitcast(FP8X4), scales=h_s[:, lo:hi], in_=h_bf[:, 4 * lo : 4 * hi])
+
+        def gather_r(nt):
+            r_got[nt] = pair.tile([P, J], F32, name="r_got")
+            nc.vector.tensor_copy(r_got[nt][:], r_all[nt][:].indirect(offsets[:]))
+
+        def down(nt, half):
+            cols = slice(half * HALF, (half + 1) * HALF)
+            ncol = slice(nt * P, (nt + 1) * P)
+            bank = ps_y.tile([P, HALF], F32, name="bank_y")
+            nc.tensor.matmul_mx(
+                out=bank[:],
+                lhsT=wd4_w[:].bitcast(U8)[:, 2 * nt * P : 2 * (nt + 1) * P].bitcast(FP4X4),
+                lhsT_scale=wd_s[:, 0, :].bitcast(U8)[:, ncol],
+                rhs=h_q[:, cols].bitcast(FP8X4),
+                rhs_scale=h_s[:, cols],
+                start=True,
+                stop=False,
+            )
+            nc.tensor.matmul_mx(
+                out=bank[:],
+                lhsT=wd8_w[:, ncol].bitcast(FP8X4),
+                lhsT_scale=wd_s[:, 1, :].bitcast(U8)[:, ncol],
+                rhs=h_q[:, cols].bitcast(FP8X4),
+                rhs_scale=h_s[:, cols],
+                start=False,
+                stop=True,
+            )
+            z = ring.tile([P, HALF], F32, name="z")
+            nc.vector.tensor_tensor(z[:], bank[:], r_got[nt][:, cols], ADD)
+            return z
+
+        def scatter(nt, half, z):
+            lo, hi = half * HALF, (half + 1) * HALF
+            nc.vector.tensor_tensor(placed[nt % 2][:].indirect(part(lo, hi)), z[:], gate[:, lo:hi], MULT)
+
+        gather_words(0, 0, J)
+        nc.vector.tensor_copy(got_s[:], tab_s[:].bitcast(U8).indirect(offsets[:]))
+        for a in range(2):
+            cast_wu(a, 0)
+            cast_wu(a, 1)
+            quant_wu(a)
+        gather_words(1, 0, HALF)
+        gather_words(1, HALF, J)
+        for b in range(4):
+            up(b)
+        gather_r(0)
+        quant_h(0, HALF)
+        for b in range(4, 8):
+            up(b)
+        quant_h(HALF, J)
+        placed.append(keep.tile([P, T], F32, name="placed1", tag="late", align_bytes=64))
+        nc.gpsimd.memset(placed[1][:], 0.0)
+        for nt in range(4):
+            zs = [down(nt, half) for half in range(2)]
+            if nt < 3:
+                gather_r(nt + 1)
+            for half in range(2):
+                scatter(nt, half, zs[half])
+            nc.sync.dma_start(out[nt * P : (nt + 1) * P, :], placed[nt % 2][:])

@@ -1,6 +1,7 @@
 from contextlib import ExitStack
 
 import concourse.mybir as mybir
+from concourse.masks import make_identity
 
 K, R, N, T, J = 1024, 512, 512, 2048, 1024
 FLOPS = 2 * K * R * J + 2 * 2 * R * N * J
@@ -13,8 +14,6 @@ U16 = mybir.dt.uint16
 U8 = mybir.dt.uint8
 FP8X4 = mybir.dt.float8_e4m3fn_x4
 FP4X4 = mybir.dt.float4_e2m1fn_x4
-ADD = mybir.AluOpType.add
-MULT = mybir.AluOpType.mult
 COPY = mybir.ActivationFunctionType.Copy
 RELU = mybir.ActivationFunctionType.Relu
 
@@ -31,8 +30,10 @@ def tile_list_modp_relu_res_res_kernel(
         keep = ctx.enter_context(tc.tile_pool(name="keep", bufs=1))
         ring = ctx.enter_context(tc.tile_pool(name="ring", bufs=4))
         pair = ctx.enter_context(tc.tile_pool(name="pair", bufs=2))
-        ps_a = ctx.enter_context(tc.psum_pool(name="ps_a", bufs=4))
-        ps_y = ctx.enter_context(tc.psum_pool(name="ps_y", bufs=4))
+        ps_a = ctx.enter_context(tc.psum_pool(name="ps_a", bufs=2))
+        ps_y = ctx.enter_context(tc.psum_pool(name="ps_y", bufs=2))
+        ps_r = ctx.enter_context(tc.psum_pool(name="ps_r", bufs=2))
+        ps_z = ctx.enter_context(tc.psum_pool(name="ps_z", bufs=2))
 
         offsets = keep.tile([P, J // 16], U16, name="offsets")
         nc.sync.dma_start(offsets[:], offs)
@@ -43,8 +44,6 @@ def tile_list_modp_relu_res_res_kernel(
         nc.vector.memset(wd_s[:], 0)
         placed = [keep.tile([P, T], F32, name="placed0")]
         nc.vector.memset(placed[0][:], 0.0)
-        for q in range(4):
-            nc.sync.dma_start(tab_s[32 * q : 32 * q + 8, :], tab_scales[:, 4 * q : 4 * q + 4, :].bitcast(I32))
         for i, src in enumerate((wd4_scales, wd8_scales)):
             for q in range(4):
                 nc.gpsimd.dma_start(wd_s[32 * q : 32 * q + 4, i, :], src[0, 4 * q : 4 * q + 4, :].bitcast(I32))
@@ -54,7 +53,11 @@ def tile_list_modp_relu_res_res_kernel(
         wd4_w = keep.tile([P, N // 2], I32, name="wd4_w", align_bytes=64)
         wd8_w = keep.tile([P, N], I32, name="wd8_w", align_bytes=64)
         r_all = [keep.tile([P, T], F32, name="r_all%d" % i) for i in range(4)]
-        gate = keep.tile([P, J], F32, name="gate")
+        gate_rows = keep.tile([P, P], F32, name="gate_rows")
+        gate = keep.tile([P, J // BLK], F32, name="gate")
+        ident = keep.tile([P, P], F32, name="ident")
+        make_identity(nc, ident[:])
+        y_t = keep.tile([P, J // BLK, N], F32, name="y_t")
 
         def load_tab(a):
             nc.sync.dma_start(tab_w[a][:], tab_words[a].rearrange("p t i -> p (t i)").bitcast(I32))
@@ -63,15 +66,21 @@ def tile_list_modp_relu_res_res_kernel(
             rows = wu[512 * a : 512 * (a + 1), 256 * c : 256 * (c + 1)]
             nc.sync.dma_start(wu_raw[a][c][:], rows.rearrange("(p j) c -> p j c", j=4))
 
+        def load_tab_s(q):
+            nc.sync.dma_start(tab_s[32 * q : 32 * q + 8, :], tab_scales[:, 4 * q : 4 * q + 4, :].bitcast(I32))
+
         load_tab(0)
-        for a in range(2):
-            for c in range(2):
-                load_wu(a, c)
+        load_wu(0, 0)
+        for q in range(4):
+            load_tab_s(q)
+        load_wu(0, 1)
+        load_wu(1, 0)
+        load_wu(1, 1)
         load_tab(1)
+        nc.sync.dma_start(gate_rows[:], wgo[0:16, :].rearrange("r (b j) -> (r b) j", j=BLK))
         nc.sync.dma_start(wd4_w[:], wd4_words[0].bitcast(I32))
         nc.sync.dma_start(wd8_w[:], wd8_words[0].rearrange("p n i -> p (n i)").bitcast(I32))
         nc.sync.dma_start(r_all[0][:], rT[0:P, :])
-        nc.sync.dma_start(gate[:], wgo)
         for nt in range(1, 4):
             nc.sync.dma_start(r_all[nt][:], rT[nt * P : (nt + 1) * P, :])
 
@@ -122,35 +131,56 @@ def tile_list_modp_relu_res_res_kernel(
             r_got[nt] = pair.tile([P, J], F32, name="r_got")
             nc.vector.tensor_copy(r_got[nt][:], r_all[nt][:].indirect(offsets[:]))
 
-        def down(nt, half):
-            cols = slice(half * HALF, (half + 1) * HALF)
-            ncol = slice(nt * P, (nt + 1) * P)
-            bank = ps_y.tile([P, HALF], F32, name="bank_y")
+        def down(b):
+            cols = slice(b * BLK, (b + 1) * BLK)
+            bank = ps_y.tile([P, N], F32, name="bank_y")
             nc.tensor.matmul_mx(
                 out=bank[:],
-                lhsT=wd4_w[:].bitcast(U8)[:, 2 * nt * P : 2 * (nt + 1) * P].bitcast(FP4X4),
-                lhsT_scale=wd_s[:, 0, :].bitcast(U8)[:, ncol],
-                rhs=h_q[:, cols].bitcast(FP8X4),
-                rhs_scale=h_s[:, cols],
+                lhsT=h_q[:, cols].bitcast(FP8X4),
+                lhsT_scale=h_s[:, cols],
+                rhs=wd4_w[:].bitcast(U8).bitcast(FP4X4),
+                rhs_scale=wd_s[:, 0, :].bitcast(U8),
                 start=True,
                 stop=False,
             )
             nc.tensor.matmul_mx(
                 out=bank[:],
-                lhsT=wd8_w[:, ncol].bitcast(FP8X4),
-                lhsT_scale=wd_s[:, 1, :].bitcast(U8)[:, ncol],
-                rhs=h_q[:, cols].bitcast(FP8X4),
-                rhs_scale=h_s[:, cols],
+                lhsT=h_q[:, cols].bitcast(FP8X4),
+                lhsT_scale=h_s[:, cols],
+                rhs=wd8_w[:].bitcast(FP8X4),
+                rhs_scale=wd_s[:, 1, :].bitcast(U8),
                 start=False,
                 stop=True,
             )
-            z = ring.tile([P, HALF], F32, name="z")
-            nc.vector.tensor_tensor(z[:], bank[:], r_got[nt][:, cols], ADD)
-            return z
+            nc.scalar.activation(y_t[:, b, :], bank[:], COPY, scale=gate[:, b : b + 1])
 
-        def scatter(nt, half, z):
-            lo, hi = half * HALF, (half + 1) * HALF
-            nc.vector.tensor_tensor(placed[nt % 2][:].indirect(part(lo, hi)), z[:], gate[:, lo:hi], MULT)
+        def turn_r(nt, half):
+            bank = ps_r.tile([P, 4, BLK], F32, name="bank_r")
+            r_t = ring.tile([P, 4, BLK], F32, name="r_t")
+            for i in range(4):
+                b = 4 * half + i
+                nc.tensor.transpose(bank[:, i, :], r_got[nt][:, b * BLK : (b + 1) * BLK], ident[:])
+            for i in range(4):
+                b = 4 * half + i
+                nc.scalar.activation(r_t[:, i, :], bank[:, i, :], COPY, scale=gate[:, b : b + 1])
+            return r_t
+
+        def combine(nt, half, r_t, z):
+            bank = ps_z.tile([P, 4, BLK], F32, name="bank_z")
+            for i in range(4):
+                b = 4 * half + i
+                nc.tensor.matmul(bank[:, i, :], r_t[:, i, :], ident[:], start=True, stop=False, is_transpose=True)
+                nc.tensor.matmul(
+                    bank[:, i, :], y_t[:, b, nt * P : (nt + 1) * P], ident[:], start=False, stop=True, is_transpose=True
+                )
+            nc.scalar.activation(z[:, half * HALF : (half + 1) * HALF], bank[:].rearrange("p i j -> p (i j)"), COPY)
+
+        def scatter(nt, lo, hi, z):
+            nc.vector.tensor_copy(placed[nt % 2][:].indirect(part(lo, hi)), z[:, lo:hi])
+
+        gate_bank = ps_r.tile([P, 4, BLK], F32, name="bank_r")
+        nc.tensor.transpose(gate_bank[:, 0, :], gate_rows[:], ident[:])
+        nc.scalar.activation(gate[:], gate_bank[:, 0, 0 : J // BLK], COPY)
 
         gather_words(0, 0, J)
         nc.vector.tensor_copy(got_s[:], tab_s[:].bitcast(U8).indirect(offsets[:]))
@@ -166,13 +196,24 @@ def tile_list_modp_relu_res_res_kernel(
         quant_h(0, HALF)
         for b in range(4, 8):
             up(b)
+        for b in range(4):
+            down(b)
         quant_h(HALF, J)
         placed.append(keep.tile([P, T], F32, name="placed1", tag="late", align_bytes=64))
         nc.gpsimd.memset(placed[1][:], 0.0)
         for nt in range(4):
-            zs = [down(nt, half) for half in range(2)]
+            z = pair.tile([P, J], F32, name="z")
+            for half in range(2):
+                r_t = turn_r(nt, half)
+                if nt == 0 and half == 1:
+                    for b in range(4, 8):
+                        down(b)
+                combine(nt, half, r_t, z)
             if nt < 3:
                 gather_r(nt + 1)
-            for half in range(2):
-                scatter(nt, half, zs[half])
+            if nt == 0:
+                scatter(nt, 0, HALF, z)
+                scatter(nt, HALF, J, z)
+            else:
+                scatter(nt, 0, J, z)
             nc.sync.dma_start(out[nt * P : (nt + 1) * P, :], placed[nt % 2][:])

@@ -14,6 +14,7 @@ U16 = mybir.dt.uint16
 U8 = mybir.dt.uint8
 FP8X4 = mybir.dt.float8_e4m3fn_x4
 FP4X4 = mybir.dt.float4_e2m1fn_x4
+MULT = mybir.AluOpType.mult
 COPY = mybir.ActivationFunctionType.Copy
 RELU = mybir.ActivationFunctionType.Relu
 
@@ -29,11 +30,7 @@ def tile_list_modp_relu_res_res_kernel(
     with ExitStack() as ctx:
         keep = ctx.enter_context(tc.tile_pool(name="keep", bufs=1))
         ring = ctx.enter_context(tc.tile_pool(name="ring", bufs=4))
-        pair = ctx.enter_context(tc.tile_pool(name="pair", bufs=2))
-        ps_a = ctx.enter_context(tc.psum_pool(name="ps_a", bufs=2))
-        ps_y = ctx.enter_context(tc.psum_pool(name="ps_y", bufs=2))
-        ps_r = ctx.enter_context(tc.psum_pool(name="ps_r", bufs=2))
-        ps_z = ctx.enter_context(tc.psum_pool(name="ps_z", bufs=2))
+        psum = ctx.enter_context(tc.psum_pool(name="psum", bufs=8))
 
         offsets = keep.tile([P, J // 16], U16, name="offsets")
         nc.sync.dma_start(offsets[:], offs)
@@ -42,22 +39,18 @@ def tile_list_modp_relu_res_res_kernel(
         wd_s = keep.tile([P, 2, N // 4], I32, name="wd_s", align_bytes=64)
         nc.vector.memset(tab_s[:], 0)
         nc.vector.memset(wd_s[:], 0)
-        placed = [keep.tile([P, T], F32, name="placed0")]
+        placed = [keep.tile([P, T], F32, name="placed%d" % i) for i in range(2)]
         nc.vector.memset(placed[0][:], 0.0)
-        for i, src in enumerate((wd4_scales, wd8_scales)):
-            for q in range(4):
-                nc.gpsimd.dma_start(wd_s[32 * q : 32 * q + 4, i, :], src[0, 4 * q : 4 * q + 4, :].bitcast(I32))
+        nc.gpsimd.memset(placed[1][:], 0.0)
 
         tab_w = [keep.tile([P, T], I32, name="tab_w%d" % a) for a in range(2)]
         wu_raw = [[keep.tile([P, 4, R // 2], F32, name="wu_raw%d%d" % (a, c)) for c in range(2)] for a in range(2)]
         wd4_w = keep.tile([P, N // 2], I32, name="wd4_w", align_bytes=64)
         wd8_w = keep.tile([P, N], I32, name="wd8_w", align_bytes=64)
-        r_all = [keep.tile([P, T], F32, name="r_all%d" % i) for i in range(4)]
-        gate_rows = keep.tile([P, P], F32, name="gate_rows")
-        gate = keep.tile([P, J // BLK], F32, name="gate")
+        r_all = [keep.tile([P, T], F32, name="r_all%d" % i, align_bytes=64) for i in range(4)]
+        gate = keep.tile([P, J], F32, name="gate")
         ident = keep.tile([P, P], F32, name="ident")
         make_identity(nc, ident[:])
-        y_t = keep.tile([P, J // BLK, N], F32, name="y_t")
 
         def load_tab(a):
             nc.sync.dma_start(tab_w[a][:], tab_words[a].rearrange("p t i -> p (t i)").bitcast(I32))
@@ -66,23 +59,32 @@ def tile_list_modp_relu_res_res_kernel(
             rows = wu[512 * a : 512 * (a + 1), 256 * c : 256 * (c + 1)]
             nc.sync.dma_start(wu_raw[a][c][:], rows.rearrange("(p j) c -> p j c", j=4))
 
-        def load_tab_s(q):
-            nc.sync.dma_start(tab_s[32 * q : 32 * q + 8, :], tab_scales[:, 4 * q : 4 * q + 4, :].bitcast(I32))
+        def load_tab_s(a):
+            for q in range(4):
+                rows = tab_scales[a, 4 * q : 4 * q + 4, :]
+                nc.sync.dma_start(tab_s[32 * q + 4 * a : 32 * q + 4 * a + 4, :], rows.bitcast(I32))
+
+        def load_wd_s(i, src, quads):
+            for q in quads:
+                nc.sync.dma_start(wd_s[32 * q : 32 * q + 4, i, :], src[0, 4 * q : 4 * q + 4, :].bitcast(I32))
 
         load_tab(0)
         load_wu(0, 0)
-        for q in range(4):
-            load_tab_s(q)
+        load_tab_s(0)
         load_wu(0, 1)
+        load_tab_s(1)
         load_wu(1, 0)
+        load_wd_s(0, wd4_scales, (0, 1))
         load_wu(1, 1)
+        load_wd_s(0, wd4_scales, (2, 3))
         load_tab(1)
-        nc.sync.dma_start(gate_rows[:], wgo[0:16, :].rearrange("r (b j) -> (r b) j", j=BLK))
-        nc.sync.dma_start(wd4_w[:], wd4_words[0].bitcast(I32))
-        nc.sync.dma_start(wd8_w[:], wd8_words[0].rearrange("p n i -> p (n i)").bitcast(I32))
-        nc.sync.dma_start(r_all[0][:], rT[0:P, :])
-        for nt in range(1, 4):
+        load_wd_s(1, wd8_scales, range(4))
+        for nt in range(4):
             nc.sync.dma_start(r_all[nt][:], rT[nt * P : (nt + 1) * P, :])
+            if nt == 1:
+                nc.sync.dma_start(wd4_w[:], wd4_words[0].bitcast(I32))
+                nc.sync.dma_start(wd8_w[:], wd8_words[0].rearrange("p n i -> p (n i)").bitcast(I32))
+        nc.sync.dma_start(gate[:], wgo)
 
         def part(lo, hi):
             return offsets[:, lo // 16 : hi // 16]
@@ -92,10 +94,10 @@ def tile_list_modp_relu_res_res_kernel(
         wu_bf = [keep.tile([P, 4 * R], BF16, name="wu_bf%d" % a, align_bytes=64) for a in range(2)]
         wu_q = keep.tile([P, 2, R], U32, name="wu_q", align_bytes=64)
         wu_s = keep.tile([P, 2, R], U8, name="wu_s", align_bytes=64)
-        h_bf = keep.tile([P, 4 * J], BF16, name="h_bf", tag="late", align_bytes=64)
-        h_q = keep.tile([P, J], U32, name="h_q", align_bytes=64)
+        h_bf = keep.tile([P, 4 * J], BF16, name="h_bf", align_bytes=64)
+        h_q = {}
         h_s = keep.tile([P, J], U8, name="h_s", align_bytes=64)
-        r_got = {}
+        r_got = [keep.tile([P, J], F32, name="r_got%d" % i) for i in range(4)]
 
         def gather_words(a, lo, hi):
             nc.vector.tensor_copy(got_w[a][:, lo:hi], tab_w[a][:].bitcast(U32).indirect(part(lo, hi)))
@@ -109,7 +111,7 @@ def tile_list_modp_relu_res_res_kernel(
 
         def up(b):
             cols = slice(b * BLK, (b + 1) * BLK)
-            bank = ps_a.tile([P, 4, BLK], F32, name="bank_a")
+            bank = psum.tile([P, 4, BLK], F32, name="bank")
             for t in range(4):
                 for a in range(2):
                     nc.tensor.matmul_mx(
@@ -124,63 +126,69 @@ def tile_list_modp_relu_res_res_kernel(
             dst = h_bf[:, 4 * b * BLK : 4 * (b + 1) * BLK].rearrange("p (n t) -> p n t", t=4)
             nc.scalar.activation(dst, bank[:].rearrange("p t n -> p n t"), RELU)
 
-        def quant_h(lo, hi):
-            nc.vector.quantize_mx(out=h_q[:, lo:hi].bitcast(FP8X4), scales=h_s[:, lo:hi], in_=h_bf[:, 4 * lo : 4 * hi])
+        def quant_h(half):
+            lo, hi = half * HALF, (half + 1) * HALF
+            h_q[half] = keep.tile([P, HALF], U32, name="h_q%d" % half, tag="r_all%d" % half, align_bytes=64)
+            nc.vector.quantize_mx(out=h_q[half][:].bitcast(FP8X4), scales=h_s[:, lo:hi], in_=h_bf[:, 4 * lo : 4 * hi])
 
-        def gather_r(nt):
-            r_got[nt] = pair.tile([P, J], F32, name="r_got")
-            nc.vector.tensor_copy(r_got[nt][:], r_all[nt][:].indirect(offsets[:]))
+        def gather_r(nt, lo, hi):
+            nc.vector.tensor_copy(r_got[nt][:, lo:hi], r_all[nt][:].indirect(part(lo, hi)))
 
-        def down(b):
-            cols = slice(b * BLK, (b + 1) * BLK)
-            bank = ps_y.tile([P, N], F32, name="bank_y")
+        def down(nt, half):
+            cols = slice(half * HALF, (half + 1) * HALF)
+            ncol = slice(nt * P, (nt + 1) * P)
+            bank = psum.tile([P, HALF], F32, name="bank")
             nc.tensor.matmul_mx(
                 out=bank[:],
-                lhsT=h_q[:, cols].bitcast(FP8X4),
-                lhsT_scale=h_s[:, cols],
-                rhs=wd4_w[:].bitcast(U8).bitcast(FP4X4),
-                rhs_scale=wd_s[:, 0, :].bitcast(U8),
+                lhsT=wd4_w[:].bitcast(U8)[:, 2 * nt * P : 2 * (nt + 1) * P].bitcast(FP4X4),
+                lhsT_scale=wd_s[:, 0, :].bitcast(U8)[:, ncol],
+                rhs=h_q[half][:].bitcast(FP8X4),
+                rhs_scale=h_s[:, cols],
                 start=True,
                 stop=False,
             )
             nc.tensor.matmul_mx(
                 out=bank[:],
-                lhsT=h_q[:, cols].bitcast(FP8X4),
-                lhsT_scale=h_s[:, cols],
-                rhs=wd8_w[:].bitcast(FP8X4),
-                rhs_scale=wd_s[:, 1, :].bitcast(U8),
+                lhsT=wd8_w[:, ncol].bitcast(FP8X4),
+                lhsT_scale=wd_s[:, 1, :].bitcast(U8)[:, ncol],
+                rhs=h_q[half][:].bitcast(FP8X4),
+                rhs_scale=h_s[:, cols],
                 start=False,
                 stop=True,
             )
-            nc.scalar.activation(y_t[:, b, :], bank[:], COPY, scale=gate[:, b : b + 1])
+            return bank
 
-        def turn_r(nt, half):
-            bank = ps_r.tile([P, 4, BLK], F32, name="bank_r")
-            r_t = ring.tile([P, 4, BLK], F32, name="r_t")
-            for i in range(4):
-                b = 4 * half + i
-                nc.tensor.transpose(bank[:, i, :], r_got[nt][:, b * BLK : (b + 1) * BLK], ident[:])
-            for i in range(4):
-                b = 4 * half + i
-                nc.scalar.activation(r_t[:, i, :], bank[:, i, :], COPY, scale=gate[:, b : b + 1])
-            return r_t
+        z = [keep.tile([P, J], F32, name="z%d" % i) for i in range(4)]
+        y_of, turned_of = {}, {}
 
-        def combine(nt, half, r_t, z):
-            bank = ps_z.tile([P, 4, BLK], F32, name="bank_z")
+        def product(nt, half):
+            y = ring.tile([P, HALF], F32, name="y")
+            nc.scalar.activation(y[:], down(nt, half)[:], COPY)
+            y_of[nt, half] = y
+
+        def add_turned(nt, half):
+            y = y_of[nt, half]
+            turned = psum.tile([P, 4, BLK], F32, name="bank")
             for i in range(4):
-                b = 4 * half + i
-                nc.tensor.matmul(bank[:, i, :], r_t[:, i, :], ident[:], start=True, stop=False, is_transpose=True)
+                lo = half * HALF + i * BLK
                 nc.tensor.matmul(
-                    bank[:, i, :], y_t[:, b, nt * P : (nt + 1) * P], ident[:], start=False, stop=True, is_transpose=True
+                    turned[:, i, :], r_got[nt][:, lo : lo + BLK], ident[:], start=True, stop=False, is_transpose=True
                 )
-            nc.scalar.activation(z[:, half * HALF : (half + 1) * HALF], bank[:].rearrange("p i j -> p (i j)"), COPY)
+                nc.tensor.matmul(
+                    turned[:, i, :], y[:, i * BLK : (i + 1) * BLK], ident[:], start=False, stop=True, is_transpose=True
+                )
+            z_t = ring.tile([P, 4, BLK], F32, name="z_t")
+            nc.scalar.activation(z_t[:], turned[:], COPY)
+            turned_of[nt, half] = z_t
 
-        def scatter(nt, lo, hi, z):
-            nc.vector.tensor_copy(placed[nt % 2][:].indirect(part(lo, hi)), z[:, lo:hi])
+        def turn_back(nt, half):
+            back = psum.tile([P, 4, BLK], F32, name="bank")
+            for i in range(4):
+                nc.tensor.transpose(back[:, i, :], turned_of[nt, half][:, i, :], ident[:])
+            nc.scalar.activation(z[nt][:, half * HALF : (half + 1) * HALF], back[:].rearrange("p i j -> p (i j)"), COPY)
 
-        gate_bank = ps_r.tile([P, 4, BLK], F32, name="bank_r")
-        nc.tensor.transpose(gate_bank[:, 0, :], gate_rows[:], ident[:])
-        nc.scalar.activation(gate[:], gate_bank[:, 0, 0 : J // BLK], COPY)
+        def scatter(nt, lo, hi):
+            nc.vector.tensor_tensor(placed[nt % 2][:].indirect(part(lo, hi)), z[nt][:, lo:hi], gate[:, lo:hi], MULT)
 
         gather_words(0, 0, J)
         nc.vector.tensor_copy(got_s[:], tab_s[:].bitcast(U8).indirect(offsets[:]))
@@ -188,32 +196,30 @@ def tile_list_modp_relu_res_res_kernel(
             cast_wu(a, 0)
             cast_wu(a, 1)
             quant_wu(a)
-        gather_words(1, 0, HALF)
-        gather_words(1, HALF, J)
-        for b in range(4):
+        gather_words(1, 0, 2 * BLK)
+        gather_words(1, 2 * BLK, J)
+        for b in range(8):
             up(b)
-        gather_r(0)
-        quant_h(0, HALF)
-        for b in range(4, 8):
-            up(b)
-        for b in range(4):
-            down(b)
-        quant_h(HALF, J)
-        placed.append(keep.tile([P, T], F32, name="placed1", tag="late", align_bytes=64))
-        nc.gpsimd.memset(placed[1][:], 0.0)
+        gather_r(0, 0, J)
+        quant_h(0)
+        gather_r(1, 0, J)
+        quant_h(1)
+        gather_r(2, 0, J)
+        gather_r(3, 0, J)
+        pairs = (((0, 0), (1, 0)), ((0, 1), (1, 1)), ((2, 0), (2, 1)), ((3, 0), (3, 1)))
+        for i, (first, second) in enumerate(pairs):
+            product(*first)
+            product(*second)
+            if i > 0:
+                turn_back(*pairs[i - 1][1])
+            add_turned(*first)
+            add_turned(*second)
+            turn_back(*first)
+        turn_back(*pairs[-1][1])
         for nt in range(4):
-            z = pair.tile([P, J], F32, name="z")
-            for half in range(2):
-                r_t = turn_r(nt, half)
-                if nt == 0 and half == 1:
-                    for b in range(4, 8):
-                        down(b)
-                combine(nt, half, r_t, z)
-            if nt < 3:
-                gather_r(nt + 1)
             if nt == 0:
-                scatter(nt, 0, HALF, z)
-                scatter(nt, HALF, J, z)
+                scatter(nt, 0, HALF)
+                scatter(nt, HALF, J)
             else:
-                scatter(nt, 0, J, z)
+                scatter(nt, 0, J)
             nc.sync.dma_start(out[nt * P : (nt + 1) * P, :], placed[nt % 2][:])

@@ -1,7 +1,6 @@
 from contextlib import ExitStack
 
 import concourse.mybir as mybir
-from concourse.masks import make_identity
 
 K, R, N, T, J = 1024, 512, 512, 2048, 1024
 FLOPS = 2 * K * R * J + 2 * 2 * R * N * J
@@ -15,6 +14,7 @@ U8 = mybir.dt.uint8
 FP8X4 = mybir.dt.float8_e4m3fn_x4
 FP4X4 = mybir.dt.float4_e2m1fn_x4
 MULT = mybir.AluOpType.mult
+ADD = mybir.AluOpType.add
 COPY = mybir.ActivationFunctionType.Copy
 RELU = mybir.ActivationFunctionType.Relu
 
@@ -29,7 +29,6 @@ def tile_list_modp_relu_res_res_kernel(
     nc = tc.nc
     with ExitStack() as ctx:
         keep = ctx.enter_context(tc.tile_pool(name="keep", bufs=1))
-        ring = ctx.enter_context(tc.tile_pool(name="ring", bufs=4))
         psum = ctx.enter_context(tc.psum_pool(name="psum", bufs=8))
 
         offsets = keep.tile([P, J // 16], U16, name="offsets")
@@ -38,53 +37,43 @@ def tile_list_modp_relu_res_res_kernel(
         tab_s = keep.tile([P, T // 4], I32, name="tab_s", align_bytes=64)
         wd_s = keep.tile([P, 2, N // 4], I32, name="wd_s", align_bytes=64)
         nc.vector.memset(tab_s[:], 0)
-        nc.vector.memset(wd_s[:], 0)
+        nc.gpsimd.memset(wd_s[:], 0)
         placed = [keep.tile([P, T], F32, name="placed%d" % i) for i in range(2)]
-        nc.vector.memset(placed[0][:], 0.0)
-        nc.gpsimd.memset(placed[1][:], 0.0)
+        for tile in placed:
+            nc.vector.memset(tile[:].bitcast(I32), 0)
 
         tab_w = [keep.tile([P, T], I32, name="tab_w%d" % a) for a in range(2)]
-        wu_raw = [[keep.tile([P, 4, R // 2], F32, name="wu_raw%d%d" % (a, c)) for c in range(2)] for a in range(2)]
+        wu_raw = [keep.tile([P, 4, R], F32, name="wu_raw%d" % a) for a in range(2)]
         wd4_w = keep.tile([P, N // 2], I32, name="wd4_w", align_bytes=64)
         wd8_w = keep.tile([P, N], I32, name="wd8_w", align_bytes=64)
         r_all = [keep.tile([P, T], F32, name="r_all%d" % i, align_bytes=64) for i in range(4)]
         gate = keep.tile([P, J], F32, name="gate")
-        ident = keep.tile([P, P], F32, name="ident")
-        make_identity(nc, ident[:])
 
         def load_tab(a):
             nc.sync.dma_start(tab_w[a][:], tab_words[a].rearrange("p t i -> p (t i)").bitcast(I32))
 
-        def load_wu(a, c):
-            rows = wu[512 * a : 512 * (a + 1), 256 * c : 256 * (c + 1)]
-            nc.sync.dma_start(wu_raw[a][c][:], rows.rearrange("(p j) c -> p j c", j=4))
+        def load_wu(a):
+            nc.sync.dma_start(wu_raw[a][:], wu[512 * a : 512 * (a + 1), :].rearrange("(p j) c -> p j c", j=4))
 
-        def load_tab_s(a):
-            for q in range(4):
-                rows = tab_scales[a, 4 * q : 4 * q + 4, :]
-                nc.sync.dma_start(tab_s[32 * q + 4 * a : 32 * q + 4 * a + 4, :], rows.bitcast(I32))
-
-        def load_wd_s(i, src, quads):
-            for q in quads:
-                nc.sync.dma_start(wd_s[32 * q : 32 * q + 4, i, :], src[0, 4 * q : 4 * q + 4, :].bitcast(I32))
+        def load_r(nt):
+            nc.sync.dma_start(r_all[nt][:], rT[nt * P : (nt + 1) * P, :])
 
         load_tab(0)
-        load_wu(0, 0)
-        load_tab_s(0)
-        load_wu(0, 1)
-        load_tab_s(1)
-        load_wu(1, 0)
-        load_wd_s(0, wd4_scales, (0, 1))
-        load_wu(1, 1)
-        load_wd_s(0, wd4_scales, (2, 3))
+        for q in range(4):
+            nc.sync.dma_start(tab_s[32 * q : 32 * q + 8, :], tab_scales[:, 4 * q : 4 * q + 4, :].bitcast(I32))
+        load_wu(0)
+        load_wu(1)
         load_tab(1)
-        load_wd_s(1, wd8_scales, range(4))
-        for nt in range(4):
-            nc.sync.dma_start(r_all[nt][:], rT[nt * P : (nt + 1) * P, :])
-            if nt == 1:
-                nc.sync.dma_start(wd4_w[:], wd4_words[0].bitcast(I32))
-                nc.sync.dma_start(wd8_w[:], wd8_words[0].rearrange("p n i -> p (n i)").bitcast(I32))
-        nc.sync.dma_start(gate[:], wgo)
+        nc.sync.dma_start(wd4_w[:], wd4_words[0].bitcast(I32))
+        nc.sync.dma_start(wd8_w[:], wd8_words[0].rearrange("p n i -> p (n i)").bitcast(I32))
+        load_r(0)
+        nc.sync.dma_start(gate[:, :HALF], wgo[:, :HALF])
+        nc.sync.dma_start(gate[:, HALF:], wgo[:, HALF:])
+        for nt in range(1, 4):
+            load_r(nt)
+        for i, src in enumerate((wd4_scales, wd8_scales)):
+            for q in range(4):
+                nc.gpsimd.dma_start(wd_s[32 * q : 32 * q + 4, i, :], src[0, 4 * q : 4 * q + 4, :].bitcast(I32))
 
         def part(lo, hi):
             return offsets[:, lo // 16 : hi // 16]
@@ -95,44 +84,46 @@ def tile_list_modp_relu_res_res_kernel(
         wu_q = keep.tile([P, 2, R], U32, name="wu_q", align_bytes=64)
         wu_s = keep.tile([P, 2, R], U8, name="wu_s", align_bytes=64)
         h_bf = keep.tile([P, 4 * J], BF16, name="h_bf", align_bytes=64)
-        h_q = {}
+        h_q = keep.tile([P, J], U32, name="h_q", align_bytes=64)
         h_s = keep.tile([P, J], U8, name="h_s", align_bytes=64)
-        r_got = [keep.tile([P, J], F32, name="r_got%d" % i) for i in range(4)]
+        y = [keep.tile([P, J], F32, name="y%d" % i) for i in range(4)]
+        z = [keep.tile([P, J], F32, name="z%d" % i) for i in range(4)]
 
         def gather_words(a, lo, hi):
             nc.vector.tensor_copy(got_w[a][:, lo:hi], tab_w[a][:].bitcast(U32).indirect(part(lo, hi)))
 
-        def cast_wu(a, c):
-            dst = wu_bf[a][:].rearrange("p (t m j) -> p m j t", t=4, j=4)[:, 64 * c : 64 * (c + 1), :, :]
-            nc.scalar.activation(dst, wu_raw[a][c][:].rearrange("p j (m t) -> p m j t", t=4), COPY)
+        def cast_wu(a):
+            dst = wu_bf[a][:].rearrange("p (t m j) -> p m j t", t=4, j=4)
+            src = wu_raw[a][:].rearrange("p j (m t) -> p m j t", t=4)
+            nc.scalar.activation(dst[:, :64, :, :], src[:, :64, :, :], COPY)
+            nc.vector.tensor_copy(dst[:, 64:, :, :], src[:, 64:, :, :])
 
         def quant_wu(a):
             nc.vector.quantize_mx(out=wu_q[:, a, :].bitcast(FP8X4), scales=wu_s[:, a, :], in_=wu_bf[a][:])
 
-        def up(b):
+        banks = {}
+
+        def up(b, a):
             cols = slice(b * BLK, (b + 1) * BLK)
-            bank = psum.tile([P, 4, BLK], F32, name="bank")
+            if a == 0:
+                banks[b] = psum.tile([P, 4, BLK], F32, name="bank")
             for t in range(4):
-                for a in range(2):
-                    nc.tensor.matmul_mx(
-                        out=bank[:, t, :],
-                        lhsT=wu_q[:, a, t * P : (t + 1) * P].bitcast(FP8X4),
-                        lhsT_scale=wu_s[:, a, t * P : (t + 1) * P],
-                        rhs=got_w[a][:, cols].bitcast(FP8X4),
-                        rhs_scale=got_s[4 * a :, cols],
-                        start=(a == 0),
-                        stop=(a == 1),
-                    )
-            dst = h_bf[:, 4 * b * BLK : 4 * (b + 1) * BLK].rearrange("p (n t) -> p n t", t=4)
-            nc.scalar.activation(dst, bank[:].rearrange("p t n -> p n t"), RELU)
+                nc.tensor.matmul_mx(
+                    out=banks[b][:, t, :],
+                    lhsT=wu_q[:, a, t * P : (t + 1) * P].bitcast(FP8X4),
+                    lhsT_scale=wu_s[:, a, t * P : (t + 1) * P],
+                    rhs=got_w[a][:, cols].bitcast(FP8X4),
+                    rhs_scale=got_s[4 * a :, cols],
+                    start=(a == 0 and t == 0),
+                    stop=(a == 1 and t == 3),
+                )
+            if a == 1:
+                dst = h_bf[:, 4 * b * BLK : 4 * (b + 1) * BLK].rearrange("p (n t) -> p n t", t=4)
+                nc.scalar.activation(dst, banks[b][:].rearrange("p t n -> p n t"), RELU)
 
         def quant_h(half):
             lo, hi = half * HALF, (half + 1) * HALF
-            h_q[half] = keep.tile([P, HALF], U32, name="h_q%d" % half, tag="r_all%d" % half, align_bytes=64)
-            nc.vector.quantize_mx(out=h_q[half][:].bitcast(FP8X4), scales=h_s[:, lo:hi], in_=h_bf[:, 4 * lo : 4 * hi])
-
-        def gather_r(nt, lo, hi):
-            nc.vector.tensor_copy(r_got[nt][:, lo:hi], r_all[nt][:].indirect(part(lo, hi)))
+            nc.vector.quantize_mx(out=h_q[:, lo:hi].bitcast(FP8X4), scales=h_s[:, lo:hi], in_=h_bf[:, 4 * lo : 4 * hi])
 
         def down(nt, half):
             cols = slice(half * HALF, (half + 1) * HALF)
@@ -142,7 +133,7 @@ def tile_list_modp_relu_res_res_kernel(
                 out=bank[:],
                 lhsT=wd4_w[:].bitcast(U8)[:, 2 * nt * P : 2 * (nt + 1) * P].bitcast(FP4X4),
                 lhsT_scale=wd_s[:, 0, :].bitcast(U8)[:, ncol],
-                rhs=h_q[half][:].bitcast(FP8X4),
+                rhs=h_q[:, cols].bitcast(FP8X4),
                 rhs_scale=h_s[:, cols],
                 start=True,
                 stop=False,
@@ -151,75 +142,48 @@ def tile_list_modp_relu_res_res_kernel(
                 out=bank[:],
                 lhsT=wd8_w[:, ncol].bitcast(FP8X4),
                 lhsT_scale=wd_s[:, 1, :].bitcast(U8)[:, ncol],
-                rhs=h_q[half][:].bitcast(FP8X4),
+                rhs=h_q[:, cols].bitcast(FP8X4),
                 rhs_scale=h_s[:, cols],
                 start=False,
                 stop=True,
             )
-            return bank
+            nc.scalar.activation(y[nt][:, cols], bank[:], COPY)
 
-        z = [keep.tile([P, J], F32, name="z%d" % i) for i in range(4)]
-        y_of, turned_of = {}, {}
-
-        def product(nt, half):
-            y = ring.tile([P, HALF], F32, name="y")
-            nc.scalar.activation(y[:], down(nt, half)[:], COPY)
-            y_of[nt, half] = y
-
-        def add_turned(nt, half):
-            y = y_of[nt, half]
-            turned = psum.tile([P, 4, BLK], F32, name="bank")
-            for i in range(4):
-                lo = half * HALF + i * BLK
-                nc.tensor.matmul(
-                    turned[:, i, :], r_got[nt][:, lo : lo + BLK], ident[:], start=True, stop=False, is_transpose=True
-                )
-                nc.tensor.matmul(
-                    turned[:, i, :], y[:, i * BLK : (i + 1) * BLK], ident[:], start=False, stop=True, is_transpose=True
-                )
-            z_t = ring.tile([P, 4, BLK], F32, name="z_t")
-            nc.scalar.activation(z_t[:], turned[:], COPY)
-            turned_of[nt, half] = z_t
-
-        def turn_back(nt, half):
-            back = psum.tile([P, 4, BLK], F32, name="bank")
-            for i in range(4):
-                nc.tensor.transpose(back[:, i, :], turned_of[nt, half][:, i, :], ident[:])
-            nc.scalar.activation(z[nt][:, half * HALF : (half + 1) * HALF], back[:].rearrange("p i j -> p (i j)"), COPY)
+        def add_residual(nt, lo, hi):
+            nc.vector.tensor_tensor(z[nt][:, lo:hi], r_all[nt][:].indirect(part(lo, hi)), y[nt][:, lo:hi], ADD)
 
         def scatter(nt, lo, hi):
             nc.vector.tensor_tensor(placed[nt % 2][:].indirect(part(lo, hi)), z[nt][:, lo:hi], gate[:, lo:hi], MULT)
+            if hi == J:
+                nc.sync.dma_start(out[nt * P : (nt + 1) * P, :], placed[nt % 2][:])
 
         gather_words(0, 0, J)
         nc.vector.tensor_copy(got_s[:], tab_s[:].bitcast(U8).indirect(offsets[:]))
         for a in range(2):
-            cast_wu(a, 0)
-            cast_wu(a, 1)
+            cast_wu(a)
             quant_wu(a)
         gather_words(1, 0, 2 * BLK)
-        gather_words(1, 2 * BLK, J)
-        for b in range(8):
-            up(b)
-        gather_r(0, 0, J)
+        gather_words(1, 2 * BLK, HALF)
+        gather_words(1, HALF, J)
+        for a in range(2):
+            for b in range(4):
+                up(b, a)
         quant_h(0)
-        gather_r(1, 0, J)
+        down(0, 0)
+        add_residual(0, 0, HALF)
+        for a in range(2):
+            for b in range(4, 8):
+                up(b, a)
         quant_h(1)
-        gather_r(2, 0, J)
-        gather_r(3, 0, J)
-        pairs = (((0, 0), (1, 0)), ((0, 1), (1, 1)), ((2, 0), (2, 1)), ((3, 0), (3, 1)))
-        for i, (first, second) in enumerate(pairs):
-            product(*first)
-            product(*second)
-            if i > 0:
-                turn_back(*pairs[i - 1][1])
-            add_turned(*first)
-            add_turned(*second)
-            turn_back(*first)
-        turn_back(*pairs[-1][1])
-        for nt in range(4):
-            if nt == 0:
-                scatter(nt, 0, HALF)
-                scatter(nt, HALF, J)
-            else:
-                scatter(nt, 0, J)
-            nc.sync.dma_start(out[nt * P : (nt + 1) * P, :], placed[nt % 2][:])
+        down(0, 1)
+        scatter(0, 0, HALF)
+        add_residual(0, HALF, J)
+        for nt in range(1, 4):
+            down(nt, 0)
+            down(nt, 1)
+        add_residual(1, 0, J)
+        scatter(0, HALF, J)
+        for nt in range(1, 4):
+            if nt < 3:
+                add_residual(nt + 1, 0, J)
+            scatter(nt, 0, J)

@@ -21,6 +21,7 @@ RELU = mybir.ActivationFunctionType.Relu
 P = 128
 HALF = 512
 BLK = 128
+PIECE = 256
 
 
 def tile_list_modp_relu_res_res_kernel(
@@ -37,17 +38,16 @@ def tile_list_modp_relu_res_res_kernel(
         tab_s = keep.tile([P, T // 4], I32, name="tab_s", align_bytes=64)
         wd_s = keep.tile([P, 2, N // 4], I32, name="wd_s", align_bytes=64)
         nc.vector.memset(tab_s[:], 0)
-        nc.gpsimd.memset(wd_s[:], 0)
+        nc.vector.memset(wd_s[:], 0)
         placed = [keep.tile([P, T], F32, name="placed%d" % i) for i in range(2)]
         for tile in placed:
             nc.vector.memset(tile[:].bitcast(I32), 0)
 
-        tab_w = [keep.tile([P, T], I32, name="tab_w%d" % a) for a in range(2)]
+        tab_w = [keep.tile([P, T], I32, name="tab_w%d" % a, align_bytes=64) for a in range(2)]
         wu_raw = [keep.tile([P, 4, R], F32, name="wu_raw%d" % a) for a in range(2)]
         wd4_w = keep.tile([P, N // 2], I32, name="wd4_w", align_bytes=64)
         wd8_w = keep.tile([P, N], I32, name="wd8_w", align_bytes=64)
-        r_all = [keep.tile([P, T], F32, name="r_all%d" % i, align_bytes=64) for i in range(4)]
-        gate = keep.tile([P, J], F32, name="gate")
+        r_all = {}
 
         def load_tab(a):
             nc.sync.dma_start(tab_w[a][:], tab_words[a].rearrange("p t i -> p (t i)").bitcast(I32))
@@ -55,25 +55,25 @@ def tile_list_modp_relu_res_res_kernel(
         def load_wu(a):
             nc.sync.dma_start(wu_raw[a][:], wu[512 * a : 512 * (a + 1), :].rearrange("(p j) c -> p j c", j=4))
 
-        def load_r(nt):
+        def load_r(nt, tag):
+            r_all[nt] = keep.tile([P, T], F32, name="r_all%d" % nt, tag=tag, align_bytes=64)
             nc.sync.dma_start(r_all[nt][:], rT[nt * P : (nt + 1) * P, :])
+
+        def load_wd_s(i, src, quads):
+            for q in quads:
+                nc.sync.dma_start(wd_s[32 * q : 32 * q + 4, i, :], src[0, 4 * q : 4 * q + 4, :].bitcast(I32))
 
         load_tab(0)
         for q in range(4):
             nc.sync.dma_start(tab_s[32 * q : 32 * q + 8, :], tab_scales[:, 4 * q : 4 * q + 4, :].bitcast(I32))
         load_wu(0)
         load_wu(1)
+        load_wd_s(0, wd4_scales, range(4))
+        load_wd_s(1, wd8_scales, range(2))
         load_tab(1)
-        nc.sync.dma_start(wd4_w[:], wd4_words[0].bitcast(I32))
         nc.sync.dma_start(wd8_w[:], wd8_words[0].rearrange("p n i -> p (n i)").bitcast(I32))
-        load_r(0)
-        nc.sync.dma_start(gate[:, :HALF], wgo[:, :HALF])
-        nc.sync.dma_start(gate[:, HALF:], wgo[:, HALF:])
-        for nt in range(1, 4):
-            load_r(nt)
-        for i, src in enumerate((wd4_scales, wd8_scales)):
-            for q in range(4):
-                nc.gpsimd.dma_start(wd_s[32 * q : 32 * q + 4, i, :], src[0, 4 * q : 4 * q + 4, :].bitcast(I32))
+        nc.sync.dma_start(wd4_w[:], wd4_words[0].bitcast(I32))
+        load_wd_s(1, wd8_scales, range(2, 4))
 
         def part(lo, hi):
             return offsets[:, lo // 16 : hi // 16]
@@ -84,9 +84,9 @@ def tile_list_modp_relu_res_res_kernel(
         wu_q = keep.tile([P, 2, R], U32, name="wu_q", align_bytes=64)
         wu_s = keep.tile([P, 2, R], U8, name="wu_s", align_bytes=64)
         h_bf = keep.tile([P, 4 * J], BF16, name="h_bf", align_bytes=64)
-        h_q = keep.tile([P, J], U32, name="h_q", align_bytes=64)
+        h_q = {}
         h_s = keep.tile([P, J], U8, name="h_s", align_bytes=64)
-        y = [keep.tile([P, J], F32, name="y%d" % i) for i in range(4)]
+        y = {}
         z = [keep.tile([P, J], F32, name="z%d" % i) for i in range(4)]
 
         def gather_words(a, lo, hi):
@@ -121,36 +121,48 @@ def tile_list_modp_relu_res_res_kernel(
                 dst = h_bf[:, 4 * b * BLK : 4 * (b + 1) * BLK].rearrange("p (n t) -> p n t", t=4)
                 nc.scalar.activation(dst, banks[b][:].rearrange("p t n -> p n t"), RELU)
 
-        def quant_h(half):
-            lo, hi = half * HALF, (half + 1) * HALF
-            nc.vector.quantize_mx(out=h_q[:, lo:hi].bitcast(FP8X4), scales=h_s[:, lo:hi], in_=h_bf[:, 4 * lo : 4 * hi])
+        def up_piece(c, a):
+            up(2 * c, a)
+            up(2 * c + 1, a)
 
-        def down(nt, half):
-            cols = slice(half * HALF, (half + 1) * HALF)
+        def quant_h(lo, hi):
+            codes = h_q[lo // HALF][:, lo % HALF : lo % HALF + hi - lo]
+            nc.vector.quantize_mx(out=codes.bitcast(FP8X4), scales=h_s[:, lo:hi], in_=h_bf[:, 4 * lo : 4 * hi])
+
+        def down(nt, lo, hi, dst):
             ncol = slice(nt * P, (nt + 1) * P)
+            width = HALF if hi - lo == HALF else BLK
             bank = psum.tile([P, HALF], F32, name="bank")
-            nc.tensor.matmul_mx(
-                out=bank[:],
-                lhsT=wd4_w[:].bitcast(U8)[:, 2 * nt * P : 2 * (nt + 1) * P].bitcast(FP4X4),
-                lhsT_scale=wd_s[:, 0, :].bitcast(U8)[:, ncol],
-                rhs=h_q[:, cols].bitcast(FP8X4),
-                rhs_scale=h_s[:, cols],
-                start=True,
-                stop=False,
-            )
-            nc.tensor.matmul_mx(
-                out=bank[:],
-                lhsT=wd8_w[:, ncol].bitcast(FP8X4),
-                lhsT_scale=wd_s[:, 1, :].bitcast(U8)[:, ncol],
-                rhs=h_q[:, cols].bitcast(FP8X4),
-                rhs_scale=h_s[:, cols],
-                start=False,
-                stop=True,
-            )
-            nc.scalar.activation(y[nt][:, cols], bank[:], COPY)
+            for at in range(lo, hi, width):
+                codes = h_q[at // HALF][:, at % HALF : at % HALF + width].bitcast(FP8X4)
+                nc.tensor.matmul_mx(
+                    out=bank[:, at - lo : at - lo + width],
+                    lhsT=wd4_w[:].bitcast(U8)[:, 2 * nt * P : 2 * (nt + 1) * P].bitcast(FP4X4),
+                    lhsT_scale=wd_s[:, 0, :].bitcast(U8)[:, ncol],
+                    rhs=codes,
+                    rhs_scale=h_s[:, at : at + width],
+                    start=True,
+                    stop=False,
+                )
+                nc.tensor.matmul_mx(
+                    out=bank[:, at - lo : at - lo + width],
+                    lhsT=wd8_w[:, ncol].bitcast(FP8X4),
+                    lhsT_scale=wd_s[:, 1, :].bitcast(U8)[:, ncol],
+                    rhs=codes,
+                    rhs_scale=h_s[:, at : at + width],
+                    start=False,
+                    stop=True,
+                )
+            nc.scalar.activation(dst, bank[:, : hi - lo], COPY)
+
+        def product(nt, lo, hi):
+            y[nt, lo] = keep.tile([P, hi - lo], F32, name="y%d_%d" % (nt, lo), align_bytes=64)
+            for at in range(lo, hi, HALF):
+                end = min(at + HALF, hi)
+                down(nt, at, end, y[nt, lo][:, at - lo : end - lo])
 
         def add_residual(nt, lo, hi):
-            nc.vector.tensor_tensor(z[nt][:, lo:hi], r_all[nt][:].indirect(part(lo, hi)), y[nt][:, lo:hi], ADD)
+            nc.vector.tensor_tensor(z[nt][:, lo:hi], r_all[nt][:].indirect(part(lo, hi)), y[nt, lo][:], ADD)
 
         def scatter(nt, lo, hi):
             nc.vector.tensor_tensor(placed[nt % 2][:].indirect(part(lo, hi)), z[nt][:, lo:hi], gate[:, lo:hi], MULT)
@@ -158,29 +170,44 @@ def tile_list_modp_relu_res_res_kernel(
                 nc.sync.dma_start(out[nt * P : (nt + 1) * P, :], placed[nt % 2][:])
 
         gather_words(0, 0, J)
+        gate = keep.tile([P, J], F32, name="gate", tag="tab_w0", align_bytes=64)
+        nc.sync.dma_start(gate[:, :HALF], wgo[:, :HALF])
         nc.vector.tensor_copy(got_s[:], tab_s[:].bitcast(U8).indirect(offsets[:]))
-        for a in range(2):
-            cast_wu(a)
-            quant_wu(a)
-        gather_words(1, 0, 2 * BLK)
-        gather_words(1, 2 * BLK, HALF)
+        load_r(0, "tab_s")
+        nc.sync.dma_start(gate[:, HALF:], wgo[:, HALF:])
+        cast_wu(0)
+        quant_wu(0)
+        load_r(1, "wu_bf0")
+        cast_wu(1)
+        quant_wu(1)
+        load_r(2, "wu_bf1")
+        gather_words(1, 0, PIECE)
+        gather_words(1, PIECE, HALF)
         gather_words(1, HALF, J)
-        for a in range(2):
-            for b in range(4):
-                up(b, a)
-        quant_h(0)
-        down(0, 0)
-        add_residual(0, 0, HALF)
-        for a in range(2):
-            for b in range(4, 8):
-                up(b, a)
-        quant_h(1)
-        down(0, 1)
-        scatter(0, 0, HALF)
+        load_r(3, "tab_w1")
+        h_q[0] = keep.tile([P, HALF], U32, name="h_q0", align_bytes=64)
+        up_piece(0, 0)
+        up_piece(1, 0)
+        up_piece(0, 1)
+        up_piece(1, 1)
+        up_piece(2, 0)
+        quant_h(0, PIECE)
+        product(0, 0, PIECE)
+        up_piece(2, 1)
+        quant_h(PIECE, HALF)
+        product(0, PIECE, HALF)
+        up_piece(3, 0)
+        up_piece(3, 1)
+        add_residual(0, 0, PIECE)
+        scatter(0, 0, PIECE)
+        add_residual(0, PIECE, HALF)
+        h_q[1] = keep.tile([P, HALF], U32, name="h_q1", tag="y0_%d" % PIECE, align_bytes=64)
+        quant_h(HALF, J)
+        product(0, HALF, J)
+        scatter(0, PIECE, HALF)
         add_residual(0, HALF, J)
         for nt in range(1, 4):
-            down(nt, 0)
-            down(nt, 1)
+            product(nt, 0, J)
         add_residual(1, 0, J)
         scatter(0, HALF, J)
         for nt in range(1, 4):

@@ -1,6 +1,7 @@
 from contextlib import ExitStack
 
 import concourse.mybir as mybir
+from concourse.masks import make_identity
 
 K, R, N, T, J = 1024, 512, 512, 2048, 1024
 FLOPS = 2 * K * R * J + 2 * 2 * R * N * J
@@ -14,7 +15,6 @@ U8 = mybir.dt.uint8
 FP8X4 = mybir.dt.float8_e4m3fn_x4
 FP4X4 = mybir.dt.float4_e2m1fn_x4
 MULT = mybir.AluOpType.mult
-ADD = mybir.AluOpType.add
 COPY = mybir.ActivationFunctionType.Copy
 RELU = mybir.ActivationFunctionType.Relu
 
@@ -30,6 +30,7 @@ def tile_list_modp_relu_res_res_kernel(
     nc = tc.nc
     with ExitStack() as ctx:
         keep = ctx.enter_context(tc.tile_pool(name="keep", bufs=1))
+        ring = ctx.enter_context(tc.tile_pool(name="ring", bufs=4))
         psum = ctx.enter_context(tc.psum_pool(name="psum", bufs=8))
 
         offsets = keep.tile([P, J // 16], U16, name="offsets")
@@ -48,6 +49,8 @@ def tile_list_modp_relu_res_res_kernel(
         wd4_w = keep.tile([P, N // 2], I32, name="wd4_w", align_bytes=64)
         wd8_w = keep.tile([P, N], I32, name="wd8_w", align_bytes=64)
         r_all = {}
+        ident = keep.tile([P, P], F32, name="ident")
+        make_identity(nc, ident[:])
 
         def load_tab(a):
             nc.sync.dma_start(tab_w[a][:], tab_words[a].rearrange("p t i -> p (t i)").bitcast(I32))
@@ -86,8 +89,8 @@ def tile_list_modp_relu_res_res_kernel(
         h_bf = keep.tile([P, 4 * J], BF16, name="h_bf", align_bytes=64)
         h_q = {}
         h_s = keep.tile([P, J], U8, name="h_s", align_bytes=64)
-        y = {}
-        z = [keep.tile([P, J], F32, name="z%d" % i) for i in range(4)]
+        r_got = [keep.tile([P, J], F32, name="r_got%d" % i) for i in range(4)]
+        y_t, r_t, z = {}, {}, {}
 
         def gather_words(a, lo, hi):
             nc.vector.tensor_copy(got_w[a][:, lo:hi], tab_w[a][:].bitcast(U32).indirect(part(lo, hi)))
@@ -129,51 +132,66 @@ def tile_list_modp_relu_res_res_kernel(
             codes = h_q[lo // HALF][:, lo % HALF : lo % HALF + hi - lo]
             nc.vector.quantize_mx(out=codes.bitcast(FP8X4), scales=h_s[:, lo:hi], in_=h_bf[:, 4 * lo : 4 * hi])
 
-        def down(nt, lo, hi, dst):
+        def gather_r(nt, lo, hi):
+            nc.vector.tensor_copy(r_got[nt][:, lo:hi], r_all[nt][:].indirect(part(lo, hi)))
+
+        def product(nt, lo, hi):
             ncol = slice(nt * P, (nt + 1) * P)
-            width = HALF if hi - lo == HALF else BLK
             bank = psum.tile([P, HALF], F32, name="bank")
-            for at in range(lo, hi, width):
-                codes = h_q[at // HALF][:, at % HALF : at % HALF + width].bitcast(FP8X4)
+            for at in range(lo, hi, BLK):
+                codes = h_q[at // HALF][:, at % HALF : at % HALF + BLK].bitcast(FP8X4)
                 nc.tensor.matmul_mx(
-                    out=bank[:, at - lo : at - lo + width],
-                    lhsT=wd4_w[:].bitcast(U8)[:, 2 * nt * P : 2 * (nt + 1) * P].bitcast(FP4X4),
-                    lhsT_scale=wd_s[:, 0, :].bitcast(U8)[:, ncol],
-                    rhs=codes,
-                    rhs_scale=h_s[:, at : at + width],
+                    out=bank[:, at - lo : at - lo + BLK],
+                    lhsT=codes,
+                    lhsT_scale=h_s[:, at : at + BLK],
+                    rhs=wd4_w[:].bitcast(U8)[:, 2 * nt * P : 2 * (nt + 1) * P].bitcast(FP4X4),
+                    rhs_scale=wd_s[:, 0, :].bitcast(U8)[:, ncol],
                     start=True,
                     stop=False,
                 )
                 nc.tensor.matmul_mx(
-                    out=bank[:, at - lo : at - lo + width],
-                    lhsT=wd8_w[:, ncol].bitcast(FP8X4),
-                    lhsT_scale=wd_s[:, 1, :].bitcast(U8)[:, ncol],
-                    rhs=codes,
-                    rhs_scale=h_s[:, at : at + width],
+                    out=bank[:, at - lo : at - lo + BLK],
+                    lhsT=codes,
+                    lhsT_scale=h_s[:, at : at + BLK],
+                    rhs=wd8_w[:, ncol].bitcast(FP8X4),
+                    rhs_scale=wd_s[:, 1, :].bitcast(U8)[:, ncol],
                     start=False,
                     stop=True,
                 )
+            y_t[nt, lo] = ring.tile([P, HALF], F32, name="y_t")
+            nc.scalar.activation(y_t[nt, lo][:, : hi - lo], bank[:, : hi - lo], COPY)
+
+        def turn_r(nt, lo, hi):
+            bank = psum.tile([P, HALF], F32, name="bank")
+            for at in range(lo, hi, BLK):
+                nc.tensor.transpose(bank[:, at - lo : at - lo + BLK], r_got[nt][:, at : at + BLK], ident[:])
+            r_t[nt, lo] = ring.tile([P, HALF], F32, name="r_t")
+            nc.scalar.activation(r_t[nt, lo][:, : hi - lo], bank[:, : hi - lo], COPY)
+
+        def add_back(nt, lo, hi, dst):
+            bank = psum.tile([P, HALF], F32, name="bank")
+            for at in range(0, hi - lo, BLK):
+                cols = slice(at, at + BLK)
+                nc.tensor.matmul(bank[:, cols], y_t[nt, lo][:, cols], ident[:], start=True, stop=False, is_transpose=True)
+                nc.tensor.matmul(bank[:, cols], r_t[nt, lo][:, cols], ident[:], start=False, stop=True, is_transpose=True)
             nc.scalar.activation(dst, bank[:, : hi - lo], COPY)
 
-        def product(nt, lo, hi):
-            y[nt, lo] = keep.tile([P, hi - lo], F32, name="y%d_%d" % (nt, lo), align_bytes=64)
+        def summed(nt, lo, hi):
+            z[nt, lo] = keep.tile([P, hi - lo], F32, name="z%d_%d" % (nt, lo), align_bytes=64)
             for at in range(lo, hi, HALF):
                 end = min(at + HALF, hi)
-                down(nt, at, end, y[nt, lo][:, at - lo : end - lo])
-
-        def add_residual(nt, lo, hi):
-            nc.vector.tensor_tensor(z[nt][:, lo:hi], r_all[nt][:].indirect(part(lo, hi)), y[nt, lo][:], ADD)
+                add_back(nt, at, end, z[nt, lo][:, at - lo : end - lo])
 
         def scatter(nt, lo, hi):
-            nc.vector.tensor_tensor(placed[nt % 2][:].indirect(part(lo, hi)), z[nt][:, lo:hi], gate[:, lo:hi], MULT)
+            nc.vector.tensor_tensor(placed[nt % 2][:].indirect(part(lo, hi)), z[nt, lo][:], gate[:, lo:hi], MULT)
             if hi == J:
                 nc.sync.dma_start(out[nt * P : (nt + 1) * P, :], placed[nt % 2][:])
 
         gather_words(0, 0, J)
-        gate = keep.tile([P, J], F32, name="gate", tag="tab_w0", align_bytes=64)
-        nc.sync.dma_start(gate[:, :HALF], wgo[:, :HALF])
+        load_r(0, "tab_w0")
         nc.vector.tensor_copy(got_s[:], tab_s[:].bitcast(U8).indirect(offsets[:]))
-        load_r(0, "tab_s")
+        gate = keep.tile([P, J], F32, name="gate", tag="tab_s", align_bytes=64)
+        nc.sync.dma_start(gate[:, :HALF], wgo[:, :HALF])
         nc.sync.dma_start(gate[:, HALF:], wgo[:, HALF:])
         cast_wu(0)
         quant_wu(0)
@@ -196,21 +214,27 @@ def tile_list_modp_relu_res_res_kernel(
         up_piece(2, 1)
         quant_h(PIECE, HALF)
         product(0, PIECE, HALF)
+        gather_r(0, 0, PIECE)
+        turn_r(0, 0, PIECE)
+        summed(0, 0, PIECE)
         up_piece(3, 0)
         up_piece(3, 1)
-        add_residual(0, 0, PIECE)
+        gather_r(0, PIECE, J)
+        turn_r(0, PIECE, HALF)
+        summed(0, PIECE, HALF)
+        turn_r(0, HALF, J)
         scatter(0, 0, PIECE)
-        add_residual(0, PIECE, HALF)
-        h_q[1] = keep.tile([P, HALF], U32, name="h_q1", tag="y0_%d" % PIECE, align_bytes=64)
+        h_q[1] = keep.tile([P, HALF], U32, name="h_q1", tag="z0_0", align_bytes=64)
         quant_h(HALF, J)
         product(0, HALF, J)
+        summed(0, HALF, J)
         scatter(0, PIECE, HALF)
-        add_residual(0, HALF, J)
         for nt in range(1, 4):
-            product(nt, 0, J)
-        add_residual(1, 0, J)
-        scatter(0, HALF, J)
-        for nt in range(1, 4):
-            if nt < 3:
-                add_residual(nt + 1, 0, J)
-            scatter(nt, 0, J)
+            gather_r(nt, 0, J)
+            product(nt, 0, HALF)
+            product(nt, HALF, J)
+            turn_r(nt, 0, HALF)
+            turn_r(nt, HALF, J)
+            summed(nt, 0, J)
+            scatter(nt - 1, HALF if nt == 1 else 0, J)
+        scatter(3, 0, J)

@@ -21,7 +21,6 @@ RELU = mybir.ActivationFunctionType.Relu
 P = 128
 HALF = 512
 BLK = 128
-PIECE = 256
 
 
 def tile_list_modp_relu_res_res_kernel(
@@ -34,21 +33,20 @@ def tile_list_modp_relu_res_res_kernel(
         psum = ctx.enter_context(tc.psum_pool(name="psum", bufs=8))
 
         offsets = keep.tile([P, J // 16], U16, name="offsets")
-        nc.sync.dma_start(offsets[:], offs)
 
         tab_s = keep.tile([P, T // 4], I32, name="tab_s", align_bytes=64)
         wd_s = keep.tile([P, 2, N // 4], I32, name="wd_s", align_bytes=64)
         nc.vector.memset(tab_s[:], 0)
         nc.vector.memset(wd_s[:], 0)
-        placed = [keep.tile([P, T], F32, name="placed%d" % i) for i in range(2)]
-        for tile in placed:
-            nc.vector.memset(tile[:].bitcast(I32), 0)
+        placed = [keep.tile([P, T], F32, name="placed0")]
+        nc.vector.memset(placed[0][:].bitcast(I32), 0)
 
         tab_w = [keep.tile([P, T], I32, name="tab_w%d" % a, align_bytes=64) for a in range(2)]
         wu_raw = [keep.tile([P, 4, R], F32, name="wu_raw%d" % a) for a in range(2)]
         wd4_w = keep.tile([P, N // 2], I32, name="wd4_w", align_bytes=64)
         wd8_w = keep.tile([P, N], I32, name="wd8_w", align_bytes=64)
-        r_all = {}
+        r_all = [keep.tile([P, T], F32, name="r_all%d" % nt, align_bytes=64) for nt in range(4)]
+        gate = keep.tile([P, J], F32, name="gate")
         ident = keep.tile([P, P], F32, name="ident")
         make_identity(nc, ident[:])
 
@@ -58,30 +56,34 @@ def tile_list_modp_relu_res_res_kernel(
         def load_wu(a):
             nc.sync.dma_start(wu_raw[a][:], wu[512 * a : 512 * (a + 1), :].rearrange("(p j) c -> p j c", j=4))
 
-        def load_r(nt, tag):
-            r_all[nt] = keep.tile([P, T], F32, name="r_all%d" % nt, tag=tag, align_bytes=64)
+        def load_r(nt):
             nc.sync.dma_start(r_all[nt][:], rT[nt * P : (nt + 1) * P, :])
 
-        def load_wd_s(i, src, quads):
-            for q in quads:
+        def load_wd_s(i, src):
+            for q in range(4):
                 nc.sync.dma_start(wd_s[32 * q : 32 * q + 4, i, :], src[0, 4 * q : 4 * q + 4, :].bitcast(I32))
 
         load_tab(0)
+        nc.sync.dma_start(offsets[:], offs)
         for q in range(4):
             nc.sync.dma_start(tab_s[32 * q : 32 * q + 8, :], tab_scales[:, 4 * q : 4 * q + 4, :].bitcast(I32))
         load_wu(0)
-        load_wu(1)
-        load_wd_s(0, wd4_scales, range(4))
-        load_wd_s(1, wd8_scales, range(2))
         load_tab(1)
+        load_wu(1)
+        load_r(0)
+        load_wd_s(0, wd4_scales)
+        load_r(1)
         nc.sync.dma_start(wd8_w[:], wd8_words[0].rearrange("p n i -> p (n i)").bitcast(I32))
         nc.sync.dma_start(wd4_w[:], wd4_words[0].bitcast(I32))
-        load_wd_s(1, wd8_scales, range(2, 4))
+        load_wd_s(1, wd8_scales)
+        load_r(2)
+        load_r(3)
+        nc.sync.dma_start(gate[:], wgo)
 
         def part(lo, hi):
             return offsets[:, lo // 16 : hi // 16]
 
-        got_w = [keep.tile([P, J], U32, name="got_w%d" % a, align_bytes=64) for a in range(2)]
+        got_w = {}
         got_s = keep.tile([P, J], U8, name="got_s", align_bytes=64)
         wu_bf = [keep.tile([P, 4 * R], BF16, name="wu_bf%d" % a, align_bytes=64) for a in range(2)]
         wu_q = keep.tile([P, 2, R], U32, name="wu_q", align_bytes=64)
@@ -92,14 +94,16 @@ def tile_list_modp_relu_res_res_kernel(
         r_got = [keep.tile([P, J], F32, name="r_got%d" % i) for i in range(4)]
         y_t, r_t, z = {}, {}, {}
 
-        def gather_words(a, lo, hi):
-            nc.vector.tensor_copy(got_w[a][:, lo:hi], tab_w[a][:].bitcast(U32).indirect(part(lo, hi)))
+        def gather_words(a, tag):
+            got_w[a] = keep.tile([P, J], U32, name="got_w%d" % a, tag=tag, align_bytes=64)
+            nc.vector.tensor_copy(got_w[a][:], tab_w[a][:].bitcast(U32).indirect(offsets[:]))
 
-        def cast_wu(a):
+        def cast_wu(a, split):
             dst = wu_bf[a][:].rearrange("p (t m j) -> p m j t", t=4, j=4)
             src = wu_raw[a][:].rearrange("p j (m t) -> p m j t", t=4)
-            nc.scalar.activation(dst[:, :64, :, :], src[:, :64, :, :], COPY)
-            nc.vector.tensor_copy(dst[:, 64:, :, :], src[:, 64:, :, :])
+            nc.scalar.activation(dst[:, :split, :, :], src[:, :split, :, :], COPY)
+            if split < P:
+                nc.vector.tensor_copy(dst[:, split:, :, :], src[:, split:, :, :])
 
         def quant_wu(a):
             nc.vector.quantize_mx(out=wu_q[:, a, :].bitcast(FP8X4), scales=wu_s[:, a, :], in_=wu_bf[a][:])
@@ -124,13 +128,10 @@ def tile_list_modp_relu_res_res_kernel(
                 dst = h_bf[:, 4 * b * BLK : 4 * (b + 1) * BLK].rearrange("p (n t) -> p n t", t=4)
                 nc.scalar.activation(dst, banks[b][:].rearrange("p t n -> p n t"), RELU)
 
-        def up_piece(c, a):
-            up(2 * c, a)
-            up(2 * c + 1, a)
-
-        def quant_h(lo, hi):
-            codes = h_q[lo // HALF][:, lo % HALF : lo % HALF + hi - lo]
-            nc.vector.quantize_mx(out=codes.bitcast(FP8X4), scales=h_s[:, lo:hi], in_=h_bf[:, 4 * lo : 4 * hi])
+        def quant_h(half, tag):
+            lo, hi = half * HALF, (half + 1) * HALF
+            h_q[half] = keep.tile([P, HALF], U32, name="h_q%d" % half, tag=tag, align_bytes=64)
+            nc.vector.quantize_mx(out=h_q[half][:].bitcast(FP8X4), scales=h_s[:, lo:hi], in_=h_bf[:, 4 * lo : 4 * hi])
 
         def gather_r(nt, lo, hi):
             nc.vector.tensor_copy(r_got[nt][:, lo:hi], r_all[nt][:].indirect(part(lo, hi)))
@@ -176,65 +177,34 @@ def tile_list_modp_relu_res_res_kernel(
                 nc.tensor.matmul(bank[:, cols], r_t[nt, lo][:, cols], ident[:], start=False, stop=True, is_transpose=True)
             nc.scalar.activation(dst, bank[:, : hi - lo], COPY)
 
-        def summed(nt, lo, hi):
-            z[nt, lo] = keep.tile([P, hi - lo], F32, name="z%d_%d" % (nt, lo), align_bytes=64)
-            for at in range(lo, hi, HALF):
-                end = min(at + HALF, hi)
-                add_back(nt, at, end, z[nt, lo][:, at - lo : end - lo])
-
         def scatter(nt, lo, hi):
             nc.vector.tensor_tensor(placed[nt % 2][:].indirect(part(lo, hi)), z[nt, lo][:], gate[:, lo:hi], MULT)
             if hi == J:
                 nc.sync.dma_start(out[nt * P : (nt + 1) * P, :], placed[nt % 2][:])
 
-        gather_words(0, 0, J)
-        load_r(0, "tab_w0")
+        gather_words(0, "got_w0")
         nc.vector.tensor_copy(got_s[:], tab_s[:].bitcast(U8).indirect(offsets[:]))
-        gate = keep.tile([P, J], F32, name="gate", tag="tab_s", align_bytes=64)
-        nc.sync.dma_start(gate[:, :HALF], wgo[:, :HALF])
-        nc.sync.dma_start(gate[:, HALF:], wgo[:, HALF:])
-        cast_wu(0)
+        cast_wu(0, P)
         quant_wu(0)
-        load_r(1, "wu_bf0")
-        cast_wu(1)
+        gather_words(1, "wu_bf0")
+        cast_wu(1, 80)
         quant_wu(1)
-        load_r(2, "wu_bf1")
-        gather_words(1, 0, PIECE)
-        gather_words(1, PIECE, HALF)
-        gather_words(1, HALF, J)
-        load_r(3, "tab_w1")
-        h_q[0] = keep.tile([P, HALF], U32, name="h_q0", align_bytes=64)
-        up_piece(0, 0)
-        up_piece(1, 0)
-        up_piece(0, 1)
-        up_piece(1, 1)
-        up_piece(2, 0)
-        quant_h(0, PIECE)
-        product(0, 0, PIECE)
-        up_piece(2, 1)
-        quant_h(PIECE, HALF)
-        product(0, PIECE, HALF)
-        gather_r(0, 0, PIECE)
-        turn_r(0, 0, PIECE)
-        summed(0, 0, PIECE)
-        up_piece(3, 0)
-        up_piece(3, 1)
-        gather_r(0, PIECE, J)
-        turn_r(0, PIECE, HALF)
-        summed(0, PIECE, HALF)
-        turn_r(0, HALF, J)
-        scatter(0, 0, PIECE)
-        h_q[1] = keep.tile([P, HALF], U32, name="h_q1", tag="z0_0", align_bytes=64)
-        quant_h(HALF, J)
-        product(0, HALF, J)
-        summed(0, HALF, J)
-        scatter(0, PIECE, HALF)
-        for nt in range(1, 4):
-            gather_r(nt, 0, J)
-            product(nt, 0, HALF)
-            product(nt, HALF, J)
-            turn_r(nt, 0, HALF)
-            turn_r(nt, HALF, J)
-            summed(nt, 0, J)
-            scatter(nt - 1, HALF if nt == 1 else 0, J)
-        scatter(3, 0, J)
+        for a in range(2):
+            for b in range(8):
+                up(b, a)
+        gather_r(0, 0, J)
+        quant_h(0, "h_q0")
+        gather_r(1, 0, J)
+        quant_h(1, "r_all1")
+        gather_r(2, 0, J)
+        gather_r(3, 0, J)
+        placed.append(keep.tile([P, T], F32, name="placed1", tag="r_all3", align_bytes=64))
+        nc.gpsimd.memset(placed[1][:], 0.0)
+        for nt in range(4):
+            z[nt, 0] = keep.tile([P, J], F32, name="z%d" % nt)
+            for lo in (0, HALF):
+                product(nt, lo, lo + HALF)
+                turn_r(nt, lo, lo + HALF)
+                add_back(nt, lo, lo + HALF, z[nt, 0][:, lo : lo + HALF])
+        for nt in range(4):
+            scatter(nt, 0, J)

@@ -29,7 +29,7 @@ def tile_list_modp_relu_res_res_kernel(
     nc = tc.nc
     with ExitStack() as ctx:
         keep = ctx.enter_context(tc.tile_pool(name="keep", bufs=1))
-        ring = ctx.enter_context(tc.tile_pool(name="ring", bufs=4))
+        ring = ctx.enter_context(tc.tile_pool(name="ring", bufs=8))
         psum = ctx.enter_context(tc.psum_pool(name="psum", bufs=8))
 
         offsets = keep.tile([P, J // 16], U16, name="offsets")
@@ -92,7 +92,8 @@ def tile_list_modp_relu_res_res_kernel(
         h_q = {}
         h_s = keep.tile([P, J], U8, name="h_s", align_bytes=64)
         r_got = [keep.tile([P, J], F32, name="r_got%d" % i) for i in range(4)]
-        y_t, r_t, z = {}, {}, {}
+        z = [keep.tile([P, J], F32, name="z%d" % i) for i in range(4)]
+        y_t, r_t = {}, {}
 
         def gather_words(a, tag):
             got_w[a] = keep.tile([P, J], U32, name="got_w%d" % a, tag=tag, align_bytes=64)
@@ -178,7 +179,7 @@ def tile_list_modp_relu_res_res_kernel(
             nc.scalar.activation(dst, bank[:, : hi - lo], COPY)
 
         def scatter(nt, lo, hi):
-            nc.vector.tensor_tensor(placed[nt % 2][:].indirect(part(lo, hi)), z[nt, lo][:], gate[:, lo:hi], MULT)
+            nc.vector.tensor_tensor(placed[nt % 2][:].indirect(part(lo, hi)), z[nt][:, lo:hi], gate[:, lo:hi], MULT)
             if hi == J:
                 nc.sync.dma_start(out[nt * P : (nt + 1) * P, :], placed[nt % 2][:])
 
@@ -193,18 +194,34 @@ def tile_list_modp_relu_res_res_kernel(
             for b in range(8):
                 up(b, a)
         gather_r(0, 0, J)
+        turn_r(0, 0, HALF)
+        turn_r(0, HALF, J)
         quant_h(0, "h_q0")
+        product(0, 0, HALF)
+        product(1, 0, HALF)
+        add_back(0, 0, HALF, z[0][:, :HALF])
         gather_r(1, 0, J)
+        turn_r(1, 0, HALF)
+        turn_r(1, HALF, J)
         quant_h(1, "r_all1")
-        gather_r(2, 0, J)
-        gather_r(3, 0, J)
+        product(0, HALF, J)
+        product(1, HALF, J)
+        add_back(0, HALF, J, z[0][:, HALF:])
+        add_back(1, 0, HALF, z[1][:, :HALF])
+        add_back(1, HALF, J, z[1][:, HALF:])
+        for nt in (2, 3):
+            product(nt, 0, HALF)
+            product(nt, HALF, J)
+        for nt in (2, 3):
+            gather_r(nt, 0, J)
+            turn_r(nt, 0, HALF)
+            turn_r(nt, HALF, J)
+        for nt in (2, 3):
+            add_back(nt, 0, HALF, z[nt][:, :HALF])
+            add_back(nt, HALF, J, z[nt][:, HALF:])
         placed.append(keep.tile([P, T], F32, name="placed1", tag="r_all3", align_bytes=64))
         nc.gpsimd.memset(placed[1][:], 0.0)
-        for nt in range(4):
-            z[nt, 0] = keep.tile([P, J], F32, name="z%d" % nt)
-            for lo in (0, HALF):
-                product(nt, lo, lo + HALF)
-                turn_r(nt, lo, lo + HALF)
-                add_back(nt, lo, lo + HALF, z[nt, 0][:, lo : lo + HALF])
-        for nt in range(4):
+        scatter(0, 0, HALF)
+        scatter(0, HALF, J)
+        for nt in range(1, 4):
             scatter(nt, 0, J)

@@ -38,8 +38,9 @@ def tile_list_modp_relu_res_res_kernel(
         wd_s = keep.tile([P, 2, N // 4], I32, name="wd_s", align_bytes=64)
         nc.vector.memset(tab_s[:], 0)
         nc.vector.memset(wd_s[:], 0)
-        placed = [keep.tile([P, T], F32, name="placed0")]
-        nc.vector.memset(placed[0][:].bitcast(I32), 0)
+        placed = [keep.tile([P, T], F32, name="placed%d" % i) for i in range(2)]
+        for tile in placed:
+            nc.vector.memset(tile[:].bitcast(I32), 0)
 
         tab_w = [keep.tile([P, T], I32, name="tab_w%d" % a, align_bytes=64) for a in range(2)]
         wu_raw = [keep.tile([P, 4, R], F32, name="wu_raw%d" % a) for a in range(2)]
@@ -219,8 +220,6 @@ def tile_list_modp_relu_res_res_kernel(
         for nt in (2, 3):
             add_back(nt, 0, HALF, z[nt][:, :HALF])
             add_back(nt, HALF, J, z[nt][:, HALF:])
-        placed.append(keep.tile([P, T], F32, name="placed1", tag="r_all3", align_bytes=64))
-        nc.gpsimd.memset(placed[1][:], 0.0)
         scatter(0, 0, HALF)
         scatter(0, HALF, J)
         for nt in range(1, 4):

@@ -78,8 +78,8 @@ def tile_list_modp_relu_res_res_kernel(
         nc.sync.dma_start(wd4_w[:], wd4_words[0].bitcast(I32))
         load_wd_s(1, wd8_scales)
         load_r(2)
-        load_r(3)
         nc.sync.dma_start(gate[:], wgo)
+        load_r(3)
 
         def part(lo, hi):
             return offsets[:, lo // 16 : hi // 16]
@@ -217,10 +217,8 @@ def tile_list_modp_relu_res_res_kernel(
             gather_r(nt, 0, J)
             turn_r(nt, 0, HALF)
             turn_r(nt, HALF, J)
-        for nt in (2, 3):
             add_back(nt, 0, HALF, z[nt][:, :HALF])
             add_back(nt, HALF, J, z[nt][:, HALF:])
-        scatter(0, 0, HALF)
-        scatter(0, HALF, J)
+            scatter(0, (nt - 2) * HALF, (nt - 1) * HALF)
         for nt in range(1, 4):
             scatter(nt, 0, J)

@@ -186,7 +186,7 @@ def tile_list_modp_relu_res_res_kernel(
 
         gather_words(0, "got_w0")
         nc.vector.tensor_copy(got_s[:], tab_s[:].bitcast(U8).indirect(offsets[:]))
-        cast_wu(0, P)
+        cast_wu(0, 80)
         quant_wu(0)
         gather_words(1, "wu_bf0")
         cast_wu(1, 80)

@@ -15,6 +15,7 @@ U8 = mybir.dt.uint8
 FP8X4 = mybir.dt.float8_e4m3fn_x4
 FP4X4 = mybir.dt.float4_e2m1fn_x4
 MULT = mybir.AluOpType.mult
+ADD = mybir.AluOpType.add
 COPY = mybir.ActivationFunctionType.Copy
 RELU = mybir.ActivationFunctionType.Relu
 
@@ -36,6 +37,8 @@ def tile_list_modp_relu_res_res_kernel(
 
         tab_s = keep.tile([P, T // 4], I32, name="tab_s", align_bytes=64)
         wd_s = keep.tile([P, 2, N // 4], I32, name="wd_s", align_bytes=64)
+        gate_rows = keep.tile([P, P], F32, name="gate_rows")
+        nc.vector.memset(gate_rows[:].bitcast(I32), 0)
         nc.vector.memset(tab_s[:], 0)
         nc.vector.memset(wd_s[:], 0)
         placed = [keep.tile([P, T], F32, name="placed%d" % i) for i in range(2)]
@@ -66,6 +69,7 @@ def tile_list_modp_relu_res_res_kernel(
 
         load_tab(0)
         nc.sync.dma_start(offsets[:], offs)
+        nc.sync.dma_start(gate_rows[0 : J // BLK, :], wgo[0].rearrange("(b c) -> b c", c=BLK))
         for q in range(4):
             nc.sync.dma_start(tab_s[32 * q : 32 * q + 8, :], tab_scales[:, 4 * q : 4 * q + 4, :].bitcast(I32))
         load_wu(0)
@@ -78,7 +82,6 @@ def tile_list_modp_relu_res_res_kernel(
         nc.sync.dma_start(wd4_w[:], wd4_words[0].bitcast(I32))
         load_wd_s(1, wd8_scales)
         load_r(2)
-        nc.sync.dma_start(gate[:], wgo)
         load_r(3)
 
         def part(lo, hi):
@@ -90,11 +93,11 @@ def tile_list_modp_relu_res_res_kernel(
         wu_q = keep.tile([P, 2, R], U32, name="wu_q", align_bytes=64)
         wu_s = keep.tile([P, 2, R], U8, name="wu_s", align_bytes=64)
         h_bf = keep.tile([P, 4 * J], BF16, name="h_bf", align_bytes=64)
-        h_q = {}
         h_s = keep.tile([P, J], U8, name="h_s", align_bytes=64)
         r_got = [keep.tile([P, J], F32, name="r_got%d" % i) for i in range(4)]
-        z = [keep.tile([P, J], F32, name="z%d" % i) for i in range(4)]
-        y_t, r_t = {}, {}
+        z = {}
+        y_t = {}
+        gate_col = keep.tile([P, J // BLK], F32, name="gate_col")
 
         def gather_words(a, tag):
             got_w[a] = keep.tile([P, J], U32, name="got_w%d" % a, tag=tag, align_bytes=64)
@@ -130,21 +133,33 @@ def tile_list_modp_relu_res_res_kernel(
                 dst = h_bf[:, 4 * b * BLK : 4 * (b + 1) * BLK].rearrange("p (n t) -> p n t", t=4)
                 nc.scalar.activation(dst, banks[b][:].rearrange("p t n -> p n t"), RELU)
 
-        def quant_h(half, tag):
+        def quant_h(half):
             lo, hi = half * HALF, (half + 1) * HALF
-            h_q[half] = keep.tile([P, HALF], U32, name="h_q%d" % half, tag=tag, align_bytes=64)
-            nc.vector.quantize_mx(out=h_q[half][:].bitcast(FP8X4), scales=h_s[:, lo:hi], in_=h_bf[:, 4 * lo : 4 * hi])
+            nc.vector.quantize_mx(out=h_q[:, lo:hi].bitcast(FP8X4), scales=h_s[:, lo:hi], in_=h_bf[:, 4 * lo : 4 * hi])
 
-        def gather_r(nt, lo, hi):
-            nc.vector.tensor_copy(r_got[nt][:, lo:hi], r_all[nt][:].indirect(part(lo, hi)))
+        def spread_gate():
+            bank = psum.tile([P, HALF], F32, name="bank")
+            nc.tensor.transpose(bank[:, :P], gate_rows[:], ident[:])
+            nc.scalar.activation(gate_col[:], bank[:, : J // BLK], COPY)
+            for half in range(2):
+                bank = psum.tile([P, HALF], F32, name="bank")
+                for i in range(4):
+                    b = 4 * half + i
+                    nc.tensor.transpose(bank[:, i * BLK : (i + 1) * BLK], gate_col[:, b : b + 1].to_broadcast([P, P]), ident[:])
+                nc.scalar.activation(gate[:, half * HALF : (half + 1) * HALF], bank[:], COPY)
 
-        def product(nt, lo, hi):
+        def gather_r(nt):
+            nc.vector.tensor_tensor(r_got[nt][:], r_all[nt][:].indirect(offsets[:]), gate[:], MULT)
+
+        def product(nt, half):
             ncol = slice(nt * P, (nt + 1) * P)
             bank = psum.tile([P, HALF], F32, name="bank")
-            for at in range(lo, hi, BLK):
-                codes = h_q[at // HALF][:, at % HALF : at % HALF + BLK].bitcast(FP8X4)
+            y_t[nt, half] = ring.tile([P, HALF], F32, name="y_t")
+            for i in range(4):
+                at = half * HALF + i * BLK
+                codes = h_q[:, at : at + BLK].bitcast(FP8X4)
                 nc.tensor.matmul_mx(
-                    out=bank[:, at - lo : at - lo + BLK],
+                    out=bank[:, i * BLK : (i + 1) * BLK],
                     lhsT=codes,
                     lhsT_scale=h_s[:, at : at + BLK],
                     rhs=wd4_w[:].bitcast(U8)[:, 2 * nt * P : 2 * (nt + 1) * P].bitcast(FP4X4),
@@ -153,7 +168,7 @@ def tile_list_modp_relu_res_res_kernel(
                     stop=False,
                 )
                 nc.tensor.matmul_mx(
-                    out=bank[:, at - lo : at - lo + BLK],
+                    out=bank[:, i * BLK : (i + 1) * BLK],
                     lhsT=codes,
                     lhsT_scale=h_s[:, at : at + BLK],
                     rhs=wd8_w[:, ncol].bitcast(FP8X4),
@@ -161,29 +176,26 @@ def tile_list_modp_relu_res_res_kernel(
                     start=False,
                     stop=True,
                 )
-            y_t[nt, lo] = ring.tile([P, HALF], F32, name="y_t")
-            nc.scalar.activation(y_t[nt, lo][:, : hi - lo], bank[:, : hi - lo], COPY)
+            for i in range(4):
+                b = 4 * half + i
+                cols = slice(i * BLK, (i + 1) * BLK)
+                nc.scalar.activation(y_t[nt, half][:, cols], bank[:, cols], COPY, scale=gate_col[:, b : b + 1])
 
-        def turn_r(nt, lo, hi):
+        def turn_back(nt, half, tag=None):
+            if half == 0:
+                z[nt] = keep.tile([P, J], F32, name="z%d" % nt, tag=tag or "z%d" % nt, align_bytes=64)
             bank = psum.tile([P, HALF], F32, name="bank")
-            for at in range(lo, hi, BLK):
-                nc.tensor.transpose(bank[:, at - lo : at - lo + BLK], r_got[nt][:, at : at + BLK], ident[:])
-            r_t[nt, lo] = ring.tile([P, HALF], F32, name="r_t")
-            nc.scalar.activation(r_t[nt, lo][:, : hi - lo], bank[:, : hi - lo], COPY)
+            for i in range(4):
+                cols = slice(i * BLK, (i + 1) * BLK)
+                nc.tensor.transpose(bank[:, cols], y_t[nt, half][:, cols], ident[:])
+            nc.scalar.activation(z[nt][:, half * HALF : (half + 1) * HALF], bank[:], COPY)
 
-        def add_back(nt, lo, hi, dst):
-            bank = psum.tile([P, HALF], F32, name="bank")
-            for at in range(0, hi - lo, BLK):
-                cols = slice(at, at + BLK)
-                nc.tensor.matmul(bank[:, cols], y_t[nt, lo][:, cols], ident[:], start=True, stop=False, is_transpose=True)
-                nc.tensor.matmul(bank[:, cols], r_t[nt, lo][:, cols], ident[:], start=False, stop=True, is_transpose=True)
-            nc.scalar.activation(dst, bank[:, : hi - lo], COPY)
-
-        def scatter(nt, lo, hi):
-            nc.vector.tensor_tensor(placed[nt % 2][:].indirect(part(lo, hi)), z[nt][:, lo:hi], gate[:, lo:hi], MULT)
+        def scatter(turn, nt, lo, hi):
+            nc.vector.tensor_tensor(placed[turn % 2][:].indirect(part(lo, hi)), z[nt][:, lo:hi], r_got[nt][:, lo:hi], ADD)
             if hi == J:
-                nc.sync.dma_start(out[nt * P : (nt + 1) * P, :], placed[nt % 2][:])
+                nc.sync.dma_start(out[nt * P : (nt + 1) * P, :], placed[turn % 2][:])
 
+        spread_gate()
         gather_words(0, "got_w0")
         nc.vector.tensor_copy(got_s[:], tab_s[:].bitcast(U8).indirect(offsets[:]))
         cast_wu(0, 80)
@@ -194,31 +206,25 @@ def tile_list_modp_relu_res_res_kernel(
         for a in range(2):
             for b in range(8):
                 up(b, a)
-        gather_r(0, 0, J)
-        turn_r(0, 0, HALF)
-        turn_r(0, HALF, J)
-        quant_h(0, "h_q0")
-        product(0, 0, HALF)
-        product(1, 0, HALF)
-        add_back(0, 0, HALF, z[0][:, :HALF])
-        gather_r(1, 0, J)
-        turn_r(1, 0, HALF)
-        turn_r(1, HALF, J)
-        quant_h(1, "r_all1")
-        product(0, HALF, J)
-        product(1, HALF, J)
-        add_back(0, HALF, J, z[0][:, HALF:])
-        add_back(1, 0, HALF, z[1][:, :HALF])
-        add_back(1, HALF, J, z[1][:, HALF:])
-        for nt in (2, 3):
-            product(nt, 0, HALF)
-            product(nt, HALF, J)
-        for nt in (2, 3):
-            gather_r(nt, 0, J)
-            turn_r(nt, 0, HALF)
-            turn_r(nt, HALF, J)
-            add_back(nt, 0, HALF, z[nt][:, :HALF])
-            add_back(nt, HALF, J, z[nt][:, HALF:])
-            scatter(0, (nt - 2) * HALF, (nt - 1) * HALF)
-        for nt in range(1, 4):
-            scatter(nt, 0, J)
+        gather_r(0)
+        gather_r(1)
+        h_q = keep.tile([P, J], U32, name="h_q", tag="r_all1", align_bytes=64)
+        quant_h(0)
+        quant_h(1)
+        product(3, 0)
+        product(3, 1)
+        turn_back(3, 0)
+        product(0, 0)
+        turn_back(3, 1)
+        product(0, 1)
+        gather_r(2)
+        gather_r(3)
+        for nt in range(3):
+            for half in range(2):
+                if nt < 2:
+                    product(nt + 1, half)
+                turn_back(nt, half, "r_all3" if nt == 0 else None)
+        scatter(0, 3, 0, HALF)
+        scatter(0, 3, HALF, J)
+        for nt in range(3):
+            scatter(nt + 1, nt, 0, J)

@@ -31,7 +31,7 @@ def tile_list_modp_relu_res_res_kernel(
     with ExitStack() as ctx:
         keep = ctx.enter_context(tc.tile_pool(name="keep", bufs=1))
         ring = ctx.enter_context(tc.tile_pool(name="ring", bufs=8))
-        psum = ctx.enter_context(tc.psum_pool(name="psum", bufs=8))
+        psum = ctx.enter_context(tc.psum_pool(name="psum", bufs=1))
 
         offsets = keep.tile([P, J // 16], U16, name="offsets")
 
@@ -96,7 +96,7 @@ def tile_list_modp_relu_res_res_kernel(
         h_s = keep.tile([P, J], U8, name="h_s", align_bytes=64)
         r_got = [keep.tile([P, J], F32, name="r_got%d" % i) for i in range(4)]
         z = {}
-        y_t = {}
+        y_t, r_t = {}, {}
         gate_col = keep.tile([P, J // BLK], F32, name="gate_col")
 
         def gather_words(a, tag):
@@ -118,7 +118,7 @@ def tile_list_modp_relu_res_res_kernel(
         def up(b, a):
             cols = slice(b * BLK, (b + 1) * BLK)
             if a == 0:
-                banks[b] = psum.tile([P, 4, BLK], F32, name="bank")
+                banks[b] = psum.tile([P, 4, BLK], F32, name="bank%d" % b)
             for t in range(4):
                 nc.tensor.matmul_mx(
                     out=banks[b][:, t, :],
@@ -138,22 +138,22 @@ def tile_list_modp_relu_res_res_kernel(
             nc.vector.quantize_mx(out=h_q[:, lo:hi].bitcast(FP8X4), scales=h_s[:, lo:hi], in_=h_bf[:, 4 * lo : 4 * hi])
 
         def spread_gate():
-            bank = psum.tile([P, HALF], F32, name="bank")
+            bank = psum.tile([P, HALF], F32, name="bank0")
             nc.tensor.transpose(bank[:, :P], gate_rows[:], ident[:])
             nc.scalar.activation(gate_col[:], bank[:, : J // BLK], COPY)
             for half in range(2):
-                bank = psum.tile([P, HALF], F32, name="bank")
+                bank = psum.tile([P, HALF], F32, name="bank%d" % (1 + half))
                 for i in range(4):
                     b = 4 * half + i
                     nc.tensor.transpose(bank[:, i * BLK : (i + 1) * BLK], gate_col[:, b : b + 1].to_broadcast([P, P]), ident[:])
                 nc.scalar.activation(gate[:, half * HALF : (half + 1) * HALF], bank[:], COPY)
 
         def gather_r(nt):
-            nc.vector.tensor_tensor(r_got[nt][:], r_all[nt][:].indirect(offsets[:]), gate[:], MULT)
+            nc.vector.tensor_copy(r_got[nt][:], r_all[nt][:].indirect(offsets[:]))
 
         def product(nt, half):
             ncol = slice(nt * P, (nt + 1) * P)
-            bank = psum.tile([P, HALF], F32, name="bank")
+            bank = psum.tile([P, HALF], F32, name="bank%d" % half)
             y_t[nt, half] = ring.tile([P, HALF], F32, name="y_t")
             for i in range(4):
                 at = half * HALF + i * BLK
@@ -176,22 +176,55 @@ def tile_list_modp_relu_res_res_kernel(
                     start=False,
                     stop=True,
                 )
+            nc.scalar.activation(y_t[nt, half][:], bank[:], COPY)
+
+        def turn_r(nt, half):
+            bank = psum.tile([P, HALF], F32, name="bank%d" % (2 + half))
             for i in range(4):
-                b = 4 * half + i
-                cols = slice(i * BLK, (i + 1) * BLK)
-                nc.scalar.activation(y_t[nt, half][:, cols], bank[:, cols], COPY, scale=gate_col[:, b : b + 1])
+                at = half * HALF + i * BLK
+                nc.tensor.transpose(bank[:, i * BLK : (i + 1) * BLK], r_got[nt][:, at : at + BLK], ident[:])
+            r_t[nt, half] = ring.tile([P, HALF], F32, name="r_t")
+            nc.scalar.activation(r_t[nt, half][:], bank[:], COPY)
+
+        def product_plain(nt, quarter):
+            ncol = slice(nt * P, (nt + 1) * P)
+            if quarter == 0:
+                z[nt] = keep.tile([P, J], F32, name="z%d" % nt, align_bytes=64)
+            bank = psum.tile([P, HALF], F32, name="bank%d" % quarter)
+            for i in range(2):
+                cols = slice((2 * quarter + i) * BLK, (2 * quarter + i + 1) * BLK)
+                nc.tensor.matmul_mx(
+                    out=bank[:, i * BLK : (i + 1) * BLK],
+                    lhsT=wd4_w[:].bitcast(U8)[:, 2 * nt * P : 2 * (nt + 1) * P].bitcast(FP4X4),
+                    lhsT_scale=wd_s[:, 0, :].bitcast(U8)[:, ncol],
+                    rhs=h_q[:, cols].bitcast(FP8X4),
+                    rhs_scale=h_s[:, cols],
+                    start=True,
+                    stop=False,
+                )
+                nc.tensor.matmul_mx(
+                    out=bank[:, i * BLK : (i + 1) * BLK],
+                    lhsT=wd8_w[:, ncol].bitcast(FP8X4),
+                    lhsT_scale=wd_s[:, 1, :].bitcast(U8)[:, ncol],
+                    rhs=h_q[:, cols].bitcast(FP8X4),
+                    rhs_scale=h_s[:, cols],
+                    start=False,
+                    stop=True,
+                )
+            nc.scalar.activation(z[nt][:, 2 * quarter * BLK : 2 * (quarter + 1) * BLK], bank[:, : 2 * BLK], COPY)
 
         def turn_back(nt, half, tag=None):
             if half == 0:
                 z[nt] = keep.tile([P, J], F32, name="z%d" % nt, tag=tag or "z%d" % nt, align_bytes=64)
-            bank = psum.tile([P, HALF], F32, name="bank")
+            bank = psum.tile([P, HALF], F32, name="bank%d" % (4 + (2 * nt + half) % 4))
             for i in range(4):
                 cols = slice(i * BLK, (i + 1) * BLK)
-                nc.tensor.transpose(bank[:, cols], y_t[nt, half][:, cols], ident[:])
+                nc.tensor.matmul(bank[:, cols], y_t[nt, half][:, cols], ident[:], start=True, stop=False, is_transpose=True)
+                nc.tensor.matmul(bank[:, cols], r_t[nt, half][:, cols], ident[:], start=False, stop=True, is_transpose=True)
             nc.scalar.activation(z[nt][:, half * HALF : (half + 1) * HALF], bank[:], COPY)
 
         def scatter(turn, nt, lo, hi):
-            nc.vector.tensor_tensor(placed[turn % 2][:].indirect(part(lo, hi)), z[nt][:, lo:hi], r_got[nt][:, lo:hi], ADD)
+            nc.vector.tensor_tensor(placed[turn % 2][:].indirect(part(lo, hi)), z[nt][:, lo:hi], gate[:, lo:hi], MULT)
             if hi == J:
                 nc.sync.dma_start(out[nt * P : (nt + 1) * P, :], placed[turn % 2][:])
 
@@ -211,20 +244,21 @@ def tile_list_modp_relu_res_res_kernel(
         h_q = keep.tile([P, J], U32, name="h_q", tag="r_all1", align_bytes=64)
         quant_h(0)
         quant_h(1)
-        product(3, 0)
-        product(3, 1)
-        turn_back(3, 0)
-        product(0, 0)
-        turn_back(3, 1)
-        product(0, 1)
+        for quarter in range(4):
+            product_plain(3, quarter)
+        for half in range(2):
+            product(0, half)
+            turn_r(0, half)
         gather_r(2)
-        gather_r(3)
+        for lo in (0, HALF):
+            nc.vector.tensor_tensor(r_got[3][:, lo : lo + HALF], r_all[3][:].indirect(part(lo, lo + HALF)), z[3][:, lo : lo + HALF], ADD)
         for nt in range(3):
             for half in range(2):
                 if nt < 2:
                     product(nt + 1, half)
+                    turn_r(nt + 1, half)
                 turn_back(nt, half, "r_all3" if nt == 0 else None)
-        scatter(0, 3, 0, HALF)
-        scatter(0, 3, HALF, J)
+        nc.vector.tensor_tensor(placed[0][:].indirect(offsets[:]), r_got[3][:], gate[:], MULT)
+        nc.sync.dma_start(out[3 * P :, :], placed[0][:])
         for nt in range(3):
             scatter(nt + 1, nt, 0, J)

@@ -37,8 +37,6 @@ def tile_list_modp_relu_res_res_kernel(
 
         tab_s = keep.tile([P, T // 4], I32, name="tab_s", align_bytes=64)
         wd_s = keep.tile([P, 2, N // 4], I32, name="wd_s", align_bytes=64)
-        gate_rows = keep.tile([P, P], F32, name="gate_rows")
-        nc.vector.memset(gate_rows[:].bitcast(I32), 0)
         nc.vector.memset(tab_s[:], 0)
         nc.vector.memset(wd_s[:], 0)
         placed = [keep.tile([P, T], F32, name="placed%d" % i) for i in range(2)]
@@ -69,12 +67,11 @@ def tile_list_modp_relu_res_res_kernel(
 
         load_tab(0)
         nc.sync.dma_start(offsets[:], offs)
-        nc.sync.dma_start(gate_rows[0 : J // BLK, :], wgo[0].rearrange("(b c) -> b c", c=BLK))
         for q in range(4):
             nc.sync.dma_start(tab_s[32 * q : 32 * q + 8, :], tab_scales[:, 4 * q : 4 * q + 4, :].bitcast(I32))
         load_wu(0)
-        load_tab(1)
         load_wu(1)
+        load_tab(1)
         load_r(0)
         load_wd_s(0, wd4_scales)
         load_r(1)
@@ -83,6 +80,7 @@ def tile_list_modp_relu_res_res_kernel(
         load_wd_s(1, wd8_scales)
         load_r(2)
         load_r(3)
+        nc.sync.dma_start(gate[:], wgo)
 
         def part(lo, hi):
             return offsets[:, lo // 16 : hi // 16]
@@ -97,7 +95,6 @@ def tile_list_modp_relu_res_res_kernel(
         r_got = [keep.tile([P, J], F32, name="r_got%d" % i) for i in range(4)]
         z = {}
         y_t, r_t = {}, {}
-        gate_col = keep.tile([P, J // BLK], F32, name="gate_col")
 
         def gather_words(a, tag):
             got_w[a] = keep.tile([P, J], U32, name="got_w%d" % a, tag=tag, align_bytes=64)
@@ -136,17 +133,6 @@ def tile_list_modp_relu_res_res_kernel(
         def quant_h(half):
             lo, hi = half * HALF, (half + 1) * HALF
             nc.vector.quantize_mx(out=h_q[:, lo:hi].bitcast(FP8X4), scales=h_s[:, lo:hi], in_=h_bf[:, 4 * lo : 4 * hi])
-
-        def spread_gate():
-            bank = psum.tile([P, HALF], F32, name="bank0")
-            nc.tensor.transpose(bank[:, :P], gate_rows[:], ident[:])
-            nc.scalar.activation(gate_col[:], bank[:, : J // BLK], COPY)
-            for half in range(2):
-                bank = psum.tile([P, HALF], F32, name="bank%d" % (1 + half))
-                for i in range(4):
-                    b = 4 * half + i
-                    nc.tensor.transpose(bank[:, i * BLK : (i + 1) * BLK], gate_col[:, b : b + 1].to_broadcast([P, P]), ident[:])
-                nc.scalar.activation(gate[:, half * HALF : (half + 1) * HALF], bank[:], COPY)
 
         def gather_r(nt):
             nc.vector.tensor_copy(r_got[nt][:], r_all[nt][:].indirect(offsets[:]))
@@ -228,14 +214,13 @@ def tile_list_modp_relu_res_res_kernel(
             if hi == J:
                 nc.sync.dma_start(out[nt * P : (nt + 1) * P, :], placed[turn % 2][:])
 
-        spread_gate()
         gather_words(0, "got_w0")
         nc.vector.tensor_copy(got_s[:], tab_s[:].bitcast(U8).indirect(offsets[:]))
-        cast_wu(0, 80)
+        cast_wu(0, 88)
         quant_wu(0)
-        gather_words(1, "wu_bf0")
-        cast_wu(1, 80)
+        cast_wu(1, 64)
         quant_wu(1)
+        gather_words(1, "got_w1")
         for a in range(2):
             for b in range(8):
                 up(b, a)

@@ -65,9 +65,12 @@ def tile_list_modp_relu_res_res_kernel(
             for q in range(4):
                 nc.sync.dma_start(wd_s[32 * q : 32 * q + 4, i, :], src[0, 4 * q : 4 * q + 4, :].bitcast(I32))
 
-        load_tab(0)
         nc.sync.dma_start(offsets[:], offs)
-        for q in range(4):
+        load_tab(0)
+        for q in range(2):
+            for a in range(2):
+                nc.sync.dma_start(tab_s[32 * q + 4 * a : 32 * q + 4 * a + 4, :], tab_scales[a, 4 * q : 4 * q + 4, :].bitcast(I32))
+        for q in range(2, 4):
             nc.sync.dma_start(tab_s[32 * q : 32 * q + 8, :], tab_scales[:, 4 * q : 4 * q + 4, :].bitcast(I32))
         load_wu(0)
         load_wu(1)
@@ -211,8 +214,11 @@ def tile_list_modp_relu_res_res_kernel(
 
         def scatter(turn, nt, lo, hi):
             nc.vector.tensor_tensor(placed[turn % 2][:].indirect(part(lo, hi)), z[nt][:, lo:hi], gate[:, lo:hi], MULT)
-            if hi == J:
+            if turn < 3:
                 nc.sync.dma_start(out[nt * P : (nt + 1) * P, :], placed[turn % 2][:])
+            else:
+                nc.sync.dma_start(out[nt * P : (nt + 1) * P, : T // 2], placed[turn % 2][:, : T // 2])
+                nc.scalar.dma_start(out[nt * P : (nt + 1) * P, T // 2 :], placed[turn % 2][:, T // 2 :])
 
         gather_words(0, "got_w0")
         nc.vector.tensor_copy(got_s[:], tab_s[:].bitcast(U8).indirect(offsets[:]))

@@ -37,11 +37,10 @@ def tile_list_modp_relu_res_res_kernel(
 
         tab_s = keep.tile([P, T // 4], I32, name="tab_s", align_bytes=64)
         wd_s = keep.tile([P, 2, N // 4], I32, name="wd_s", align_bytes=64)
-        nc.vector.memset(tab_s[:], 0)
+        nc.gpsimd.memset(tab_s[:], 0)
         nc.vector.memset(wd_s[:], 0)
-        placed = [keep.tile([P, T], F32, name="placed%d" % i) for i in range(2)]
-        for tile in placed:
-            nc.vector.memset(tile[:].bitcast(I32), 0)
+        placed = [keep.tile([P, T], F32, name="placed0")]
+        nc.vector.memset(placed[0][:].bitcast(I32), 0)
 
         tab_w = [keep.tile([P, T], I32, name="tab_w%d" % a, align_bytes=64) for a in range(2)]
         wu_raw = [keep.tile([P, 4, R], F32, name="wu_raw%d" % a) for a in range(2)]
@@ -68,10 +67,10 @@ def tile_list_modp_relu_res_res_kernel(
         nc.sync.dma_start(offsets[:], offs)
         load_tab(0)
         for q in range(2):
+            nc.sync.dma_start(tab_s[32 * q : 32 * q + 8, :], tab_scales[:, 4 * q : 4 * q + 4, :].bitcast(I32))
+        for q in range(2, 4):
             for a in range(2):
                 nc.sync.dma_start(tab_s[32 * q + 4 * a : 32 * q + 4 * a + 4, :], tab_scales[a, 4 * q : 4 * q + 4, :].bitcast(I32))
-        for q in range(2, 4):
-            nc.sync.dma_start(tab_s[32 * q : 32 * q + 8, :], tab_scales[:, 4 * q : 4 * q + 4, :].bitcast(I32))
         load_wu(0)
         load_wu(1)
         load_tab(1)
@@ -99,9 +98,10 @@ def tile_list_modp_relu_res_res_kernel(
         z = {}
         y_t, r_t = {}, {}
 
-        def gather_words(a, tag):
+        def gather_words(a, tag, step):
             got_w[a] = keep.tile([P, J], U32, name="got_w%d" % a, tag=tag, align_bytes=64)
-            nc.vector.tensor_copy(got_w[a][:], tab_w[a][:].bitcast(U32).indirect(offsets[:]))
+            for lo in range(0, J, step):
+                nc.vector.tensor_copy(got_w[a][:, lo : lo + step], tab_w[a][:].bitcast(U32).indirect(part(lo, lo + step)))
 
         def cast_wu(a, split):
             dst = wu_bf[a][:].rearrange("p (t m j) -> p m j t", t=4, j=4)
@@ -118,7 +118,7 @@ def tile_list_modp_relu_res_res_kernel(
         def up(b, a):
             cols = slice(b * BLK, (b + 1) * BLK)
             if a == 0:
-                banks[b] = psum.tile([P, 4, BLK], F32, name="bank%d" % b)
+                banks[b] = psum.tile([P, 4, BLK], F32, name="bank%d" % (b % 4))
             for t in range(4):
                 nc.tensor.matmul_mx(
                     out=banks[b][:, t, :],
@@ -202,9 +202,9 @@ def tile_list_modp_relu_res_res_kernel(
                 )
             nc.scalar.activation(z[nt][:, 2 * quarter * BLK : 2 * (quarter + 1) * BLK], bank[:, : 2 * BLK], COPY)
 
-        def turn_back(nt, half, tag=None):
+        def turn_back(nt, half):
             if half == 0:
-                z[nt] = keep.tile([P, J], F32, name="z%d" % nt, tag=tag or "z%d" % nt, align_bytes=64)
+                z[nt] = keep.tile([P, J], F32, name="z%d" % nt, align_bytes=64)
             bank = psum.tile([P, HALF], F32, name="bank%d" % (4 + (2 * nt + half) % 4))
             for i in range(4):
                 cols = slice(i * BLK, (i + 1) * BLK)
@@ -220,15 +220,18 @@ def tile_list_modp_relu_res_res_kernel(
                 nc.sync.dma_start(out[nt * P : (nt + 1) * P, : T // 2], placed[turn % 2][:, : T // 2])
                 nc.scalar.dma_start(out[nt * P : (nt + 1) * P, T // 2 :], placed[turn % 2][:, T // 2 :])
 
-        gather_words(0, "got_w0")
+        gather_words(0, "got_w0", J)
         nc.vector.tensor_copy(got_s[:], tab_s[:].bitcast(U8).indirect(offsets[:]))
         cast_wu(0, 88)
         quant_wu(0)
         cast_wu(1, 64)
         quant_wu(1)
-        gather_words(1, "got_w1")
+        gather_words(1, "got_w1", HALF)
         for a in range(2):
-            for b in range(8):
+            for b in range(4):
+                up(b, a)
+        for b in range(4, 8):
+            for a in range(2):
                 up(b, a)
         gather_r(0)
         gather_r(1)
@@ -248,7 +251,9 @@ def tile_list_modp_relu_res_res_kernel(
                 if nt < 2:
                     product(nt + 1, half)
                     turn_r(nt + 1, half)
-                turn_back(nt, half, "r_all3" if nt == 0 else None)
+                turn_back(nt, half)
+        placed.append(keep.tile([P, T], F32, name="placed1", tag="r_all3", align_bytes=64))
+        nc.gpsimd.memset(placed[1][:].bitcast(I32), 0)
         nc.vector.tensor_tensor(placed[0][:].indirect(offsets[:]), r_got[3][:], gate[:], MULT)
         nc.sync.dma_start(out[3 * P :, :], placed[0][:])
         for nt in range(3):

@@ -75,12 +75,12 @@ def tile_list_modp_relu_res_res_kernel(
         load_wu(1)
         load_tab(1)
         load_r(0)
-        load_wd_s(0, wd4_scales)
         load_r(1)
+        load_wd_s(0, wd4_scales)
         nc.sync.dma_start(wd8_w[:], wd8_words[0].rearrange("p n i -> p (n i)").bitcast(I32))
         nc.sync.dma_start(wd4_w[:], wd4_words[0].bitcast(I32))
-        load_wd_s(1, wd8_scales)
         load_r(2)
+        load_wd_s(1, wd8_scales)
         load_r(3)
         nc.sync.dma_start(gate[:], wgo)
 

@@ -36,9 +36,11 @@ def tile_list_modp_relu_res_res_kernel(
         offsets = keep.tile([P, J // 16], U16, name="offsets")
 
         tab_s = keep.tile([P, T // 4], I32, name="tab_s", align_bytes=64)
-        wd_s = keep.tile([P, 2, N // 4], I32, name="wd_s", align_bytes=64)
+        wd4_s = keep.tile([P, N // 4], I32, name="wd4_s", align_bytes=64)
+        h_s = keep.tile([P, J], U8, name="h_s", align_bytes=64)
+        wd8_s = h_s[:, J // 4 : J // 4 + N]
         nc.gpsimd.memset(tab_s[:], 0)
-        nc.vector.memset(wd_s[:], 0)
+        nc.vector.memset(wd4_s[:], 0)
         placed = [keep.tile([P, T], F32, name="placed0")]
         nc.vector.memset(placed[0][:].bitcast(I32), 0)
 
@@ -57,12 +59,16 @@ def tile_list_modp_relu_res_res_kernel(
         def load_wu(a):
             nc.sync.dma_start(wu_raw[a][:], wu[512 * a : 512 * (a + 1), :].rearrange("(p j) c -> p j c", j=4))
 
-        def load_r(nt):
-            nc.sync.dma_start(r_all[nt][:], rT[nt * P : (nt + 1) * P, :])
+        def chans(nt, width=1):
+            first = (nt + 1) % 4 * P
+            return slice(width * first, width * (first + P))
 
-        def load_wd_s(i, src):
+        def load_r(nt):
+            nc.sync.dma_start(r_all[nt][:], rT[chans(nt), :])
+
+        def load_wd_s(dst, first, src):
             for q in range(4):
-                nc.sync.dma_start(wd_s[32 * q : 32 * q + 4, i, :], src[0, 4 * q : 4 * q + 4, :].bitcast(I32))
+                nc.sync.dma_start(dst[32 * q + first : 32 * q + first + 4, :], src[0, 4 * q : 4 * q + 4, :].bitcast(I32))
 
         nc.sync.dma_start(offsets[:], offs)
         load_tab(0)
@@ -76,11 +82,11 @@ def tile_list_modp_relu_res_res_kernel(
         load_tab(1)
         load_r(0)
         load_r(1)
-        load_wd_s(0, wd4_scales)
+        load_wd_s(wd8_s.bitcast(I32), 4, wd8_scales)
         nc.sync.dma_start(wd8_w[:], wd8_words[0].rearrange("p n i -> p (n i)").bitcast(I32))
         nc.sync.dma_start(wd4_w[:], wd4_words[0].bitcast(I32))
         load_r(2)
-        load_wd_s(1, wd8_scales)
+        load_wd_s(wd4_s[:], 0, wd4_scales)
         load_r(3)
         nc.sync.dma_start(gate[:], wgo)
 
@@ -93,7 +99,7 @@ def tile_list_modp_relu_res_res_kernel(
         wu_q = keep.tile([P, 2, R], U32, name="wu_q", align_bytes=64)
         wu_s = keep.tile([P, 2, R], U8, name="wu_s", align_bytes=64)
         h_bf = keep.tile([P, 4 * J], BF16, name="h_bf", align_bytes=64)
-        h_s = keep.tile([P, J], U8, name="h_s", align_bytes=64)
+        h_q = keep.tile([P, J], U32, name="h_q", align_bytes=64)
         r_got = [keep.tile([P, J], F32, name="r_got%d" % i) for i in range(4)]
         z = {}
         y_t, r_t = {}, {}
@@ -141,7 +147,7 @@ def tile_list_modp_relu_res_res_kernel(
             nc.vector.tensor_copy(r_got[nt][:], r_all[nt][:].indirect(offsets[:]))
 
         def product(nt, half):
-            ncol = slice(nt * P, (nt + 1) * P)
+            ncol = chans(nt)
             bank = psum.tile([P, HALF], F32, name="bank%d" % half)
             y_t[nt, half] = ring.tile([P, HALF], F32, name="y_t")
             for i in range(4):
@@ -151,8 +157,8 @@ def tile_list_modp_relu_res_res_kernel(
                     out=bank[:, i * BLK : (i + 1) * BLK],
                     lhsT=codes,
                     lhsT_scale=h_s[:, at : at + BLK],
-                    rhs=wd4_w[:].bitcast(U8)[:, 2 * nt * P : 2 * (nt + 1) * P].bitcast(FP4X4),
-                    rhs_scale=wd_s[:, 0, :].bitcast(U8)[:, ncol],
+                    rhs=wd4_w[:].bitcast(U8)[:, chans(nt, 2)].bitcast(FP4X4),
+                    rhs_scale=wd4_s[:].bitcast(U8)[:, ncol],
                     start=True,
                     stop=False,
                 )
@@ -161,7 +167,7 @@ def tile_list_modp_relu_res_res_kernel(
                     lhsT=codes,
                     lhsT_scale=h_s[:, at : at + BLK],
                     rhs=wd8_w[:, ncol].bitcast(FP8X4),
-                    rhs_scale=wd_s[:, 1, :].bitcast(U8)[:, ncol],
+                    rhs_scale=wd8_s[4:, ncol],
                     start=False,
                     stop=True,
                 )
@@ -176,7 +182,7 @@ def tile_list_modp_relu_res_res_kernel(
             nc.scalar.activation(r_t[nt, half][:], bank[:], COPY)
 
         def product_plain(nt, quarter):
-            ncol = slice(nt * P, (nt + 1) * P)
+            ncol = chans(nt)
             if quarter == 0:
                 z[nt] = keep.tile([P, J], F32, name="z%d" % nt, align_bytes=64)
             bank = psum.tile([P, HALF], F32, name="bank%d" % quarter)
@@ -184,8 +190,8 @@ def tile_list_modp_relu_res_res_kernel(
                 cols = slice((2 * quarter + i) * BLK, (2 * quarter + i + 1) * BLK)
                 nc.tensor.matmul_mx(
                     out=bank[:, i * BLK : (i + 1) * BLK],
-                    lhsT=wd4_w[:].bitcast(U8)[:, 2 * nt * P : 2 * (nt + 1) * P].bitcast(FP4X4),
-                    lhsT_scale=wd_s[:, 0, :].bitcast(U8)[:, ncol],
+                    lhsT=wd4_w[:].bitcast(U8)[:, chans(nt, 2)].bitcast(FP4X4),
+                    lhsT_scale=wd4_s[:].bitcast(U8)[:, ncol],
                     rhs=h_q[:, cols].bitcast(FP8X4),
                     rhs_scale=h_s[:, cols],
                     start=True,
@@ -194,7 +200,7 @@ def tile_list_modp_relu_res_res_kernel(
                 nc.tensor.matmul_mx(
                     out=bank[:, i * BLK : (i + 1) * BLK],
                     lhsT=wd8_w[:, ncol].bitcast(FP8X4),
-                    lhsT_scale=wd_s[:, 1, :].bitcast(U8)[:, ncol],
+                    lhsT_scale=wd8_s[4:, ncol],
                     rhs=h_q[:, cols].bitcast(FP8X4),
                     rhs_scale=h_s[:, cols],
                     start=False,
@@ -215,10 +221,10 @@ def tile_list_modp_relu_res_res_kernel(
         def scatter(turn, nt, lo, hi):
             nc.vector.tensor_tensor(placed[turn % 2][:].indirect(part(lo, hi)), z[nt][:, lo:hi], gate[:, lo:hi], MULT)
             if turn < 3:
-                nc.sync.dma_start(out[nt * P : (nt + 1) * P, :], placed[turn % 2][:])
+                nc.sync.dma_start(out[chans(nt), :], placed[turn % 2][:])
             else:
-                nc.sync.dma_start(out[nt * P : (nt + 1) * P, : T // 2], placed[turn % 2][:, : T // 2])
-                nc.scalar.dma_start(out[nt * P : (nt + 1) * P, T // 2 :], placed[turn % 2][:, T // 2 :])
+                nc.sync.dma_start(out[chans(nt), : T // 2], placed[turn % 2][:, : T // 2])
+                nc.scalar.dma_start(out[chans(nt), T // 2 :], placed[turn % 2][:, T // 2 :])
 
         gather_words(0, "got_w0", J)
         nc.vector.tensor_copy(got_s[:], tab_s[:].bitcast(U8).indirect(offsets[:]))
@@ -235,7 +241,6 @@ def tile_list_modp_relu_res_res_kernel(
                 up(b, a)
         gather_r(0)
         gather_r(1)
-        h_q = keep.tile([P, J], U32, name="h_q", tag="r_all1", align_bytes=64)
         quant_h(0)
         quant_h(1)
         for quarter in range(4):
@@ -255,6 +260,6 @@ def tile_list_modp_relu_res_res_kernel(
         placed.append(keep.tile([P, T], F32, name="placed1", tag="r_all3", align_bytes=64))
         nc.gpsimd.memset(placed[1][:].bitcast(I32), 0)
         nc.vector.tensor_tensor(placed[0][:].indirect(offsets[:]), r_got[3][:], gate[:], MULT)
-        nc.sync.dma_start(out[3 * P :, :], placed[0][:])
+        nc.sync.dma_start(out[chans(3), :], placed[0][:])
         for nt in range(3):
             scatter(nt + 1, nt, 0, J)

@@ -50,6 +50,7 @@ def tile_list_modp_relu_res_res_kernel(
         wd8_w = keep.tile([P, N], I32, name="wd8_w", align_bytes=64)
         r_all = [keep.tile([P, T], F32, name="r_all%d" % nt, align_bytes=64) for nt in range(4)]
         gate = keep.tile([P, J], F32, name="gate")
+        gate_col = keep.tile([P, J // P], F32, name="gate_col")
         ident = keep.tile([P, P], F32, name="ident")
         make_identity(nc, ident[:])
 
@@ -79,6 +80,7 @@ def tile_list_modp_relu_res_res_kernel(
                 nc.sync.dma_start(tab_s[32 * q + 4 * a : 32 * q + 4 * a + 4, :], tab_scales[a, 4 * q : 4 * q + 4, :].bitcast(I32))
         load_wu(0)
         load_wu(1)
+        nc.sync.dma_start(gate_col[:], wgo[0, :].rearrange("(p i) -> p i", p=P))
         load_tab(1)
         load_r(0)
         load_r(1)
@@ -88,7 +90,6 @@ def tile_list_modp_relu_res_res_kernel(
         load_r(2)
         load_wd_s(wd4_s[:], 0, wd4_scales)
         load_r(3)
-        nc.sync.dma_start(gate[:], wgo)
 
         def part(lo, hi):
             return offsets[:, lo // 16 : hi // 16]
@@ -232,6 +233,13 @@ def tile_list_modp_relu_res_res_kernel(
         quant_wu(0)
         cast_wu(1, 64)
         quant_wu(1)
+        for half in range(2):
+            bank = psum.tile([P, 4, P], F32, name="bank%d" % (4 + half))
+            for i in range(4):
+                at = 4 * half + i
+                nc.tensor.transpose(bank[:, i, :], gate_col[:, at : at + 1].to_broadcast([P, P]), ident[:])
+            dst = gate[:].rearrange("m (q i) -> m q i", i=J // P)[:, :, 4 * half : 4 * half + 4]
+            nc.scalar.activation(dst, bank[:].rearrange("m i q -> m q i"), COPY)
         gather_words(1, "got_w1", HALF)
         for a in range(2):
             for b in range(4):

@@ -221,11 +221,7 @@ def tile_list_modp_relu_res_res_kernel(
 
         def scatter(turn, nt, lo, hi):
             nc.vector.tensor_tensor(placed[turn % 2][:].indirect(part(lo, hi)), z[nt][:, lo:hi], gate[:, lo:hi], MULT)
-            if turn < 3:
-                nc.sync.dma_start(out[chans(nt), :], placed[turn % 2][:])
-            else:
-                nc.sync.dma_start(out[chans(nt), : T // 2], placed[turn % 2][:, : T // 2])
-                nc.scalar.dma_start(out[chans(nt), T // 2 :], placed[turn % 2][:, T // 2 :])
+            nc.sync.dma_start(out[chans(nt), :], placed[turn % 2][:])
 
         gather_words(0, "got_w0", J)
         nc.vector.tensor_copy(got_s[:], tab_s[:].bitcast(U8).indirect(offsets[:]))

@@ -37,10 +37,12 @@ def tile_list_modp_relu_res_res_kernel(
 
         tab_s = keep.tile([P, T // 4], I32, name="tab_s", align_bytes=64)
         wd4_s = keep.tile([P, N // 4], I32, name="wd4_s", align_bytes=64)
-        h_s = keep.tile([P, J], U8, name="h_s", align_bytes=64)
-        wd8_s = h_s[:, J // 4 : J // 4 + N]
+        planes = keep.tile([P, J + P], U8, name="planes", align_bytes=64)
+        h_s = [planes[:, :HALF], planes[:, HALF + P :]]
+        wd8_s = planes[:, HALF : HALF + N]
         nc.gpsimd.memset(tab_s[:], 0)
         nc.vector.memset(wd4_s[:], 0)
+        nc.vector.memset(wd8_s[:, :P].bitcast(I32), 0)
         placed = [keep.tile([P, T], F32, name="placed0")]
         nc.vector.memset(placed[0][:].bitcast(I32), 0)
 
@@ -50,7 +52,6 @@ def tile_list_modp_relu_res_res_kernel(
         wd8_w = keep.tile([P, N], I32, name="wd8_w", align_bytes=64)
         r_all = [keep.tile([P, T], F32, name="r_all%d" % nt, align_bytes=64) for nt in range(4)]
         gate = keep.tile([P, J], F32, name="gate")
-        gate_col = keep.tile([P, J // P], F32, name="gate_col")
         ident = keep.tile([P, P], F32, name="ident")
         make_identity(nc, ident[:])
 
@@ -61,7 +62,7 @@ def tile_list_modp_relu_res_res_kernel(
             nc.sync.dma_start(wu_raw[a][:], wu[512 * a : 512 * (a + 1), :].rearrange("(p j) c -> p j c", j=4))
 
         def chans(nt, width=1):
-            first = (nt + 1) % 4 * P
+            first = nt * P
             return slice(width * first, width * (first + P))
 
         def load_r(nt):
@@ -80,16 +81,16 @@ def tile_list_modp_relu_res_res_kernel(
                 nc.sync.dma_start(tab_s[32 * q + 4 * a : 32 * q + 4 * a + 4, :], tab_scales[a, 4 * q : 4 * q + 4, :].bitcast(I32))
         load_wu(0)
         load_wu(1)
-        nc.sync.dma_start(gate_col[:], wgo[0, :].rearrange("(p i) -> p i", p=P))
         load_tab(1)
         load_r(0)
+        load_wd_s(wd4_s[:], 0, wd4_scales)
         load_r(1)
         load_wd_s(wd8_s.bitcast(I32), 4, wd8_scales)
         nc.sync.dma_start(wd8_w[:], wd8_words[0].rearrange("p n i -> p (n i)").bitcast(I32))
         nc.sync.dma_start(wd4_w[:], wd4_words[0].bitcast(I32))
         load_r(2)
-        load_wd_s(wd4_s[:], 0, wd4_scales)
         load_r(3)
+        nc.sync.dma_start(gate[:], wgo)
 
         def part(lo, hi):
             return offsets[:, lo // 16 : hi // 16]
@@ -142,14 +143,14 @@ def tile_list_modp_relu_res_res_kernel(
 
         def quant_h(half):
             lo, hi = half * HALF, (half + 1) * HALF
-            nc.vector.quantize_mx(out=h_q[:, lo:hi].bitcast(FP8X4), scales=h_s[:, lo:hi], in_=h_bf[:, 4 * lo : 4 * hi])
+            nc.vector.quantize_mx(out=h_q[:, lo:hi].bitcast(FP8X4), scales=h_s[half], in_=h_bf[:, 4 * lo : 4 * hi])
 
         def gather_r(nt):
             nc.vector.tensor_copy(r_got[nt][:], r_all[nt][:].indirect(offsets[:]))
 
         def product(nt, half):
             ncol = chans(nt)
-            bank = psum.tile([P, HALF], F32, name="bank%d" % half)
+            bank = psum.tile([P, HALF], F32, name="bank%d" % ((0 if nt == 0 else 4) + half))
             y_t[nt, half] = ring.tile([P, HALF], F32, name="y_t")
             for i in range(4):
                 at = half * HALF + i * BLK
@@ -157,7 +158,7 @@ def tile_list_modp_relu_res_res_kernel(
                 nc.tensor.matmul_mx(
                     out=bank[:, i * BLK : (i + 1) * BLK],
                     lhsT=codes,
-                    lhsT_scale=h_s[:, at : at + BLK],
+                    lhsT_scale=h_s[half][:, i * BLK : (i + 1) * BLK],
                     rhs=wd4_w[:].bitcast(U8)[:, chans(nt, 2)].bitcast(FP4X4),
                     rhs_scale=wd4_s[:].bitcast(U8)[:, ncol],
                     start=True,
@@ -166,7 +167,7 @@ def tile_list_modp_relu_res_res_kernel(
                 nc.tensor.matmul_mx(
                     out=bank[:, i * BLK : (i + 1) * BLK],
                     lhsT=codes,
-                    lhsT_scale=h_s[:, at : at + BLK],
+                    lhsT_scale=h_s[half][:, i * BLK : (i + 1) * BLK],
                     rhs=wd8_w[:, ncol].bitcast(FP8X4),
                     rhs_scale=wd8_s[4:, ncol],
                     start=False,
@@ -175,44 +176,17 @@ def tile_list_modp_relu_res_res_kernel(
             nc.scalar.activation(y_t[nt, half][:], bank[:], COPY)
 
         def turn_r(nt, half):
-            bank = psum.tile([P, HALF], F32, name="bank%d" % (2 + half))
+            bank = psum.tile([P, HALF], F32, name="bank%d" % ((2 if nt == 0 else 4) + half))
             for i in range(4):
                 at = half * HALF + i * BLK
                 nc.tensor.transpose(bank[:, i * BLK : (i + 1) * BLK], r_got[nt][:, at : at + BLK], ident[:])
             r_t[nt, half] = ring.tile([P, HALF], F32, name="r_t")
             nc.scalar.activation(r_t[nt, half][:], bank[:], COPY)
 
-        def product_plain(nt, quarter):
-            ncol = chans(nt)
-            if quarter == 0:
-                z[nt] = keep.tile([P, J], F32, name="z%d" % nt, align_bytes=64)
-            bank = psum.tile([P, HALF], F32, name="bank%d" % quarter)
-            for i in range(2):
-                cols = slice((2 * quarter + i) * BLK, (2 * quarter + i + 1) * BLK)
-                nc.tensor.matmul_mx(
-                    out=bank[:, i * BLK : (i + 1) * BLK],
-                    lhsT=wd4_w[:].bitcast(U8)[:, chans(nt, 2)].bitcast(FP4X4),
-                    lhsT_scale=wd4_s[:].bitcast(U8)[:, ncol],
-                    rhs=h_q[:, cols].bitcast(FP8X4),
-                    rhs_scale=h_s[:, cols],
-                    start=True,
-                    stop=False,
-                )
-                nc.tensor.matmul_mx(
-                    out=bank[:, i * BLK : (i + 1) * BLK],
-                    lhsT=wd8_w[:, ncol].bitcast(FP8X4),
-                    lhsT_scale=wd8_s[4:, ncol],
-                    rhs=h_q[:, cols].bitcast(FP8X4),
-                    rhs_scale=h_s[:, cols],
-                    start=False,
-                    stop=True,
-                )
-            nc.scalar.activation(z[nt][:, 2 * quarter * BLK : 2 * (quarter + 1) * BLK], bank[:, : 2 * BLK], COPY)
-
         def turn_back(nt, half):
             if half == 0:
                 z[nt] = keep.tile([P, J], F32, name="z%d" % nt, align_bytes=64)
-            bank = psum.tile([P, HALF], F32, name="bank%d" % (4 + (2 * nt + half) % 4))
+            bank = psum.tile([P, HALF], F32, name="bank%d" % ((4 if nt == 0 else 6) + half))
             for i in range(4):
                 cols = slice(i * BLK, (i + 1) * BLK)
                 nc.tensor.matmul(bank[:, cols], y_t[nt, half][:, cols], ident[:], start=True, stop=False, is_transpose=True)
@@ -229,13 +203,6 @@ def tile_list_modp_relu_res_res_kernel(
         quant_wu(0)
         cast_wu(1, 64)
         quant_wu(1)
-        for half in range(2):
-            bank = psum.tile([P, 4, P], F32, name="bank%d" % (4 + half))
-            for i in range(4):
-                at = 4 * half + i
-                nc.tensor.transpose(bank[:, i, :], gate_col[:, at : at + 1].to_broadcast([P, P]), ident[:])
-            dst = gate[:].rearrange("m (q i) -> m q i", i=J // P)[:, :, 4 * half : 4 * half + 4]
-            nc.scalar.activation(dst, bank[:].rearrange("m i q -> m q i"), COPY)
         gather_words(1, "got_w1", HALF)
         for a in range(2):
             for b in range(4):
@@ -244,26 +211,16 @@ def tile_list_modp_relu_res_res_kernel(
             for a in range(2):
                 up(b, a)
         gather_r(0)
-        gather_r(1)
         quant_h(0)
+        gather_r(1)
         quant_h(1)
-        for quarter in range(4):
-            product_plain(3, quarter)
-        for half in range(2):
-            product(0, half)
-            turn_r(0, half)
         gather_r(2)
-        for lo in (0, HALF):
-            nc.vector.tensor_tensor(r_got[3][:, lo : lo + HALF], r_all[3][:].indirect(part(lo, lo + HALF)), z[3][:, lo : lo + HALF], ADD)
-        for nt in range(3):
-            for half in range(2):
-                if nt < 2:
-                    product(nt + 1, half)
-                    turn_r(nt + 1, half)
-                turn_back(nt, half)
+        gather_r(3)
+        for nt in range(4):
+            for step in (turn_r, product, turn_back):
+                for half in range(2):
+                    step(nt, half)
         placed.append(keep.tile([P, T], F32, name="placed1", tag="r_all3", align_bytes=64))
         nc.gpsimd.memset(placed[1][:].bitcast(I32), 0)
-        nc.vector.tensor_tensor(placed[0][:].indirect(offsets[:]), r_got[3][:], gate[:], MULT)
-        nc.sync.dma_start(out[chans(3), :], placed[0][:])
-        for nt in range(3):
-            scatter(nt + 1, nt, 0, J)
+        for nt in range(4):
+            scatter(nt, nt, 0, J)

@@ -100,7 +100,7 @@ def tile_list_modp_relu_res_res_kernel(
         wu_bf = [keep.tile([P, 4 * R], BF16, name="wu_bf%d" % a, align_bytes=64) for a in range(2)]
         wu_q = keep.tile([P, 2, R], U32, name="wu_q", align_bytes=64)
         wu_s = keep.tile([P, 2, R], U8, name="wu_s", align_bytes=64)
-        h_bf = keep.tile([P, 4 * J], BF16, name="h_bf", align_bytes=64)
+        h_bf = [keep.tile([P, 4 * HALF], BF16, name="h_bf%d" % half, align_bytes=64) for half in range(2)]
         h_q = keep.tile([P, J], U32, name="h_q", align_bytes=64)
         r_got = [keep.tile([P, J], F32, name="r_got%d" % i) for i in range(4)]
         z = {}
@@ -138,19 +138,19 @@ def tile_list_modp_relu_res_res_kernel(
                     stop=(a == 1 and t == 3),
                 )
             if a == 1:
-                dst = h_bf[:, 4 * b * BLK : 4 * (b + 1) * BLK].rearrange("p (n t) -> p n t", t=4)
+                dst = h_bf[b // 4][:, 4 * (b % 4) * BLK : 4 * (b % 4 + 1) * BLK].rearrange("p (n t) -> p n t", t=4)
                 nc.scalar.activation(dst, banks[b][:].rearrange("p t n -> p n t"), RELU)
 
         def quant_h(half):
             lo, hi = half * HALF, (half + 1) * HALF
-            nc.vector.quantize_mx(out=h_q[:, lo:hi].bitcast(FP8X4), scales=h_s[half], in_=h_bf[:, 4 * lo : 4 * hi])
+            nc.vector.quantize_mx(out=h_q[:, lo:hi].bitcast(FP8X4), scales=h_s[half], in_=h_bf[half][:])
 
         def gather_r(nt):
             nc.vector.tensor_copy(r_got[nt][:], r_all[nt][:].indirect(offsets[:]))
 
         def product(nt, half):
             ncol = chans(nt)
-            bank = psum.tile([P, HALF], F32, name="bank%d" % ((0 if nt == 0 else 4) + half))
+            bank = psum.tile([P, HALF], F32, name="bank3")
             y_t[nt, half] = ring.tile([P, HALF], F32, name="y_t")
             for i in range(4):
                 at = half * HALF + i * BLK
@@ -176,17 +176,44 @@ def tile_list_modp_relu_res_res_kernel(
             nc.scalar.activation(y_t[nt, half][:], bank[:], COPY)
 
         def turn_r(nt, half):
-            bank = psum.tile([P, HALF], F32, name="bank%d" % ((2 if nt == 0 else 4) + half))
+            bank = psum.tile([P, HALF], F32, name="bank2")
             for i in range(4):
                 at = half * HALF + i * BLK
                 nc.tensor.transpose(bank[:, i * BLK : (i + 1) * BLK], r_got[nt][:, at : at + BLK], ident[:])
             r_t[nt, half] = ring.tile([P, HALF], F32, name="r_t")
             nc.scalar.activation(r_t[nt, half][:], bank[:], COPY)
 
+        def first_sum(half):
+            cols = slice(half * HALF, (half + 1) * HALF)
+            if half == 0:
+                z[0] = keep.tile([P, J], F32, name="z0", tag="h_bf1", align_bytes=64)
+            bank = psum.tile([P, HALF], F32, name="bank%d" % (2 + half))
+            nc.tensor.matmul_mx(
+                out=bank[:],
+                lhsT=wd4_w[:].bitcast(U8)[:, chans(0, 2)].bitcast(FP4X4),
+                lhsT_scale=wd4_s[:].bitcast(U8)[:, chans(0)],
+                rhs=h_q[:, cols].bitcast(FP8X4),
+                rhs_scale=h_s[half],
+                start=True,
+                stop=False,
+            )
+            nc.tensor.matmul_mx(
+                out=bank[:],
+                lhsT=wd8_w[:, chans(0)].bitcast(FP8X4),
+                lhsT_scale=wd8_s[4:, chans(0)],
+                rhs=h_q[:, cols].bitcast(FP8X4),
+                rhs_scale=h_s[half],
+                start=False,
+                stop=True,
+            )
+            y_first = ring.tile([P, HALF], F32, name="y_first")
+            nc.scalar.activation(y_first[:], bank[:], COPY)
+            nc.gpsimd.tensor_tensor(z[0][:, cols], y_first[:], r_got[0][:, cols], ADD)
+
         def turn_back(nt, half):
             if half == 0:
                 z[nt] = keep.tile([P, J], F32, name="z%d" % nt, align_bytes=64)
-            bank = psum.tile([P, HALF], F32, name="bank%d" % ((4 if nt == 0 else 6) + half))
+            bank = psum.tile([P, HALF], F32, name="bank%d" % (4 + half))
             for i in range(4):
                 cols = slice(i * BLK, (i + 1) * BLK)
                 nc.tensor.matmul(bank[:, cols], y_t[nt, half][:, cols], ident[:], start=True, stop=False, is_transpose=True)
@@ -216,7 +243,9 @@ def tile_list_modp_relu_res_res_kernel(
         quant_h(1)
         gather_r(2)
         gather_r(3)
-        for nt in range(4):
+        for half in range(2):
+            first_sum(half)
+        for nt in range(1, 4):
             for step in (turn_r, product, turn_back):
                 for half in range(2):
                     step(nt, half)

@@ -37,12 +37,11 @@ def tile_list_modp_relu_res_res_kernel(
 
         tab_s = keep.tile([P, T // 4], I32, name="tab_s", align_bytes=64)
         wd4_s = keep.tile([P, N // 4], I32, name="wd4_s", align_bytes=64)
-        planes = keep.tile([P, J + P], U8, name="planes", align_bytes=64)
-        h_s = [planes[:, :HALF], planes[:, HALF + P :]]
-        wd8_s = planes[:, HALF : HALF + N]
+        planes = keep.tile([P, J], U8, name="planes", align_bytes=64)
+        h_s = [planes[:, :HALF], planes[:, HALF:]]
+        wd8_s = planes[:, J // 4 : J // 4 + N]
         nc.gpsimd.memset(tab_s[:], 0)
         nc.vector.memset(wd4_s[:], 0)
-        nc.vector.memset(wd8_s[:, :P].bitcast(I32), 0)
         placed = [keep.tile([P, T], F32, name="placed0")]
         nc.vector.memset(placed[0][:].bitcast(I32), 0)
 
@@ -72,6 +71,10 @@ def tile_list_modp_relu_res_res_kernel(
             for q in range(4):
                 nc.sync.dma_start(dst[32 * q + first : 32 * q + first + 4, :], src[0, 4 * q : 4 * q + 4, :].bitcast(I32))
 
+        def load_wd_w(lo, hi):
+            nc.sync.dma_start(wd8_w[:, lo:hi], wd8_words[0].rearrange("p n i -> p (n i)").bitcast(I32)[:, lo:hi])
+            nc.sync.dma_start(wd4_w[:, lo // 2 : hi // 2], wd4_words[0].bitcast(I32)[:, lo // 2 : hi // 2])
+
         nc.sync.dma_start(offsets[:], offs)
         load_tab(0)
         for q in range(2):
@@ -83,14 +86,14 @@ def tile_list_modp_relu_res_res_kernel(
         load_wu(1)
         load_tab(1)
         load_r(0)
-        load_wd_s(wd4_s[:], 0, wd4_scales)
         load_r(1)
         load_wd_s(wd8_s.bitcast(I32), 4, wd8_scales)
-        nc.sync.dma_start(wd8_w[:], wd8_words[0].rearrange("p n i -> p (n i)").bitcast(I32))
-        nc.sync.dma_start(wd4_w[:], wd4_words[0].bitcast(I32))
+        load_wd_w(0, N // 2)
         load_r(2)
+        load_wd_s(wd4_s[:], 0, wd4_scales)
         load_r(3)
         nc.sync.dma_start(gate[:], wgo)
+        load_wd_w(N // 2, N)
 
         def part(lo, hi):
             return offsets[:, lo // 16 : hi // 16]
@@ -100,9 +103,10 @@ def tile_list_modp_relu_res_res_kernel(
         wu_bf = [keep.tile([P, 4 * R], BF16, name="wu_bf%d" % a, align_bytes=64) for a in range(2)]
         wu_q = keep.tile([P, 2, R], U32, name="wu_q", align_bytes=64)
         wu_s = keep.tile([P, 2, R], U8, name="wu_s", align_bytes=64)
-        h_bf = [keep.tile([P, 4 * HALF], BF16, name="h_bf%d" % half, align_bytes=64) for half in range(2)]
+        h_bf = keep.tile([P, 4 * J], BF16, name="h_bf", align_bytes=64)
         h_q = keep.tile([P, J], U32, name="h_q", align_bytes=64)
         r_got = [keep.tile([P, J], F32, name="r_got%d" % i) for i in range(4)]
+        y_first = keep.tile([P, J], F32, name="y_first")
         z = {}
         y_t, r_t = {}, {}
 
@@ -138,12 +142,8 @@ def tile_list_modp_relu_res_res_kernel(
                     stop=(a == 1 and t == 3),
                 )
             if a == 1:
-                dst = h_bf[b // 4][:, 4 * (b % 4) * BLK : 4 * (b % 4 + 1) * BLK].rearrange("p (n t) -> p n t", t=4)
+                dst = h_bf[:, 4 * b * BLK : 4 * (b + 1) * BLK].rearrange("p (n t) -> p n t", t=4)
                 nc.scalar.activation(dst, banks[b][:].rearrange("p t n -> p n t"), RELU)
-
-        def quant_h(half):
-            lo, hi = half * HALF, (half + 1) * HALF
-            nc.vector.quantize_mx(out=h_q[:, lo:hi].bitcast(FP8X4), scales=h_s[half], in_=h_bf[half][:])
 
         def gather_r(nt):
             nc.vector.tensor_copy(r_got[nt][:], r_all[nt][:].indirect(offsets[:]))
@@ -183,32 +183,35 @@ def tile_list_modp_relu_res_res_kernel(
             r_t[nt, half] = ring.tile([P, HALF], F32, name="r_t")
             nc.scalar.activation(r_t[nt, half][:], bank[:], COPY)
 
-        def first_sum(half):
-            cols = slice(half * HALF, (half + 1) * HALF)
-            if half == 0:
-                z[0] = keep.tile([P, J], F32, name="z0", tag="h_bf1", align_bytes=64)
-            bank = psum.tile([P, HALF], F32, name="bank%d" % (2 + half))
-            nc.tensor.matmul_mx(
-                out=bank[:],
-                lhsT=wd4_w[:].bitcast(U8)[:, chans(0, 2)].bitcast(FP4X4),
-                lhsT_scale=wd4_s[:].bitcast(U8)[:, chans(0)],
-                rhs=h_q[:, cols].bitcast(FP8X4),
-                rhs_scale=h_s[half],
-                start=True,
-                stop=False,
-            )
-            nc.tensor.matmul_mx(
-                out=bank[:],
-                lhsT=wd8_w[:, chans(0)].bitcast(FP8X4),
-                lhsT_scale=wd8_s[4:, chans(0)],
-                rhs=h_q[:, cols].bitcast(FP8X4),
-                rhs_scale=h_s[half],
-                start=False,
-                stop=True,
-            )
-            y_first = ring.tile([P, HALF], F32, name="y_first")
-            nc.scalar.activation(y_first[:], bank[:], COPY)
-            nc.gpsimd.tensor_tensor(z[0][:, cols], y_first[:], r_got[0][:, cols], ADD)
+        def first_sum(quarter):
+            lo = 2 * quarter * BLK
+            if quarter == 0:
+                z[0] = keep.tile([P, J], F32, name="z0", align_bytes=64)
+            bank = psum.tile([P, 2 * BLK], F32, name="bank%d" % quarter)
+            for i in range(2):
+                cols = slice(lo + i * BLK, lo + (i + 1) * BLK)
+                nc.tensor.matmul_mx(
+                    out=bank[:, i * BLK : (i + 1) * BLK],
+                    lhsT=wd4_w[:].bitcast(U8)[:, chans(0, 2)].bitcast(FP4X4),
+                    lhsT_scale=wd4_s[:].bitcast(U8)[:, chans(0)],
+                    rhs=h_q[:, cols].bitcast(FP8X4),
+                    rhs_scale=planes[:, cols],
+                    start=True,
+                    stop=False,
+                )
+                nc.tensor.matmul_mx(
+                    out=bank[:, i * BLK : (i + 1) * BLK],
+                    lhsT=wd8_w[:, chans(0)].bitcast(FP8X4),
+                    lhsT_scale=wd8_s[4:, chans(0)],
+                    rhs=h_q[:, cols].bitcast(FP8X4),
+                    rhs_scale=planes[:, cols],
+                    start=False,
+                    stop=True,
+                )
+            nc.scalar.activation(y_first[:, lo : lo + 2 * BLK], bank[:], COPY)
+            if quarter != 2:
+                cols = slice(min(lo, HALF), lo + 2 * BLK)
+                nc.gpsimd.tensor_tensor(z[0][:, cols], y_first[:, cols], r_got[0][:, cols], ADD)
 
         def turn_back(nt, half):
             if half == 0:
@@ -238,13 +241,12 @@ def tile_list_modp_relu_res_res_kernel(
             for a in range(2):
                 up(b, a)
         gather_r(0)
-        quant_h(0)
         gather_r(1)
-        quant_h(1)
+        nc.vector.quantize_mx(out=h_q[:].bitcast(FP8X4), scales=planes[:], in_=h_bf[:])
         gather_r(2)
         gather_r(3)
-        for half in range(2):
-            first_sum(half)
+        for quarter in range(4):
+            first_sum(quarter)
         for nt in range(1, 4):
             for step in (turn_r, product, turn_back):
                 for half in range(2):

@@ -22,6 +22,7 @@ RELU = mybir.ActivationFunctionType.Relu
 P = 128
 HALF = 512
 BLK = 128
+SCALAR_GROUPS = (88, 56)
 
 
 def tile_list_modp_relu_res_res_kernel(
@@ -30,228 +31,197 @@ def tile_list_modp_relu_res_res_kernel(
     nc = tc.nc
     with ExitStack() as ctx:
         keep = ctx.enter_context(tc.tile_pool(name="keep", bufs=1))
-        ring = ctx.enter_context(tc.tile_pool(name="ring", bufs=8))
+        ring = ctx.enter_context(tc.tile_pool(name="ring", bufs=6))
         psum = ctx.enter_context(tc.psum_pool(name="psum", bufs=1))
 
         offsets = keep.tile([P, J // 16], U16, name="offsets")
-
         tab_s = keep.tile([P, T // 4], I32, name="tab_s", align_bytes=64)
         wd4_s = keep.tile([P, N // 4], I32, name="wd4_s", align_bytes=64)
         planes = keep.tile([P, J], U8, name="planes", align_bytes=64)
-        h_s = [planes[:, :HALF], planes[:, HALF:]]
         wd8_s = planes[:, J // 4 : J // 4 + N]
-        nc.gpsimd.memset(tab_s[:], 0)
-        nc.vector.memset(wd4_s[:], 0)
-        placed = [keep.tile([P, T], F32, name="placed0")]
-        nc.vector.memset(placed[0][:].bitcast(I32), 0)
-
+        pages = [keep.tile([P, T], F32, name="page0")]
         tab_w = [keep.tile([P, T], I32, name="tab_w%d" % a, align_bytes=64) for a in range(2)]
         wu_raw = [keep.tile([P, 4, R], F32, name="wu_raw%d" % a) for a in range(2)]
         wd4_w = keep.tile([P, N // 2], I32, name="wd4_w", align_bytes=64)
         wd8_w = keep.tile([P, N], I32, name="wd8_w", align_bytes=64)
-        r_all = [keep.tile([P, T], F32, name="r_all%d" % nt, align_bytes=64) for nt in range(4)]
+        r_all = [keep.tile([P, T], F32, name="r_all%d" % c, align_bytes=64) for c in range(4)]
         gate = keep.tile([P, J], F32, name="gate")
         ident = keep.tile([P, P], F32, name="ident")
+        got_w, r_got = {}, {}
+        got_s = keep.tile([P, J], U8, name="got_s", align_bytes=64)
+        wu_bf = [keep.tile([P, 4 * R], BF16, name="wu_bf%d" % a, align_bytes=64) for a in range(2)]
+        wu_q = [keep.tile([P, R], U32, name="wu_q%d" % a, align_bytes=64) for a in range(2)]
+        wu_s = [keep.tile([P, R], U8, name="wu_s%d" % a, align_bytes=64) for a in range(2)]
+        h_bf = keep.tile([P, 4 * J], BF16, name="h_bf", align_bytes=64)
+        h_q = keep.tile([P, J], U32, name="h_q", align_bytes=64)
+        y_first = keep.tile([P, J], F32, name="y_first")
+        z = [keep.tile([P, J], F32, name="z%d" % c) for c in range(4)]
+
+        nc.gpsimd.memset(tab_s[:], 0)
+        nc.vector.memset(wd4_s[:], 0)
+        nc.vector.memset(pages[0][:].bitcast(I32), 0)
         make_identity(nc, ident[:])
+
+        def chans(c, width=1):
+            return slice(width * c * P, width * (c + 1) * P)
 
         def load_tab(a):
             nc.sync.dma_start(tab_w[a][:], tab_words[a].rearrange("p t i -> p (t i)").bitcast(I32))
 
+        def load_tab_scales():
+            for q in range(2):
+                nc.sync.dma_start(tab_s[32 * q : 32 * q + 8, :], tab_scales[:, 4 * q : 4 * q + 4, :].bitcast(I32))
+            for q in range(2, 4):
+                for a in range(2):
+                    first = 32 * q + 4 * a
+                    nc.sync.dma_start(tab_s[first : first + 4, :], tab_scales[a, 4 * q : 4 * q + 4, :].bitcast(I32))
+
         def load_wu(a):
             nc.sync.dma_start(wu_raw[a][:], wu[512 * a : 512 * (a + 1), :].rearrange("(p j) c -> p j c", j=4))
 
-        def chans(nt, width=1):
-            first = nt * P
-            return slice(width * first, width * (first + P))
+        def load_r(c):
+            nc.sync.dma_start(r_all[c][:], rT[chans(c), :])
 
-        def load_r(nt):
-            nc.sync.dma_start(r_all[nt][:], rT[chans(nt), :])
-
-        def load_wd_s(dst, first, src):
+        def load_wd_scales(dst, first, src):
             for q in range(4):
                 nc.sync.dma_start(dst[32 * q + first : 32 * q + first + 4, :], src[0, 4 * q : 4 * q + 4, :].bitcast(I32))
 
-        def load_wd_w(lo, hi):
+        def load_wd_words(lo, hi):
             nc.sync.dma_start(wd8_w[:, lo:hi], wd8_words[0].rearrange("p n i -> p (n i)").bitcast(I32)[:, lo:hi])
             nc.sync.dma_start(wd4_w[:, lo // 2 : hi // 2], wd4_words[0].bitcast(I32)[:, lo // 2 : hi // 2])
 
-        nc.sync.dma_start(offsets[:], offs)
-        load_tab(0)
-        for q in range(2):
-            nc.sync.dma_start(tab_s[32 * q : 32 * q + 8, :], tab_scales[:, 4 * q : 4 * q + 4, :].bitcast(I32))
-        for q in range(2, 4):
-            for a in range(2):
-                nc.sync.dma_start(tab_s[32 * q + 4 * a : 32 * q + 4 * a + 4, :], tab_scales[a, 4 * q : 4 * q + 4, :].bitcast(I32))
-        load_wu(0)
-        load_wu(1)
-        load_tab(1)
-        load_r(0)
-        load_r(1)
-        load_wd_s(wd8_s.bitcast(I32), 4, wd8_scales)
-        load_wd_w(0, N // 2)
-        load_r(2)
-        load_wd_s(wd4_s[:], 0, wd4_scales)
-        load_r(3)
-        nc.sync.dma_start(gate[:], wgo)
-        load_wd_w(N // 2, N)
-
-        def part(lo, hi):
-            return offsets[:, lo // 16 : hi // 16]
-
-        got_w = {}
-        got_s = keep.tile([P, J], U8, name="got_s", align_bytes=64)
-        wu_bf = [keep.tile([P, 4 * R], BF16, name="wu_bf%d" % a, align_bytes=64) for a in range(2)]
-        wu_q = keep.tile([P, 2, R], U32, name="wu_q", align_bytes=64)
-        wu_s = keep.tile([P, 2, R], U8, name="wu_s", align_bytes=64)
-        h_bf = keep.tile([P, 4 * J], BF16, name="h_bf", align_bytes=64)
-        h_q = keep.tile([P, J], U32, name="h_q", align_bytes=64)
-        r_got = [keep.tile([P, J], F32, name="r_got%d" % i) for i in range(4)]
-        y_first = keep.tile([P, J], F32, name="y_first")
-        z = {}
-        y_t, r_t = {}, {}
-
-        def gather_words(a, tag, step):
+        def gather_words(a, tag):
             got_w[a] = keep.tile([P, J], U32, name="got_w%d" % a, tag=tag, align_bytes=64)
-            for lo in range(0, J, step):
-                nc.vector.tensor_copy(got_w[a][:, lo : lo + step], tab_w[a][:].bitcast(U32).indirect(part(lo, lo + step)))
+            nc.vector.tensor_copy(got_w[a][:], tab_w[a][:].bitcast(U32).indirect(offsets[:]))
 
-        def cast_wu(a, split):
+        def gather_r(c, tag):
+            r_got[c] = keep.tile([P, J], F32, name="r_got%d" % c, tag=tag, align_bytes=64)
+            nc.vector.tensor_copy(r_got[c][:], r_all[c][:].indirect(offsets[:]))
+
+        def quantise_wu(a):
+            split = SCALAR_GROUPS[a]
             dst = wu_bf[a][:].rearrange("p (t m j) -> p m j t", t=4, j=4)
             src = wu_raw[a][:].rearrange("p j (m t) -> p m j t", t=4)
             nc.scalar.activation(dst[:, :split, :, :], src[:, :split, :, :], COPY)
-            if split < P:
-                nc.vector.tensor_copy(dst[:, split:, :, :], src[:, split:, :, :])
+            nc.vector.tensor_copy(dst[:, split:, :, :], src[:, split:, :, :])
+            nc.vector.quantize_mx(out=wu_q[a][:].bitcast(FP8X4), scales=wu_s[a][:], in_=wu_bf[a][:])
 
-        def quant_wu(a):
-            nc.vector.quantize_mx(out=wu_q[:, a, :].bitcast(FP8X4), scales=wu_s[:, a, :], in_=wu_bf[a][:])
-
-        banks = {}
-
-        def up(b, a):
+        def up_passes(bank, b, a):
             cols = slice(b * BLK, (b + 1) * BLK)
-            if a == 0:
-                banks[b] = psum.tile([P, 4, BLK], F32, name="bank%d" % (b % 4))
             for t in range(4):
                 nc.tensor.matmul_mx(
-                    out=banks[b][:, t, :],
-                    lhsT=wu_q[:, a, t * P : (t + 1) * P].bitcast(FP8X4),
-                    lhsT_scale=wu_s[:, a, t * P : (t + 1) * P],
+                    out=bank[:, t, :],
+                    lhsT=wu_q[a][:, chans(t)].bitcast(FP8X4),
+                    lhsT_scale=wu_s[a][:, chans(t)],
                     rhs=got_w[a][:, cols].bitcast(FP8X4),
                     rhs_scale=got_s[4 * a :, cols],
                     start=(a == 0 and t == 0),
                     stop=(a == 1 and t == 3),
                 )
-            if a == 1:
-                dst = h_bf[:, 4 * b * BLK : 4 * (b + 1) * BLK].rearrange("p (n t) -> p n t", t=4)
-                nc.scalar.activation(dst, banks[b][:].rearrange("p t n -> p n t"), RELU)
 
-        def gather_r(nt):
-            nc.vector.tensor_copy(r_got[nt][:], r_all[nt][:].indirect(offsets[:]))
+        def relu(bank, b):
+            dst = h_bf[:, 4 * b * BLK : 4 * (b + 1) * BLK].rearrange("p (n t) -> p n t", t=4)
+            nc.scalar.activation(dst, bank[:].rearrange("p t n -> p n t"), RELU)
 
-        def product(nt, half):
-            ncol = chans(nt)
-            bank = psum.tile([P, HALF], F32, name="bank3")
-            y_t[nt, half] = ring.tile([P, HALF], F32, name="y_t")
-            for i in range(4):
-                at = half * HALF + i * BLK
-                codes = h_q[:, at : at + BLK].bitcast(FP8X4)
+        def quantise_h(half):
+            cols = slice(half * HALF, (half + 1) * HALF)
+            nc.vector.quantize_mx(
+                out=h_q[:, cols].bitcast(FP8X4), scales=planes[:, cols], in_=h_bf[:, 4 * half * HALF : 4 * (half + 1) * HALF]
+            )
+
+        def wd_operands(c):
+            return (
+                (wd4_w[:].bitcast(U8)[:, chans(c, 2)].bitcast(FP4X4), wd4_s[:].bitcast(U8)[:, chans(c)]),
+                (wd8_w[:, chans(c)].bitcast(FP8X4), wd8_s[4:, chans(c)]),
+            )
+
+        def first_sum(half):
+            cols = slice(half * HALF, (half + 1) * HALF)
+            bank = psum.tile([P, HALF], F32, name="bank%d" % half)
+            for tier, (words, scales) in enumerate(wd_operands(0)):
                 nc.tensor.matmul_mx(
-                    out=bank[:, i * BLK : (i + 1) * BLK],
-                    lhsT=codes,
-                    lhsT_scale=h_s[half][:, i * BLK : (i + 1) * BLK],
-                    rhs=wd4_w[:].bitcast(U8)[:, chans(nt, 2)].bitcast(FP4X4),
-                    rhs_scale=wd4_s[:].bitcast(U8)[:, ncol],
-                    start=True,
-                    stop=False,
-                )
-                nc.tensor.matmul_mx(
-                    out=bank[:, i * BLK : (i + 1) * BLK],
-                    lhsT=codes,
-                    lhsT_scale=h_s[half][:, i * BLK : (i + 1) * BLK],
-                    rhs=wd8_w[:, ncol].bitcast(FP8X4),
-                    rhs_scale=wd8_s[4:, ncol],
-                    start=False,
-                    stop=True,
-                )
-            nc.scalar.activation(y_t[nt, half][:], bank[:], COPY)
-
-        def turn_r(nt, half):
-            bank = psum.tile([P, HALF], F32, name="bank2")
-            for i in range(4):
-                at = half * HALF + i * BLK
-                nc.tensor.transpose(bank[:, i * BLK : (i + 1) * BLK], r_got[nt][:, at : at + BLK], ident[:])
-            r_t[nt, half] = ring.tile([P, HALF], F32, name="r_t")
-            nc.scalar.activation(r_t[nt, half][:], bank[:], COPY)
-
-        def first_sum(quarter):
-            lo = 2 * quarter * BLK
-            if quarter == 0:
-                z[0] = keep.tile([P, J], F32, name="z0", align_bytes=64)
-            bank = psum.tile([P, 2 * BLK], F32, name="bank%d" % quarter)
-            for i in range(2):
-                cols = slice(lo + i * BLK, lo + (i + 1) * BLK)
-                nc.tensor.matmul_mx(
-                    out=bank[:, i * BLK : (i + 1) * BLK],
-                    lhsT=wd4_w[:].bitcast(U8)[:, chans(0, 2)].bitcast(FP4X4),
-                    lhsT_scale=wd4_s[:].bitcast(U8)[:, chans(0)],
+                    out=bank[:],
+                    lhsT=words,
+                    lhsT_scale=scales,
                     rhs=h_q[:, cols].bitcast(FP8X4),
                     rhs_scale=planes[:, cols],
-                    start=True,
-                    stop=False,
+                    start=(tier == 0),
+                    stop=(tier == 1),
                 )
-                nc.tensor.matmul_mx(
-                    out=bank[:, i * BLK : (i + 1) * BLK],
-                    lhsT=wd8_w[:, chans(0)].bitcast(FP8X4),
-                    lhsT_scale=wd8_s[4:, chans(0)],
-                    rhs=h_q[:, cols].bitcast(FP8X4),
-                    rhs_scale=planes[:, cols],
-                    start=False,
-                    stop=True,
-                )
-            nc.scalar.activation(y_first[:, lo : lo + 2 * BLK], bank[:], COPY)
-            if quarter != 2:
-                cols = slice(min(lo, HALF), lo + 2 * BLK)
-                nc.gpsimd.tensor_tensor(z[0][:, cols], y_first[:, cols], r_got[0][:, cols], ADD)
+            nc.scalar.activation(y_first[:, cols], bank[:], COPY)
+            nc.gpsimd.tensor_tensor(z[0][:, cols], y_first[:, cols], r_got[0][:, cols], ADD)
 
-        def turn_back(nt, half):
-            if half == 0:
-                z[nt] = keep.tile([P, J], F32, name="z%d" % nt, align_bytes=64)
-            bank = psum.tile([P, HALF], F32, name="bank%d" % (4 + half))
-            for i in range(4):
-                cols = slice(i * BLK, (i + 1) * BLK)
-                nc.tensor.matmul(bank[:, cols], y_t[nt, half][:, cols], ident[:], start=True, stop=False, is_transpose=True)
-                nc.tensor.matmul(bank[:, cols], r_t[nt, half][:, cols], ident[:], start=False, stop=True, is_transpose=True)
-            nc.scalar.activation(z[nt][:, half * HALF : (half + 1) * HALF], bank[:], COPY)
+        def turned_sum(c):
+            r_t, y_t = [], []
+            for half in range(2):
+                bank = psum.tile([P, HALF], F32, name="bank1")
+                for i in range(4):
+                    at = half * HALF + i * BLK
+                    nc.tensor.transpose(bank[:, chans(i)], r_got[c][:, at : at + BLK], ident[:])
+                r_t.append(ring.tile([P, HALF], F32, name="r_t"))
+                nc.scalar.activation(r_t[half][:], bank[:], COPY)
+            for half in range(2):
+                bank = psum.tile([P, HALF], F32, name="bank0")
+                for i in range(4):
+                    cols = slice(half * HALF + i * BLK, half * HALF + (i + 1) * BLK)
+                    for tier, (words, scales) in enumerate(wd_operands(c)):
+                        nc.tensor.matmul_mx(
+                            out=bank[:, chans(i)],
+                            lhsT=h_q[:, cols].bitcast(FP8X4),
+                            lhsT_scale=planes[:, cols],
+                            rhs=words,
+                            rhs_scale=scales,
+                            start=(tier == 0),
+                            stop=(tier == 1),
+                        )
+                y_t.append(ring.tile([P, HALF], F32, name="y_t"))
+                nc.scalar.activation(y_t[half][:], bank[:], COPY)
+            for half in range(2):
+                bank = psum.tile([P, HALF], F32, name="bank%d" % (4 + half))
+                for i in range(4):
+                    nc.tensor.matmul(bank[:, chans(i)], y_t[half][:, chans(i)], ident[:], start=True, stop=False, is_transpose=True)
+                    nc.tensor.matmul(bank[:, chans(i)], r_t[half][:, chans(i)], ident[:], start=False, stop=True, is_transpose=True)
+                nc.scalar.activation(z[c][:, half * HALF : (half + 1) * HALF], bank[:], COPY)
 
-        def scatter(turn, nt, lo, hi):
-            nc.vector.tensor_tensor(placed[turn % 2][:].indirect(part(lo, hi)), z[nt][:, lo:hi], gate[:, lo:hi], MULT)
-            nc.sync.dma_start(out[chans(nt), :], placed[turn % 2][:])
+        nc.sync.dma_start(offsets[:], offs)
+        load_tab(0)
+        load_tab_scales()
+        load_wu(0)
+        load_tab(1)
+        load_wu(1)
+        load_r(0)
+        load_r(1)
+        load_wd_scales(wd8_s.bitcast(I32), 4, wd8_scales)
+        load_wd_words(0, N // 2)
+        load_r(2)
+        load_wd_scales(wd4_s[:], 0, wd4_scales)
+        load_r(3)
+        nc.sync.dma_start(gate[:], wgo)
+        load_wd_words(N // 2, N)
 
-        gather_words(0, "got_w0", J)
+        gather_words(0, "got_w0")
         nc.vector.tensor_copy(got_s[:], tab_s[:].bitcast(U8).indirect(offsets[:]))
-        cast_wu(0, 88)
-        quant_wu(0)
-        cast_wu(1, 64)
-        quant_wu(1)
-        gather_words(1, "got_w1", HALF)
-        for a in range(2):
-            for b in range(4):
-                up(b, a)
-        for b in range(4, 8):
-            for a in range(2):
-                up(b, a)
-        gather_r(0)
-        gather_r(1)
-        nc.vector.quantize_mx(out=h_q[:].bitcast(FP8X4), scales=planes[:], in_=h_bf[:])
-        gather_r(2)
-        gather_r(3)
-        for quarter in range(4):
-            first_sum(quarter)
-        for nt in range(1, 4):
-            for step in (turn_r, product, turn_back):
-                for half in range(2):
-                    step(nt, half)
-        placed.append(keep.tile([P, T], F32, name="placed1", tag="r_all3", align_bytes=64))
-        nc.gpsimd.memset(placed[1][:].bitcast(I32), 0)
-        for nt in range(4):
-            scatter(nt, nt, 0, J)
+        quantise_wu(0)
+        banks = [psum.tile([P, 4, BLK], F32, name="bank%d" % b) for b in range(8)]
+        for b in range(8):
+            up_passes(banks[b], b, 0)
+        gather_words(1, "wu_bf0")
+        quantise_wu(1)
+        for b in range(8):
+            up_passes(banks[b], b, 1)
+            relu(banks[b], b)
+        gather_r(0, "wu_bf1")
+        gather_r(1, "r_got1")
+        for half in range(2):
+            quantise_h(half)
+        gather_r(2, "h_bf")
+        gather_r(3, "r_got3")
+        for half in range(2):
+            first_sum(half)
+        for c in range(1, 4):
+            turned_sum(c)
+        pages.append(keep.tile([P, T], F32, name="page1", tag="y_first"))
+        nc.gpsimd.memset(pages[1][:].bitcast(I32), 0)
+        for c in range(4):
+            nc.vector.tensor_tensor(pages[c % 2][:].indirect(offsets[:]), z[c][:], gate[:], MULT)
+            nc.sync.dma_start(out[chans(c), :], pages[c % 2][:])

@@ -22,7 +22,7 @@ RELU = mybir.ActivationFunctionType.Relu
 P = 128
 HALF = 512
 BLK = 128
-SCALAR_GROUPS = (88, 56)
+SCALAR_GROUPS = (80, 44)
 
 
 def tile_list_modp_relu_res_res_kernel(
@@ -41,7 +41,7 @@ def tile_list_modp_relu_res_res_kernel(
         wd8_s = planes[:, J // 4 : J // 4 + N]
         pages = [keep.tile([P, T], F32, name="page0")]
         tab_w = [keep.tile([P, T], I32, name="tab_w%d" % a, align_bytes=64) for a in range(2)]
-        wu_raw = [keep.tile([P, 4, R], F32, name="wu_raw%d" % a) for a in range(2)]
+        wu_raw = [keep.tile([P, 4, R], F32, name="wu_raw%d" % a, align_bytes=64) for a in range(2)]
         wd4_w = keep.tile([P, N // 2], I32, name="wd4_w", align_bytes=64)
         wd8_w = keep.tile([P, N], I32, name="wd8_w", align_bytes=64)
         r_all = [keep.tile([P, T], F32, name="r_all%d" % c, align_bytes=64) for c in range(4)]
@@ -103,7 +103,12 @@ def tile_list_modp_relu_res_res_kernel(
             dst = wu_bf[a][:].rearrange("p (t m j) -> p m j t", t=4, j=4)
             src = wu_raw[a][:].rearrange("p j (m t) -> p m j t", t=4)
             nc.scalar.activation(dst[:, :split, :, :], src[:, :split, :, :], COPY)
-            nc.vector.tensor_copy(dst[:, split:, :, :], src[:, split:, :, :])
+            if a == 0:
+                by_slot = wu_bf[a][:].rearrange("p (t m j) -> p t m j", t=4, j=4)
+                raw = wu_raw[a][:].rearrange("p j (m t) -> p t m j", t=4)
+                nc.gpsimd.tensor_scalar(by_slot[:, :, split:, :], raw[:, :, split:, :], 1.0, 0.0, MULT, ADD)
+            else:
+                nc.vector.tensor_copy(dst[:, split:, :, :], src[:, split:, :, :])
             nc.vector.quantize_mx(out=wu_q[a][:].bitcast(FP8X4), scales=wu_s[a][:], in_=wu_bf[a][:])
 
         def up_passes(bank, b, a):
@@ -205,16 +210,16 @@ def tile_list_modp_relu_res_res_kernel(
         banks = [psum.tile([P, 4, BLK], F32, name="bank%d" % b) for b in range(8)]
         for b in range(8):
             up_passes(banks[b], b, 0)
-        gather_words(1, "wu_bf0")
+        gather_words(1, "wu_raw0")
         quantise_wu(1)
         for b in range(8):
             up_passes(banks[b], b, 1)
             relu(banks[b], b)
-        gather_r(0, "wu_bf1")
+        gather_r(0, "wu_raw1")
         gather_r(1, "r_got1")
         for half in range(2):
             quantise_h(half)
-        gather_r(2, "h_bf")
+        gather_r(2, "r_got2")
         gather_r(3, "r_got3")
         for half in range(2):
             first_sum(half)

@@ -22,7 +22,8 @@ RELU = mybir.ActivationFunctionType.Relu
 P = 128
 HALF = 512
 BLK = 128
-SCALAR_GROUPS = (80, 44)
+TAB_HEAD = 640
+SCALAR_GROUPS = (88, 52)
 
 
 def tile_list_modp_relu_res_res_kernel(
@@ -65,16 +66,13 @@ def tile_list_modp_relu_res_res_kernel(
         def chans(c, width=1):
             return slice(width * c * P, width * (c + 1) * P)
 
-        def load_tab(a):
-            nc.sync.dma_start(tab_w[a][:], tab_words[a].rearrange("p t i -> p (t i)").bitcast(I32))
+        def load_tab(a, lo, hi):
+            nc.sync.dma_start(tab_w[a][:, lo:hi], tab_words[a].rearrange("p t i -> p (t i)").bitcast(I32)[:, lo:hi])
 
-        def load_tab_scales():
-            for q in range(2):
-                nc.sync.dma_start(tab_s[32 * q : 32 * q + 8, :], tab_scales[:, 4 * q : 4 * q + 4, :].bitcast(I32))
-            for q in range(2, 4):
-                for a in range(2):
-                    first = 32 * q + 4 * a
-                    nc.sync.dma_start(tab_s[first : first + 4, :], tab_scales[a, 4 * q : 4 * q + 4, :].bitcast(I32))
+        def load_tab_scales(lo, hi):
+            for row in range(lo, hi):
+                a, r = row % 2, row // 2
+                nc.sync.dma_start(tab_s[4 * a + r : P : 32, :], tab_scales[a, r:16:4, :].bitcast(I32))
 
         def load_wu(a):
             nc.sync.dma_start(wu_raw[a][:], wu[512 * a : 512 * (a + 1), :].rearrange("(p j) c -> p j c", j=4))
@@ -189,10 +187,12 @@ def tile_list_modp_relu_res_res_kernel(
                 nc.scalar.activation(z[c][:, half * HALF : (half + 1) * HALF], bank[:], COPY)
 
         nc.sync.dma_start(offsets[:], offs)
-        load_tab(0)
-        load_tab_scales()
+        load_tab(0, 0, TAB_HEAD)
+        load_tab_scales(0, 2)
+        load_tab(0, TAB_HEAD, T)
+        load_tab_scales(2, 8)
         load_wu(0)
-        load_tab(1)
+        load_tab(1, 0, T)
         load_wu(1)
         load_r(0)
         load_r(1)
@@ -201,7 +201,8 @@ def tile_list_modp_relu_res_res_kernel(
         load_r(2)
         load_wd_scales(wd4_s[:], 0, wd4_scales)
         load_r(3)
-        nc.sync.dma_start(gate[:], wgo)
+        for lo in (0, HALF):
+            nc.sync.dma_start(gate[:, lo : lo + HALF], wgo[:, lo : lo + HALF])
         load_wd_words(N // 2, N)
 
         gather_words(0, "got_w0")
@@ -229,4 +230,6 @@ def tile_list_modp_relu_res_res_kernel(
         nc.gpsimd.memset(pages[1][:].bitcast(I32), 0)
         for c in range(4):
             nc.vector.tensor_tensor(pages[c % 2][:].indirect(offsets[:]), z[c][:], gate[:], MULT)
-            nc.sync.dma_start(out[chans(c), :], pages[c % 2][:])
+            width = T if c == 3 else T // 2
+            for at in range(0, T, width):
+                nc.sync.dma_start(out[chans(c), at : at + width], pages[c % 2][:, at : at + width])

@@ -20,6 +20,7 @@ COPY = mybir.ActivationFunctionType.Copy
 RELU = mybir.ActivationFunctionType.Relu
 
 P = 128
+ALIGN = 256
 HALF = 512
 BLK = 128
 TAB_HEAD = 640
@@ -36,27 +37,27 @@ def tile_list_modp_relu_res_res_kernel(
         psum = ctx.enter_context(tc.psum_pool(name="psum", bufs=1))
 
         offsets = keep.tile([P, J // 16], U16, name="offsets")
-        tab_s = keep.tile([P, T // 4], I32, name="tab_s", align_bytes=64)
-        wd4_s = keep.tile([P, N // 4], I32, name="wd4_s", align_bytes=64)
-        planes = keep.tile([P, J], U8, name="planes", align_bytes=64)
+        tab_s = keep.tile([P, T // 4], I32, name="tab_s", align_bytes=ALIGN)
+        wd4_s = keep.tile([P, N // 4], I32, name="wd4_s", align_bytes=ALIGN)
+        planes = keep.tile([P, J], U8, name="planes", align_bytes=ALIGN)
         wd8_s = planes[:, J // 4 : J // 4 + N]
-        pages = [keep.tile([P, T], F32, name="page0")]
-        tab_w = [keep.tile([P, T], I32, name="tab_w%d" % a, align_bytes=64) for a in range(2)]
-        wu_raw = [keep.tile([P, 4, R], F32, name="wu_raw%d" % a, align_bytes=64) for a in range(2)]
-        wd4_w = keep.tile([P, N // 2], I32, name="wd4_w", align_bytes=64)
-        wd8_w = keep.tile([P, N], I32, name="wd8_w", align_bytes=64)
-        r_all = [keep.tile([P, T], F32, name="r_all%d" % c, align_bytes=64) for c in range(4)]
-        gate = keep.tile([P, J], F32, name="gate")
-        ident = keep.tile([P, P], F32, name="ident")
+        pages = [keep.tile([P, T], F32, name="page0", align_bytes=ALIGN)]
+        tab_w = [keep.tile([P, T], I32, name="tab_w%d" % a, align_bytes=ALIGN) for a in range(2)]
+        wu_raw = [keep.tile([P, 4, R], F32, name="wu_raw%d" % a, align_bytes=ALIGN) for a in range(2)]
+        wd4_w = keep.tile([P, N // 2], I32, name="wd4_w", align_bytes=ALIGN)
+        wd8_w = keep.tile([P, N], I32, name="wd8_w", align_bytes=ALIGN)
+        r_all = [keep.tile([P, T], F32, name="r_all%d" % c, align_bytes=ALIGN) for c in range(4)]
+        gate = keep.tile([P, J], F32, name="gate", align_bytes=ALIGN)
+        ident = keep.tile([P, P], F32, name="ident", align_bytes=ALIGN)
         got_w, r_got = {}, {}
-        got_s = keep.tile([P, J], U8, name="got_s", align_bytes=64)
-        wu_bf = [keep.tile([P, 4 * R], BF16, name="wu_bf%d" % a, align_bytes=64) for a in range(2)]
-        wu_q = [keep.tile([P, R], U32, name="wu_q%d" % a, align_bytes=64) for a in range(2)]
-        wu_s = [keep.tile([P, R], U8, name="wu_s%d" % a, align_bytes=64) for a in range(2)]
-        h_bf = keep.tile([P, 4 * J], BF16, name="h_bf", align_bytes=64)
-        h_q = keep.tile([P, J], U32, name="h_q", align_bytes=64)
-        y_first = keep.tile([P, J], F32, name="y_first")
-        z = [keep.tile([P, J], F32, name="z%d" % c) for c in range(4)]
+        got_s = keep.tile([P, J], U8, name="got_s", align_bytes=ALIGN)
+        wu_bf = [keep.tile([P, 4 * R], BF16, name="wu_bf%d" % a, align_bytes=ALIGN) for a in range(2)]
+        wu_q = [keep.tile([P, R], U32, name="wu_q%d" % a, align_bytes=ALIGN) for a in range(2)]
+        wu_s = [keep.tile([P, R], U8, name="wu_s%d" % a, align_bytes=ALIGN) for a in range(2)]
+        h_bf = keep.tile([P, 4 * J], BF16, name="h_bf", align_bytes=ALIGN)
+        h_q = keep.tile([P, J], U32, name="h_q", align_bytes=ALIGN)
+        y_first = keep.tile([P, J], F32, name="y_first", align_bytes=ALIGN)
+        z = [keep.tile([P, J], F32, name="z%d" % c, align_bytes=ALIGN) for c in range(4)]
 
         nc.gpsimd.memset(tab_s[:], 0)
         nc.vector.memset(wd4_s[:], 0)
@@ -89,11 +90,11 @@ def tile_list_modp_relu_res_res_kernel(
             nc.sync.dma_start(wd4_w[:, lo // 2 : hi // 2], wd4_words[0].bitcast(I32)[:, lo // 2 : hi // 2])
 
         def gather_words(a, tag):
-            got_w[a] = keep.tile([P, J], U32, name="got_w%d" % a, tag=tag, align_bytes=64)
+            got_w[a] = keep.tile([P, J], U32, name="got_w%d" % a, tag=tag, align_bytes=ALIGN)
             nc.vector.tensor_copy(got_w[a][:], tab_w[a][:].bitcast(U32).indirect(offsets[:]))
 
         def gather_r(c, tag):
-            r_got[c] = keep.tile([P, J], F32, name="r_got%d" % c, tag=tag, align_bytes=64)
+            r_got[c] = keep.tile([P, J], F32, name="r_got%d" % c, tag=tag, align_bytes=ALIGN)
             nc.vector.tensor_copy(r_got[c][:], r_all[c][:].indirect(offsets[:]))
 
         def quantise_wu(a):
@@ -226,7 +227,7 @@ def tile_list_modp_relu_res_res_kernel(
             first_sum(half)
         for c in range(1, 4):
             turned_sum(c)
-        pages.append(keep.tile([P, T], F32, name="page1", tag="y_first"))
+        pages.append(keep.tile([P, T], F32, name="page1", tag="y_first", align_bytes=ALIGN))
         nc.gpsimd.memset(pages[1][:].bitcast(I32), 0)
         for c in range(4):
             nc.vector.tensor_tensor(pages[c % 2][:].indirect(offsets[:]), z[c][:], gate[:], MULT)

@@ -24,7 +24,7 @@ ALIGN = 256
 HALF = 512
 BLK = 128
 TAB_HEAD = 640
-SCALAR_GROUPS = (88, 52)
+SCALAR_GROUPS = 88
 
 
 def tile_list_modp_relu_res_res_kernel(
@@ -97,18 +97,32 @@ def tile_list_modp_relu_res_res_kernel(
             r_got[c] = keep.tile([P, J], F32, name="r_got%d" % c, tag=tag, align_bytes=ALIGN)
             nc.vector.tensor_copy(r_got[c][:], r_all[c][:].indirect(offsets[:]))
 
-        def quantise_wu(a):
-            split = SCALAR_GROUPS[a]
+        def rounding_views(a):
             dst = wu_bf[a][:].rearrange("p (t m j) -> p m j t", t=4, j=4)
             src = wu_raw[a][:].rearrange("p j (m t) -> p m j t", t=4)
-            nc.scalar.activation(dst[:, :split, :, :], src[:, :split, :, :], COPY)
-            if a == 0:
-                by_slot = wu_bf[a][:].rearrange("p (t m j) -> p t m j", t=4, j=4)
-                raw = wu_raw[a][:].rearrange("p j (m t) -> p t m j", t=4)
-                nc.gpsimd.tensor_scalar(by_slot[:, :, split:, :], raw[:, :, split:, :], 1.0, 0.0, MULT, ADD)
-            else:
-                nc.vector.tensor_copy(dst[:, split:, :, :], src[:, split:, :, :])
-            nc.vector.quantize_mx(out=wu_q[a][:].bitcast(FP8X4), scales=wu_s[a][:], in_=wu_bf[a][:])
+            return dst, src
+
+        def quantise_wu(a, lo, hi):
+            nc.vector.quantize_mx(
+                out=wu_q[a][:, lo * P : hi * P].bitcast(FP8X4),
+                scales=wu_s[a][:, lo * P : hi * P],
+                in_=wu_bf[a][:, 4 * lo * P : 4 * hi * P],
+            )
+
+        def first_wu():
+            dst, src = rounding_views(0)
+            nc.scalar.activation(dst[:, :SCALAR_GROUPS, :, :], src[:, :SCALAR_GROUPS, :, :], COPY)
+            by_slot = wu_bf[0][:].rearrange("p (t m j) -> p t m j", t=4, j=4)
+            raw = wu_raw[0][:].rearrange("p j (m t) -> p t m j", t=4)
+            nc.gpsimd.tensor_scalar(by_slot[:, :, SCALAR_GROUPS:, :], raw[:, :, SCALAR_GROUPS:, :], 1.0, 0.0, MULT, ADD)
+            quantise_wu(0, 0, 4)
+
+        def second_wu():
+            dst, src = rounding_views(1)
+            nc.scalar.activation(dst[:, :, :, :2], src[:, :, :, :2], COPY)
+            nc.vector.tensor_copy(dst[:, :, :, 2:], src[:, :, :, 2:])
+            quantise_wu(1, 0, 2)
+            quantise_wu(1, 2, 4)
 
         def up_passes(bank, b, a):
             cols = slice(b * BLK, (b + 1) * BLK)
@@ -208,12 +222,12 @@ def tile_list_modp_relu_res_res_kernel(
 
         gather_words(0, "got_w0")
         nc.vector.tensor_copy(got_s[:], tab_s[:].bitcast(U8).indirect(offsets[:]))
-        quantise_wu(0)
+        first_wu()
         banks = [psum.tile([P, 4, BLK], F32, name="bank%d" % b) for b in range(8)]
         for b in range(8):
             up_passes(banks[b], b, 0)
         gather_words(1, "wu_raw0")
-        quantise_wu(1)
+        second_wu()
         for b in range(8):
             up_passes(banks[b], b, 1)
             relu(banks[b], b)

@@ -57,7 +57,8 @@ def tile_list_modp_relu_res_res_kernel(
         h_bf = keep.tile([P, 4 * J], BF16, name="h_bf", align_bytes=ALIGN)
         h_q = keep.tile([P, J], U32, name="h_q", align_bytes=ALIGN)
         y_first = keep.tile([P, J], F32, name="y_first", align_bytes=ALIGN)
-        z = [keep.tile([P, J], F32, name="z%d" % c, align_bytes=ALIGN) for c in range(4)]
+        z = [keep.tile([P, J], F32, name="z%d" % c, align_bytes=ALIGN) for c in range(3)]
+        gate_col = keep.tile([P, J // P], F32, name="gate_col")
 
         nc.gpsimd.memset(tab_s[:], 0)
         nc.vector.memset(wd4_s[:], 0)
@@ -169,6 +170,19 @@ def tile_list_modp_relu_res_res_kernel(
             nc.scalar.activation(y_first[:, cols], bank[:], COPY)
             nc.gpsimd.tensor_tensor(z[0][:, cols], y_first[:, cols], r_got[0][:, cols], ADD)
 
+        def gate_columns():
+            for half in range(2):
+                bank = psum.tile([P, 4, BLK], F32, name="bank%d" % (6 + half))
+                for i in range(4):
+                    at = half * HALF + i * BLK
+                    nc.tensor.transpose(bank[:, i, :], gate[:, at : at + BLK], ident[:])
+                nc.scalar.activation(gate_col[:, 4 * half : 4 * half + 4], bank[:, :, 0], COPY)
+
+        def weighed_copy(dst, bank, half):
+            for i in range(4):
+                at = 4 * half + i
+                nc.scalar.activation(dst[:, chans(i)], bank[:, chans(i)], COPY, scale=gate_col[:, at : at + 1])
+
         def turned_sum(c):
             r_t, y_t = [], []
             for half in range(2):
@@ -177,7 +191,7 @@ def tile_list_modp_relu_res_res_kernel(
                     at = half * HALF + i * BLK
                     nc.tensor.transpose(bank[:, chans(i)], r_got[c][:, at : at + BLK], ident[:])
                 r_t.append(ring.tile([P, HALF], F32, name="r_t"))
-                nc.scalar.activation(r_t[half][:], bank[:], COPY)
+                weighed_copy(r_t[half], bank, half)
             for half in range(2):
                 bank = psum.tile([P, HALF], F32, name="bank0")
                 for i in range(4):
@@ -193,13 +207,41 @@ def tile_list_modp_relu_res_res_kernel(
                             stop=(tier == 1),
                         )
                 y_t.append(ring.tile([P, HALF], F32, name="y_t"))
-                nc.scalar.activation(y_t[half][:], bank[:], COPY)
+                weighed_copy(y_t[half], bank, half)
             for half in range(2):
                 bank = psum.tile([P, HALF], F32, name="bank%d" % (4 + half))
                 for i in range(4):
                     nc.tensor.matmul(bank[:, chans(i)], y_t[half][:, chans(i)], ident[:], start=True, stop=False, is_transpose=True)
                     nc.tensor.matmul(bank[:, chans(i)], r_t[half][:, chans(i)], ident[:], start=False, stop=True, is_transpose=True)
                 nc.scalar.activation(z[c][:, half * HALF : (half + 1) * HALF], bank[:], COPY)
+
+        def late_product(c):
+            y = keep.tile([P, J], F32, name="y%d" % c, align_bytes=ALIGN)
+            for half in range(2):
+                cols = slice(half * HALF, (half + 1) * HALF)
+                bank = psum.tile([P, HALF], F32, name="bank%d" % (4 + half))
+                for tier, (words, scales) in enumerate(wd_operands(c)):
+                    nc.tensor.matmul_mx(
+                        out=bank[:],
+                        lhsT=words,
+                        lhsT_scale=scales,
+                        rhs=h_q[:, cols].bitcast(FP8X4),
+                        rhs_scale=planes[:, cols],
+                        start=(tier == 0),
+                        stop=(tier == 1),
+                    )
+                nc.scalar.activation(y[:, cols], bank[:], COPY)
+            return y
+
+        def late_sum(c, y):
+            total = keep.tile([P, J], F32, name="total%d" % c, tag="z%d" % (c - 2), align_bytes=ALIGN)
+            nc.gpsimd.tensor_tensor(total[:], y[:], r_got[c][:], ADD)
+            return total
+
+        def store(c):
+            width = T if c == 3 else T // 2
+            for at in range(0, T, width):
+                nc.sync.dma_start(out[chans(c), at : at + width], pages[c % 2][:, at : at + width])
 
         nc.sync.dma_start(offsets[:], offs)
         load_tab(0, 0, TAB_HEAD)
@@ -239,12 +281,18 @@ def tile_list_modp_relu_res_res_kernel(
         gather_r(3, "r_got3")
         for half in range(2):
             first_sum(half)
-        for c in range(1, 4):
-            turned_sum(c)
+        gate_columns()
+        turned_sum(1)
+        y_late = {c: late_product(c) for c in (2, 3)}
         pages.append(keep.tile([P, T], F32, name="page1", tag="y_first", align_bytes=ALIGN))
         nc.gpsimd.memset(pages[1][:].bitcast(I32), 0)
-        for c in range(4):
-            nc.vector.tensor_tensor(pages[c % 2][:].indirect(offsets[:]), z[c][:], gate[:], MULT)
-            width = T if c == 3 else T // 2
-            for at in range(0, T, width):
-                nc.sync.dma_start(out[chans(c), at : at + width], pages[c % 2][:, at : at + width])
+        nc.vector.tensor_tensor(pages[0][:].indirect(offsets[:]), z[0][:], gate[:], MULT)
+        store(0)
+        nc.gpsimd.tensor_tensor(z[2][:], late_sum(2, y_late[2])[:], gate[:], MULT)
+        nc.vector.tensor_copy(pages[1][:].indirect(offsets[:]), z[1][:])
+        store(1)
+        last = late_sum(3, y_late[3])
+        nc.vector.tensor_copy(pages[0][:].indirect(offsets[:]), z[2][:])
+        store(2)
+        nc.vector.tensor_tensor(pages[1][:].indirect(offsets[:]), last[:], gate[:], MULT)
+        store(3)

@@ -23,7 +23,6 @@ P = 128
 ALIGN = 256
 HALF = 512
 BLK = 128
-TAB_HEAD = 640
 SCALAR_GROUPS = 88
 
 
@@ -68,13 +67,16 @@ def tile_list_modp_relu_res_res_kernel(
         def chans(c, width=1):
             return slice(width * c * P, width * (c + 1) * P)
 
-        def load_tab(a, lo, hi):
-            nc.sync.dma_start(tab_w[a][:, lo:hi], tab_words[a].rearrange("p t i -> p (t i)").bitcast(I32)[:, lo:hi])
+        def load_tab(a):
+            nc.sync.dma_start(tab_w[a][:], tab_words[a].rearrange("p t i -> p (t i)").bitcast(I32))
 
-        def load_tab_scales(lo, hi):
-            for row in range(lo, hi):
-                a, r = row % 2, row // 2
-                nc.sync.dma_start(tab_s[4 * a + r : P : 32, :], tab_scales[a, r:16:4, :].bitcast(I32))
+        def load_tab_scales():
+            for q in (0, 1):
+                nc.sync.dma_start(tab_s[32 * q : 32 * q + 8, :], tab_scales[:, 4 * q : 4 * q + 4, :].bitcast(I32))
+            for q in (2, 3):
+                for a in range(2):
+                    rows = slice(32 * q + 4 * a, 32 * q + 4 * a + 4)
+                    nc.sync.dma_start(tab_s[rows, :], tab_scales[a, 4 * q : 4 * q + 4, :].bitcast(I32))
 
         def load_wu(a):
             nc.sync.dma_start(wu_raw[a][:], wu[512 * a : 512 * (a + 1), :].rearrange("(p j) c -> p j c", j=4))
@@ -239,17 +241,13 @@ def tile_list_modp_relu_res_res_kernel(
             return total
 
         def store(c):
-            width = T if c == 3 else T // 2
-            for at in range(0, T, width):
-                nc.sync.dma_start(out[chans(c), at : at + width], pages[c % 2][:, at : at + width])
+            nc.sync.dma_start(out[chans(c), :], pages[c % 2][:])
 
         nc.sync.dma_start(offsets[:], offs)
-        load_tab(0, 0, TAB_HEAD)
-        load_tab_scales(0, 2)
-        load_tab(0, TAB_HEAD, T)
-        load_tab_scales(2, 8)
+        load_tab(0)
+        load_tab_scales()
         load_wu(0)
-        load_tab(1, 0, T)
+        load_tab(1)
         load_wu(1)
         load_r(0)
         load_r(1)
@@ -258,8 +256,7 @@ def tile_list_modp_relu_res_res_kernel(
         load_r(2)
         load_wd_scales(wd4_s[:], 0, wd4_scales)
         load_r(3)
-        for lo in (0, HALF):
-            nc.sync.dma_start(gate[:, lo : lo + HALF], wgo[:, lo : lo + HALF])
+        nc.sync.dma_start(gate[:], wgo)
         load_wd_words(N // 2, N)
 
         gather_words(0, "got_w0")

@@ -23,7 +23,9 @@ P = 128
 ALIGN = 256
 HALF = 512
 BLK = 128
-SCALAR_GROUPS = 88
+SCALAR_GROUPS = 56
+EARLY_SCALES = 2
+PARKED = 12
 
 
 def tile_list_modp_relu_res_res_kernel(
@@ -33,6 +35,7 @@ def tile_list_modp_relu_res_res_kernel(
     with ExitStack() as ctx:
         keep = ctx.enter_context(tc.tile_pool(name="keep", bufs=1))
         ring = ctx.enter_context(tc.tile_pool(name="ring", bufs=6))
+        reuse = ctx.enter_context(tc.tile_pool(name="reuse", bufs=1))
         psum = ctx.enter_context(tc.psum_pool(name="psum", bufs=1))
 
         offsets = keep.tile([P, J // 16], U16, name="offsets")
@@ -42,7 +45,10 @@ def tile_list_modp_relu_res_res_kernel(
         wd8_s = planes[:, J // 4 : J // 4 + N]
         pages = [keep.tile([P, T], F32, name="page0", align_bytes=ALIGN)]
         tab_w = [keep.tile([P, T], I32, name="tab_w%d" % a, align_bytes=ALIGN) for a in range(2)]
-        wu_raw = [keep.tile([P, 4, R], F32, name="wu_raw%d" % a, align_bytes=ALIGN) for a in range(2)]
+        wu_raw = [
+            keep.tile([P, 4, R], F32, name="wu_raw0", align_bytes=ALIGN),
+            reuse.tile([P, 4, R], F32, name="wu_raw1", offset=0, align_bytes=ALIGN),
+        ]
         wd4_w = keep.tile([P, N // 2], I32, name="wd4_w", align_bytes=ALIGN)
         wd8_w = keep.tile([P, N], I32, name="wd8_w", align_bytes=ALIGN)
         r_all = [keep.tile([P, T], F32, name="r_all%d" % c, align_bytes=ALIGN) for c in range(4)]
@@ -50,9 +56,9 @@ def tile_list_modp_relu_res_res_kernel(
         ident = keep.tile([P, P], F32, name="ident", align_bytes=ALIGN)
         got_w, r_got = {}, {}
         got_s = keep.tile([P, J], U8, name="got_s", align_bytes=ALIGN)
-        wu_bf = [keep.tile([P, 4 * R], BF16, name="wu_bf%d" % a, align_bytes=ALIGN) for a in range(2)]
+        wu_bf = [keep.tile([P, 4 * R], BF16, name="wu_bf0", align_bytes=ALIGN)]
         wu_q = [keep.tile([P, R], U32, name="wu_q%d" % a, align_bytes=ALIGN) for a in range(2)]
-        wu_s = [keep.tile([P, R], U8, name="wu_s%d" % a, align_bytes=ALIGN) for a in range(2)]
+        wu_s = {(a, u): keep.tile([P, R // 2], U8, name="wu_s%d%d" % (a, u), align_bytes=ALIGN) for a, u in ((0, 0), (0, 1), (1, 0))}
         h_bf = keep.tile([P, 4 * J], BF16, name="h_bf", align_bytes=ALIGN)
         h_q = keep.tile([P, J], U32, name="h_q", align_bytes=ALIGN)
         y_first = keep.tile([P, J], F32, name="y_first", align_bytes=ALIGN)
@@ -70,13 +76,10 @@ def tile_list_modp_relu_res_res_kernel(
         def load_tab(a):
             nc.sync.dma_start(tab_w[a][:], tab_words[a].rearrange("p t i -> p (t i)").bitcast(I32))
 
-        def load_tab_scales():
-            for q in (0, 1):
-                nc.sync.dma_start(tab_s[32 * q : 32 * q + 8, :], tab_scales[:, 4 * q : 4 * q + 4, :].bitcast(I32))
-            for q in (2, 3):
-                for a in range(2):
-                    rows = slice(32 * q + 4 * a, 32 * q + 4 * a + 4)
-                    nc.sync.dma_start(tab_s[rows, :], tab_scales[a, 4 * q : 4 * q + 4, :].bitcast(I32))
+        def load_tab_scales(lo, hi):
+            for row in range(lo, hi):
+                a, r = row % 2, row // 2
+                nc.sync.dma_start(tab_s[4 * a + r : P : 32, :], tab_scales[a, r:16:4, :].bitcast(I32))
 
         def load_wu(a):
             nc.sync.dma_start(wu_raw[a][:], wu[512 * a : 512 * (a + 1), :].rearrange("(p j) c -> p j c", j=4))
@@ -96,8 +99,11 @@ def tile_list_modp_relu_res_res_kernel(
             got_w[a] = keep.tile([P, J], U32, name="got_w%d" % a, tag=tag, align_bytes=ALIGN)
             nc.vector.tensor_copy(got_w[a][:], tab_w[a][:].bitcast(U32).indirect(offsets[:]))
 
-        def gather_r(c, tag):
-            r_got[c] = keep.tile([P, J], F32, name="r_got%d" % c, tag=tag, align_bytes=ALIGN)
+        def gather_r(c):
+            if c == 0:
+                r_got[c] = reuse.tile([P, J], F32, name="r_got0", offset=0, align_bytes=ALIGN)
+            else:
+                r_got[c] = keep.tile([P, J], F32, name="r_got%d" % c, align_bytes=ALIGN)
             nc.vector.tensor_copy(r_got[c][:], r_all[c][:].indirect(offsets[:]))
 
         def rounding_views(a):
@@ -105,40 +111,51 @@ def tile_list_modp_relu_res_res_kernel(
             src = wu_raw[a][:].rearrange("p j (m t) -> p m j t", t=4)
             return dst, src
 
-        def quantise_wu(a, lo, hi):
+        def quantise_wu(a, u):
             nc.vector.quantize_mx(
-                out=wu_q[a][:, lo * P : hi * P].bitcast(FP8X4),
-                scales=wu_s[a][:, lo * P : hi * P],
-                in_=wu_bf[a][:, 4 * lo * P : 4 * hi * P],
+                out=wu_q[a][:, chans(u, 2)].bitcast(FP8X4),
+                scales=wu_s[a, u][:],
+                in_=wu_bf[a][:, chans(u, 8)],
             )
 
         def first_wu():
             dst, src = rounding_views(0)
-            nc.scalar.activation(dst[:, :SCALAR_GROUPS, :, :], src[:, :SCALAR_GROUPS, :, :], COPY)
+            nc.scalar.activation(dst[:, :, :, :2], src[:, :, :, :2], COPY)
+            nc.scalar.activation(dst[:, :SCALAR_GROUPS, :, 2:], src[:, :SCALAR_GROUPS, :, 2:], COPY)
             by_slot = wu_bf[0][:].rearrange("p (t m j) -> p t m j", t=4, j=4)
             raw = wu_raw[0][:].rearrange("p j (m t) -> p t m j", t=4)
-            nc.gpsimd.tensor_scalar(by_slot[:, :, SCALAR_GROUPS:, :], raw[:, :, SCALAR_GROUPS:, :], 1.0, 0.0, MULT, ADD)
-            quantise_wu(0, 0, 4)
+            nc.gpsimd.tensor_scalar(by_slot[:, 2:, SCALAR_GROUPS:, :], raw[:, 2:, SCALAR_GROUPS:, :], 1.0, 0.0, MULT, ADD)
+            quantise_wu(0, 0)
+            quantise_wu(0, 1)
 
         def second_wu():
+            wu_bf.append(keep.tile([P, 4 * R], BF16, name="wu_bf1", tag="wu_raw0", align_bytes=ALIGN))
             dst, src = rounding_views(1)
             nc.scalar.activation(dst[:, :, :, :2], src[:, :, :, :2], COPY)
             nc.vector.tensor_copy(dst[:, :, :, 2:], src[:, :, :, 2:])
-            quantise_wu(1, 0, 2)
-            quantise_wu(1, 2, 4)
+            quantise_wu(1, 0)
+            wu_s[1, 1] = reuse.tile([P, R // 2], U8, name="wu_s11", offset=4 * J, align_bytes=ALIGN)
+            quantise_wu(1, 1)
 
-        def up_passes(bank, b, a):
+        def up_passes(bank, b, order, lo, hi):
             cols = slice(b * BLK, (b + 1) * BLK)
-            for t in range(4):
+            for at in range(lo, hi):
+                a, t = order[at]
                 nc.tensor.matmul_mx(
                     out=bank[:, t, :],
                     lhsT=wu_q[a][:, chans(t)].bitcast(FP8X4),
-                    lhsT_scale=wu_s[a][:, chans(t)],
+                    lhsT_scale=wu_s[a, t // 2][:, chans(t % 2)],
                     rhs=got_w[a][:, cols].bitcast(FP8X4),
                     rhs_scale=got_s[4 * a :, cols],
-                    start=(a == 0 and t == 0),
-                    stop=(a == 1 and t == 3),
+                    start=(at == 0),
+                    stop=(at == 7),
                 )
+
+        def pass_order(b):
+            parked = min(4, max(0, PARKED - 4 * b))
+            second = [(1, t) for t in ((0, 1, 2, 3) if b == 0 else (2, 3, 0, 1))]
+            first = [(0, t) for t in range(4)]
+            return first[:parked] + second + first[parked:], parked
 
         def relu(bank, b):
             dst = h_bf[:, 4 * b * BLK : 4 * (b + 1) * BLK].rearrange("p (n t) -> p n t", t=4)
@@ -245,37 +262,40 @@ def tile_list_modp_relu_res_res_kernel(
 
         nc.sync.dma_start(offsets[:], offs)
         load_tab(0)
-        load_tab_scales()
-        load_wu(0)
+        load_tab_scales(0, EARLY_SCALES)
         load_tab(1)
+        load_tab_scales(EARLY_SCALES, 8)
+        load_wu(0)
         load_wu(1)
         load_r(0)
         load_r(1)
         load_wd_scales(wd8_s.bitcast(I32), 4, wd8_scales)
-        load_wd_words(0, N // 2)
+        load_wd_words(0, N)
         load_r(2)
         load_wd_scales(wd4_s[:], 0, wd4_scales)
         load_r(3)
         nc.sync.dma_start(gate[:], wgo)
-        load_wd_words(N // 2, N)
 
         gather_words(0, "got_w0")
+        gather_words(1, "got_w1")
         nc.vector.tensor_copy(got_s[:], tab_s[:].bitcast(U8).indirect(offsets[:]))
         first_wu()
         banks = [psum.tile([P, 4, BLK], F32, name="bank%d" % b) for b in range(8)]
-        for b in range(8):
-            up_passes(banks[b], b, 0)
-        gather_words(1, "wu_raw0")
+        for lo in (0, 2):
+            for b in range(8):
+                order, parked = pass_order(b)
+                up_passes(banks[b], b, order, lo, min(lo + 2, parked))
         second_wu()
         for b in range(8):
-            up_passes(banks[b], b, 1)
+            order, parked = pass_order(b)
+            up_passes(banks[b], b, order, parked, 8)
             relu(banks[b], b)
-        gather_r(0, "wu_raw1")
-        gather_r(1, "r_got1")
+        gather_r(0)
+        gather_r(1)
         for half in range(2):
             quantise_h(half)
-        gather_r(2, "r_got2")
-        gather_r(3, "r_got3")
+        gather_r(2)
+        gather_r(3)
         for half in range(2):
             first_sum(half)
         gate_columns()

@@ -260,8 +260,8 @@ def tile_list_modp_relu_res_res_kernel(
         def store(c):
             nc.sync.dma_start(out[chans(c), :], pages[c % 2][:])
 
-        nc.sync.dma_start(offsets[:], offs)
         load_tab(0)
+        nc.sync.dma_start(offsets[:], offs)
         load_tab_scales(0, EARLY_SCALES)
         load_tab(1)
         load_tab_scales(EARLY_SCALES, 8)

from contextlib import ExitStack

import concourse.mybir as mybir
from concourse.masks import make_identity

K, R, N, T, J = 1024, 512, 512, 2048, 1024
FLOPS = 2 * K * R * J + 2 * 2 * R * N * J

F32 = mybir.dt.float32
BF16 = mybir.dt.bfloat16
I32 = mybir.dt.int32
U32 = mybir.dt.uint32
U16 = mybir.dt.uint16
U8 = mybir.dt.uint8
FP8X4 = mybir.dt.float8_e4m3fn_x4
FP4X4 = mybir.dt.float4_e2m1fn_x4
MULT = mybir.AluOpType.mult
ADD = mybir.AluOpType.add
COPY = mybir.ActivationFunctionType.Copy
RELU = mybir.ActivationFunctionType.Relu

P = 128
ALIGN = 256
HALF = 512
BLK = 128
SCALAR_GROUPS = 56
EARLY_SCALES = 2
PARKED = 12


def tile_list_modp_relu_res_res_kernel(
    tc, tab_words, tab_scales, wu, wd4_words, wd4_scales, wd8_words, wd8_scales, rT, wgo, offs, out
):
    nc = tc.nc
    with ExitStack() as ctx:
        keep = ctx.enter_context(tc.tile_pool(name="keep", bufs=1))
        ring = ctx.enter_context(tc.tile_pool(name="ring", bufs=6))
        reuse = ctx.enter_context(tc.tile_pool(name="reuse", bufs=1))
        psum = ctx.enter_context(tc.psum_pool(name="psum", bufs=1))

        offsets = keep.tile([P, J // 16], U16, name="offsets")
        tab_s = keep.tile([P, T // 4], I32, name="tab_s", align_bytes=ALIGN)
        wd4_s = keep.tile([P, N // 4], I32, name="wd4_s", align_bytes=ALIGN)
        planes = keep.tile([P, J], U8, name="planes", align_bytes=ALIGN)
        wd8_s = planes[:, J // 4 : J // 4 + N]
        pages = [keep.tile([P, T], F32, name="page0", align_bytes=ALIGN)]
        tab_w = [keep.tile([P, T], I32, name="tab_w%d" % a, align_bytes=ALIGN) for a in range(2)]
        wu_raw = [
            keep.tile([P, 4, R], F32, name="wu_raw0", align_bytes=ALIGN),
            reuse.tile([P, 4, R], F32, name="wu_raw1", offset=0, align_bytes=ALIGN),
        ]
        wd4_w = keep.tile([P, N // 2], I32, name="wd4_w", align_bytes=ALIGN)
        wd8_w = keep.tile([P, N], I32, name="wd8_w", align_bytes=ALIGN)
        r_all = [keep.tile([P, T], F32, name="r_all%d" % c, align_bytes=ALIGN) for c in range(4)]
        gate = keep.tile([P, J], F32, name="gate", align_bytes=ALIGN)
        ident = keep.tile([P, P], F32, name="ident", align_bytes=ALIGN)
        got_w, r_got = {}, {}
        got_s = keep.tile([P, J], U8, name="got_s", align_bytes=ALIGN)
        wu_bf = [keep.tile([P, 4 * R], BF16, name="wu_bf0", align_bytes=ALIGN)]
        wu_q = [keep.tile([P, R], U32, name="wu_q%d" % a, align_bytes=ALIGN) for a in range(2)]
        wu_s = {(a, u): keep.tile([P, R // 2], U8, name="wu_s%d%d" % (a, u), align_bytes=ALIGN) for a, u in ((0, 0), (0, 1), (1, 0))}
        h_bf = keep.tile([P, 4 * J], BF16, name="h_bf", align_bytes=ALIGN)
        h_q = keep.tile([P, J], U32, name="h_q", align_bytes=ALIGN)
        y_first = keep.tile([P, J], F32, name="y_first", align_bytes=ALIGN)
        z = [keep.tile([P, J], F32, name="z%d" % c, align_bytes=ALIGN) for c in range(3)]
        gate_col = keep.tile([P, J // P], F32, name="gate_col")

        nc.gpsimd.memset(tab_s[:], 0)
        nc.vector.memset(wd4_s[:], 0)
        nc.vector.memset(pages[0][:].bitcast(I32), 0)
        make_identity(nc, ident[:])

        def chans(c, width=1):
            return slice(width * c * P, width * (c + 1) * P)

        def load_tab(a):
            nc.sync.dma_start(tab_w[a][:], tab_words[a].rearrange("p t i -> p (t i)").bitcast(I32))

        def load_tab_scales(lo, hi):
            for row in range(lo, hi):
                a, r = row % 2, row // 2
                nc.sync.dma_start(tab_s[4 * a + r : P : 32, :], tab_scales[a, r:16:4, :].bitcast(I32))

        def load_wu(a):
            nc.sync.dma_start(wu_raw[a][:], wu[512 * a : 512 * (a + 1), :].rearrange("(p j) c -> p j c", j=4))

        def load_r(c):
            nc.sync.dma_start(r_all[c][:], rT[chans(c), :])

        def load_wd_scales(dst, first, src):
            for q in range(4):
                nc.sync.dma_start(dst[32 * q + first : 32 * q + first + 4, :], src[0, 4 * q : 4 * q + 4, :].bitcast(I32))

        def load_wd_words(lo, hi):
            nc.sync.dma_start(wd8_w[:, lo:hi], wd8_words[0].rearrange("p n i -> p (n i)").bitcast(I32)[:, lo:hi])
            nc.sync.dma_start(wd4_w[:, lo // 2 : hi // 2], wd4_words[0].bitcast(I32)[:, lo // 2 : hi // 2])

        def gather_words(a, tag):
            got_w[a] = keep.tile([P, J], U32, name="got_w%d" % a, tag=tag, align_bytes=ALIGN)
            nc.vector.tensor_copy(got_w[a][:], tab_w[a][:].bitcast(U32).indirect(offsets[:]))

        def gather_r(c):
            if c == 0:
                r_got[c] = reuse.tile([P, J], F32, name="r_got0", offset=0, align_bytes=ALIGN)
            else:
                r_got[c] = keep.tile([P, J], F32, name="r_got%d" % c, align_bytes=ALIGN)
            nc.vector.tensor_copy(r_got[c][:], r_all[c][:].indirect(offsets[:]))

        def rounding_views(a):
            dst = wu_bf[a][:].rearrange("p (t m j) -> p m j t", t=4, j=4)
            src = wu_raw[a][:].rearrange("p j (m t) -> p m j t", t=4)
            return dst, src

        def quantise_wu(a, u):
            nc.vector.quantize_mx(
                out=wu_q[a][:, chans(u, 2)].bitcast(FP8X4),
                scales=wu_s[a, u][:],
                in_=wu_bf[a][:, chans(u, 8)],
            )

        def first_wu():
            dst, src = rounding_views(0)
            nc.scalar.activation(dst[:, :, :, :2], src[:, :, :, :2], COPY)
            nc.scalar.activation(dst[:, :SCALAR_GROUPS, :, 2:], src[:, :SCALAR_GROUPS, :, 2:], COPY)
            by_slot = wu_bf[0][:].rearrange("p (t m j) -> p t m j", t=4, j=4)
            raw = wu_raw[0][:].rearrange("p j (m t) -> p t m j", t=4)
            nc.gpsimd.tensor_scalar(by_slot[:, 2:, SCALAR_GROUPS:, :], raw[:, 2:, SCALAR_GROUPS:, :], 1.0, 0.0, MULT, ADD)
            quantise_wu(0, 0)
            quantise_wu(0, 1)

        def second_wu():
            wu_bf.append(keep.tile([P, 4 * R], BF16, name="wu_bf1", tag="wu_raw0", align_bytes=ALIGN))
            dst, src = rounding_views(1)
            nc.scalar.activation(dst[:, :, :, :2], src[:, :, :, :2], COPY)
            nc.vector.tensor_copy(dst[:, :, :, 2:], src[:, :, :, 2:])
            quantise_wu(1, 0)
            wu_s[1, 1] = reuse.tile([P, R // 2], U8, name="wu_s11", offset=4 * J, align_bytes=ALIGN)
            quantise_wu(1, 1)

        def up_passes(bank, b, order, lo, hi):
            cols = slice(b * BLK, (b + 1) * BLK)
            for at in range(lo, hi):
                a, t = order[at]
                nc.tensor.matmul_mx(
                    out=bank[:, t, :],
                    lhsT=wu_q[a][:, chans(t)].bitcast(FP8X4),
                    lhsT_scale=wu_s[a, t // 2][:, chans(t % 2)],
                    rhs=got_w[a][:, cols].bitcast(FP8X4),
                    rhs_scale=got_s[4 * a :, cols],
                    start=(at == 0),
                    stop=(at == 7),
                )

        def pass_order(b):
            parked = min(4, max(0, PARKED - 4 * b))
            second = [(1, t) for t in ((0, 1, 2, 3) if b == 0 else (2, 3, 0, 1))]
            first = [(0, t) for t in range(4)]
            return first[:parked] + second + first[parked:], parked

        def relu(bank, b):
            dst = h_bf[:, 4 * b * BLK : 4 * (b + 1) * BLK].rearrange("p (n t) -> p n t", t=4)
            nc.scalar.activation(dst, bank[:].rearrange("p t n -> p n t"), RELU)

        def quantise_h(half):
            cols = slice(half * HALF, (half + 1) * HALF)
            nc.vector.quantize_mx(
                out=h_q[:, cols].bitcast(FP8X4), scales=planes[:, cols], in_=h_bf[:, 4 * half * HALF : 4 * (half + 1) * HALF]
            )

        def wd_operands(c):
            return (
                (wd4_w[:].bitcast(U8)[:, chans(c, 2)].bitcast(FP4X4), wd4_s[:].bitcast(U8)[:, chans(c)]),
                (wd8_w[:, chans(c)].bitcast(FP8X4), wd8_s[4:, chans(c)]),
            )

        def first_sum(half):
            cols = slice(half * HALF, (half + 1) * HALF)
            bank = psum.tile([P, HALF], F32, name="bank%d" % half)
            for tier, (words, scales) in enumerate(wd_operands(0)):
                nc.tensor.matmul_mx(
                    out=bank[:],
                    lhsT=words,
                    lhsT_scale=scales,
                    rhs=h_q[:, cols].bitcast(FP8X4),
                    rhs_scale=planes[:, cols],
                    start=(tier == 0),
                    stop=(tier == 1),
                )
            nc.scalar.activation(y_first[:, cols], bank[:], COPY)
            nc.gpsimd.tensor_tensor(z[0][:, cols], y_first[:, cols], r_got[0][:, cols], ADD)

        def gate_columns():
            for half in range(2):
                bank = psum.tile([P, 4, BLK], F32, name="bank%d" % (6 + half))
                for i in range(4):
                    at = half * HALF + i * BLK
                    nc.tensor.transpose(bank[:, i, :], gate[:, at : at + BLK], ident[:])
                nc.scalar.activation(gate_col[:, 4 * half : 4 * half + 4], bank[:, :, 0], COPY)

        def weighed_copy(dst, bank, half):
            for i in range(4):
                at = 4 * half + i
                nc.scalar.activation(dst[:, chans(i)], bank[:, chans(i)], COPY, scale=gate_col[:, at : at + 1])

        def turned_sum(c):
            r_t, y_t = [], []
            for half in range(2):
                bank = psum.tile([P, HALF], F32, name="bank1")
                for i in range(4):
                    at = half * HALF + i * BLK
                    nc.tensor.transpose(bank[:, chans(i)], r_got[c][:, at : at + BLK], ident[:])
                r_t.append(ring.tile([P, HALF], F32, name="r_t"))
                weighed_copy(r_t[half], bank, half)
            for half in range(2):
                bank = psum.tile([P, HALF], F32, name="bank0")
                for i in range(4):
                    cols = slice(half * HALF + i * BLK, half * HALF + (i + 1) * BLK)
                    for tier, (words, scales) in enumerate(wd_operands(c)):
                        nc.tensor.matmul_mx(
                            out=bank[:, chans(i)],
                            lhsT=h_q[:, cols].bitcast(FP8X4),
                            lhsT_scale=planes[:, cols],
                            rhs=words,
                            rhs_scale=scales,
                            start=(tier == 0),
                            stop=(tier == 1),
                        )
                y_t.append(ring.tile([P, HALF], F32, name="y_t"))
                weighed_copy(y_t[half], bank, half)
            for half in range(2):
                bank = psum.tile([P, HALF], F32, name="bank%d" % (4 + half))
                for i in range(4):
                    nc.tensor.matmul(bank[:, chans(i)], y_t[half][:, chans(i)], ident[:], start=True, stop=False, is_transpose=True)
                    nc.tensor.matmul(bank[:, chans(i)], r_t[half][:, chans(i)], ident[:], start=False, stop=True, is_transpose=True)
                nc.scalar.activation(z[c][:, half * HALF : (half + 1) * HALF], bank[:], COPY)

        def late_product(c):
            y = keep.tile([P, J], F32, name="y%d" % c, align_bytes=ALIGN)
            for half in range(2):
                cols = slice(half * HALF, (half + 1) * HALF)
                bank = psum.tile([P, HALF], F32, name="bank%d" % (4 + half))
                for tier, (words, scales) in enumerate(wd_operands(c)):
                    nc.tensor.matmul_mx(
                        out=bank[:],
                        lhsT=words,
                        lhsT_scale=scales,
                        rhs=h_q[:, cols].bitcast(FP8X4),
                        rhs_scale=planes[:, cols],
                        start=(tier == 0),
                        stop=(tier == 1),
                    )
                nc.scalar.activation(y[:, cols], bank[:], COPY)
            return y

        def late_sum(c, y):
            total = keep.tile([P, J], F32, name="total%d" % c, tag="z%d" % (c - 2), align_bytes=ALIGN)
            nc.gpsimd.tensor_tensor(total[:], y[:], r_got[c][:], ADD)
            return total

        def store(c):
            nc.sync.dma_start(out[chans(c), :], pages[c % 2][:])

        load_tab(0)
        nc.sync.dma_start(offsets[:], offs)
        load_tab_scales(0, EARLY_SCALES)
        load_tab(1)
        load_tab_scales(EARLY_SCALES, 8)
        load_wu(0)
        load_wu(1)
        load_r(0)
        load_r(1)
        load_wd_scales(wd8_s.bitcast(I32), 4, wd8_scales)
        load_wd_words(0, N)
        load_r(2)
        load_wd_scales(wd4_s[:], 0, wd4_scales)
        load_r(3)
        nc.sync.dma_start(gate[:], wgo)

        gather_words(0, "got_w0")
        gather_words(1, "got_w1")
        nc.vector.tensor_copy(got_s[:], tab_s[:].bitcast(U8).indirect(offsets[:]))
        first_wu()
        banks = [psum.tile([P, 4, BLK], F32, name="bank%d" % b) for b in range(8)]
        for lo in (0, 2):
            for b in range(8):
                order, parked = pass_order(b)
                up_passes(banks[b], b, order, lo, min(lo + 2, parked))
        second_wu()
        for b in range(8):
            order, parked = pass_order(b)
            up_passes(banks[b], b, order, parked, 8)
            relu(banks[b], b)
        gather_r(0)
        gather_r(1)
        for half in range(2):
            quantise_h(half)
        gather_r(2)
        gather_r(3)
        for half in range(2):
            first_sum(half)
        gate_columns()
        turned_sum(1)
        y_late = {c: late_product(c) for c in (2, 3)}
        pages.append(keep.tile([P, T], F32, name="page1", tag="y_first", align_bytes=ALIGN))
        nc.gpsimd.memset(pages[1][:].bitcast(I32), 0)
        nc.vector.tensor_tensor(pages[0][:].indirect(offsets[:]), z[0][:], gate[:], MULT)
        store(0)
        nc.gpsimd.tensor_tensor(z[2][:], late_sum(2, y_late[2])[:], gate[:], MULT)
        nc.vector.tensor_copy(pages[1][:].indirect(offsets[:]), z[1][:])
        store(1)
        last = late_sum(3, y_late[3])
        nc.vector.tensor_copy(pages[0][:].indirect(offsets[:]), z[2][:])
        store(2)
        nc.vector.tensor_tensor(pages[1][:].indirect(offsets[:]), last[:], gate[:], MULT)
        store(3)
